import numpy as np
import ml_dtypes


def mxq(x, axis, fmt="e4m3"):
    dtype, down = {"e4m3": (ml_dtypes.float8_e4m3fn, 7), "e5m2": (ml_dtypes.float8_e5m2, 14)}[fmt]
    v = np.moveaxis(np.asarray(x, np.float32).astype(ml_dtypes.bfloat16).astype(np.float64), axis, -1)
    blocks = v.reshape(v.shape[:-1] + (-1, 32))
    amax = np.abs(blocks).max(-1, keepdims=True)
    byte = np.maximum(np.where(amax > 0, np.frexp(amax)[1] - 1 + 127, 0) - down, 1)
    scale = np.exp2(byte - 127.0)
    codes = (blocks / scale).astype(np.float32).astype(dtype).astype(np.float64)
    return np.moveaxis((codes * scale).reshape(v.shape), -1, axis)


WIDE = False


def mx_kscale(k):
    if not WIDE:
        return np.ones(k)
    levels = np.array([10, -10, 5, -5, 0])
    if k % 512:
        return np.exp2(np.random.permutation(np.resize(levels, k // 32))).repeat(32)
    a = np.empty((k // 512, 16))
    for p in range(k // 512):
        a[p, :8] = np.random.permutation(np.resize(levels, 8))
        for g in range(8):
            far = levels[np.abs(levels - a[p, g]) >= 10]
            a[p, g + 8] = far[np.random.randint(len(far))]
    return np.exp2(a.ravel()).repeat(32)


def f64(x):
    return np.asarray(x).astype(np.float64)


def striped(idx):
    return np.tile(idx.reshape(-1, 16).T, (8, 1)).astype(np.uint16)


def unstriped(offs):
    return offs[:16].T.reshape(-1).astype(np.int64)


E2M1 = np.array([0.0, 0.5, 1.0, 1.5, 2.0, 3.0, 4.0, 6.0, -0.0, -0.5, -1.0, -1.5, -2.0, -3.0, -4.0, -6.0])


def pack_weight(w, fmt):
    k, n = w.shape
    w = f64(np.asarray(w, np.float32).astype(ml_dtypes.bfloat16)).reshape(k // 32, 32, n)
    amax = np.abs(w).max(1)
    if fmt == "e4m3":
        byte = np.frexp(amax)[1] - 1 + 127 - 7
    else:
        mant, ex = np.frexp(amax / 6.0)
        byte = np.where(mant > 0.5, ex, ex - 1) + 127
    byte = np.clip(np.where(amax > 0, byte, 1), 1, 254)
    scaled = (w * np.exp2(127.0 - byte)[:, None, :]).reshape(k, n).astype(np.float32)
    by_word = np.ascontiguousarray(scaled.reshape(k // 512, 128, 4, n).transpose(0, 1, 3, 2))
    if fmt == "e4m3":
        words = by_word.astype(ml_dtypes.float8_e4m3fn).view(np.uint8)
    else:
        c = by_word.astype(ml_dtypes.float4_e2m1fn).view(np.uint8) & 0xF
        words = (c[..., 0::2] | (c[..., 1::2] << 4)).reshape(k // 512, 128, 2 * n)
    return np.ascontiguousarray(words), np.ascontiguousarray(byte.astype(np.uint8).reshape(k // 512, 16, n))


def unpack_weight(words, scales, fmt):
    g, _, n = scales.shape
    words = np.ascontiguousarray(words).reshape(g, 128, n, -1)
    if fmt == "e4m3":
        vals = words.view(ml_dtypes.float8_e4m3fn).astype(np.float64)
    else:
        nib = np.empty((g, 128, n, 4), np.uint8)
        nib[..., 0::2] = words & 0xF
        nib[..., 1::2] = words >> 4
        vals = E2M1[nib]
    vals = vals * np.repeat(np.exp2(scales.astype(np.float64) - 127.0), 8, axis=1)[..., None]
    return vals.transpose(0, 1, 3, 2).reshape(g * 512, n)


def gelu(v):
    return 0.5 * v * (1.0 + np.tanh(np.sqrt(2.0 / np.pi) * (v + 0.044715 * v**3)))


K, T, S, H, N = 512, 4096, 1024, 1536, 512

def setup_inputs():
    n = np.random.standard_normal
    s = mx_kscale(K)[:, None]
    u = mx_kscale(H)[:, None]
    tab_words, tab_scales = pack_weight(n((K, T)) * s, "e4m3")
    w2_words, w2_scales = pack_weight(n((K, H)) / np.sqrt(K) / s * u.T, "e2m1")
    w3_words, w3_scales = pack_weight(n((H, N)) / np.sqrt(H) / u, "e4m3")
    return {
        "tab_words": tab_words, "tab_scales": tab_scales,
        "offs": striped(np.random.permutation(T)[:S]),
        "w1": (1.5 * n((K, H)) / np.sqrt(K) / s).astype(np.float32),
        "w2_words": w2_words, "w2_scales": w2_scales,
        "rt": np.exp(0.4 * n((H, S))).astype(np.float32),
        "w3_words": w3_words, "w3_scales": w3_scales,
        "offs2": striped(np.random.permutation(S)),
        "wgo": np.exp(0.3 * n((128, S))).astype(np.float32),
        "x0": (0.5 * n((N, S))).astype(np.float32),
    }

def reference(tab_words, tab_scales, offs, w1, w2_words, w2_scales, rt, w3_words, w3_scales, offs2, wgo, x0):
    v = unpack_weight(tab_words, tab_scales, "e4m3")[:, unstriped(offs)]
    a = mxq(f64(w1), 0, "e4m3").T @ v
    b = unpack_weight(w2_words, w2_scales, "e2m1").T @ v
    h = a / (1.0 + np.exp(-a)) * b * f64(rt)
    y = unpack_weight(w3_words, w3_scales, "e4m3").T @ mxq(h, 0, "e4m3")
    page = np.zeros((N, S))
    page[:, unstriped(offs2)] = np.tile(f64(wgo), (N // 128, 1)) * y
    return np.tanh(f64(x0) + page)

@@ -1,0 +1,271 @@
+from contextlib import ExitStack
+
+import concourse.mybir as mybir
+
+K, T, S, H, N = 512, 4096, 1024, 1536, 512
+FLOPS = 2 * (2 * K * H * S + H * N * S)
+
+F32 = mybir.dt.float32
+BF16 = mybir.dt.bfloat16
+I32 = mybir.dt.int32
+U32 = mybir.dt.uint32
+U16 = mybir.dt.uint16
+U8 = mybir.dt.uint8
+FP8X4 = mybir.dt.float8_e4m3fn_x4
+FP4X4 = mybir.dt.float4_e2m1fn_x4
+MULT = mybir.AluOpType.mult
+ADD = mybir.AluOpType.add
+ACT = mybir.ActivationFunctionType
+
+P = 128
+PACK = 4
+PASS = P * PACK
+NB = H // PASS
+Q = 256
+NQ = S // Q
+HALF = 512
+NT = N // P
+M_SPLIT = 80
+
+
+def tile_list_email_expert_return_kernel(
+    tc, tab_words, tab_scales, offs, w1, w2_words, w2_scales, rt, w3_words, w3_scales, offs2, wgo, x0, out
+):
+    nc = tc.nc
+    with ExitStack() as ctx:
+        keep = ctx.enter_context(tc.tile_pool(name="keep", bufs=1))
+        work = ctx.enter_context(tc.tile_pool(name="work", bufs=3))
+        psum = ctx.enter_context(tc.psum_pool(name="psum", bufs=3))
+        psum_y = ctx.enter_context(tc.psum_pool(name="psum_y", bufs=2))
+
+        def held(shape, dtype, name):
+            return keep.tile(shape, dtype, name=name, align_bytes=64)
+
+        idx = keep.tile([P, S // 16], U16, name="idx")
+        idx2 = keep.tile([P, S // 16], U16, name="idx2")
+        tab_plane = held([P, T], U8, "tab_plane")
+        w2_plane_raw = held([P, H], U8, "w2_plane_raw")
+        w3_plane = held([P, N], U8, "w3_plane")
+        nc.vector.memset(tab_plane[:].bitcast(I32), 0)
+        nc.vector.memset(w2_plane_raw[:].bitcast(I32), 0)
+        nc.gpsimd.memset(w3_plane[:].bitcast(I32), 0)
+        warm = held([P, 2], F32, "warm")
+        nc.gpsimd.memset(warm[:, 0:1], 0.0)
+        nc.scalar.activation(warm[:, 1:2], warm[:, 0:1], ACT.Silu)
+        tab = held([P, T], U32, "tab")
+        tab_src = tab_words[0].rearrange("p t i -> p (t i)").bitcast(I32)
+        nc.sync.dma_start(tab[:, : T // 4].bitcast(I32), tab_src[:, : T // 4])
+        for quad in range(4):
+            nc.sync.dma_start(
+                tab_plane[32 * quad : 32 * quad + 4, :].bitcast(I32), tab_scales[0, 4 * quad : 4 * quad + 4, :].bitcast(I32)
+            )
+        nc.sync.dma_start(idx[:], offs)
+        w2_raw = {}
+
+        def load_w2(first, count):
+            tile = held([P, 2 * count * PASS], U8, "w2_raw%d" % first)
+            nc.sync.dma_start(tile[:].bitcast(I32), w2_words[0, :, 2 * first * PASS : 2 * (first + count) * PASS].bitcast(I32))
+            for i in range(count):
+                w2_raw[first + i] = tile[:, 2 * i * PASS : 2 * (i + 1) * PASS]
+
+        load_w2(0, 1)
+        nc.sync.dma_start(tab[:, T // 4 :].bitcast(I32), tab_src[:, T // 4 :])
+        for quad in range(4):
+            nc.sync.dma_start(
+                w2_plane_raw[32 * quad : 32 * quad + 4, :].bitcast(I32), w2_scales[0, 4 * quad : 4 * quad + 4, :].bitcast(I32)
+            )
+
+        rt_sb = {}
+
+        def load_rt(b, first_q, count):
+            tile = held([P, PACK, count * Q], F32, "rt_%d_%d" % (b, first_q))
+            rows = rt[b * PASS : (b + 1) * PASS, first_q * Q : (first_q + count) * Q]
+            nc.sync.dma_start(tile[:], rows.rearrange("(p t) n -> p t n", t=PACK))
+            for i in range(count):
+                rt_sb[(b, first_q + i)] = tile[:, :, i * Q : (i + 1) * Q]
+
+        w1_raw = {}
+
+        def load_w1(b):
+            tile = held([P, PACK, PASS], F32, "w1_raw%d" % b)
+            nc.sync.dma_start(tile[:], w1[:, b * PASS : (b + 1) * PASS].rearrange("(p j) c -> p j c", j=PACK))
+            w1_raw[b] = tile
+
+        load_rt(0, 0, 1)
+        load_w1(0)
+        load_rt(0, 1, 1)
+        load_w2(1, 2)
+        load_w1(1)
+        load_rt(1, 0, 2)
+        load_w1(2)
+        load_rt(2, 0, 2)
+        w3 = [held([P, N], U32, "w3_%d" % b) for b in range(NB)]
+        for b in range(NB):
+            nc.sync.dma_start(w3[b][:].bitcast(I32), w3_words[b].rearrange("p n i -> p (n i)").bitcast(I32))
+        for quad in range(4):
+            nc.sync.dma_start(
+                w3_plane[32 * quad : 32 * quad + 4 * NB, :].bitcast(I32), w3_scales[:, 4 * quad : 4 * quad + 4, :].bitcast(I32)
+            )
+        wgo_sb = held([P, S], F32, "wgo_sb")
+        nc.sync.dma_start(wgo_sb[:], wgo)
+        nc.sync.dma_start(idx2[:], offs2)
+        for b in range(NB):
+            load_rt(b, 2, 2)
+        x0_sb = [held([P, S], F32, "x0_%d" % i) for i in range(NT)]
+        for i in range(NT):
+            nc.sync.dma_start(x0_sb[i][:], x0[i * P : (i + 1) * P, :])
+
+        v_words = [held([P, HALF], U32, "v_words%d" % h) for h in range(2)]
+        v_plane = [held([P, HALF], U8, "v_plane%d" % h) for h in range(2)]
+
+        def gather(dst, window, h):
+            nc.vector.tensor_copy(dst[h][:], window[:].indirect(idx[:, h * HALF // 16 : (h + 1) * HALF // 16]))
+
+        w2c = [held([P, 2 * PASS], U8, "w2c%d" % b) for b in range(NB)]
+        w2s = [held([P, PASS], U8, "w2s%d" % b) for b in range(NB)]
+
+        def order_w2(b):
+            nc.vector.tensor_copy(
+                w2c[b][:].bitcast(U16).rearrange("p (t m) -> p t m", t=PACK),
+                w2_raw[b].bitcast(U16).rearrange("p (m t) -> p t m", t=PACK),
+            )
+            nc.vector.tensor_copy(
+                w2s[b][:].rearrange("p (t m) -> p t m", t=PACK),
+                w2_plane_raw[:, b * PASS : (b + 1) * PASS].rearrange("p (m t) -> p t m", t=PACK),
+            )
+
+        w1c = [held([P, PASS], U32, "w1c%d" % b) for b in range(NB)]
+        w1s = [held([P, PASS], U8, "w1s%d" % b) for b in range(NB)]
+
+        def quantize_w1(b):
+            grouped = work.tile([P, PACK, P, PACK], BF16, name="w1_grouped", bufs=2, align_bytes=64)
+            dst = grouped[:].rearrange("p t m j -> p m t j")
+            src = w1_raw[b][:].rearrange("p j (m t) -> p m t j", t=PACK)
+            if b == 0:
+                nc.vector.tensor_copy(dst[:, :M_SPLIT], src[:, :M_SPLIT])
+                nc.scalar.copy(dst[:, M_SPLIT:], src[:, M_SPLIT:])
+            else:
+                nc.scalar.copy(dst, src)
+            nc.vector.quantize_mx(
+                out=w1c[b][:].bitcast(FP8X4), scales=w1s[b][:], in_=grouped[:].rearrange("p t m j -> p (t m j)")
+            )
+
+        def v_operand(q):
+            cols = slice((q % 2) * Q, (q % 2 + 1) * Q)
+            return v_words[q // 2][:, cols].bitcast(FP8X4), v_plane[q // 2][:, cols]
+
+        gated = {}
+
+        def up(b, q):
+            rhs, rhs_scale = v_operand(q)
+            prod = work.tile([P, 2, Q, 2], F32, name="prod")
+            for u in range(2):
+                bank = psum.tile([P, 2, Q], F32, name="bank_b")
+                for e in range(2):
+                    t = 2 * u + e
+                    nc.tensor.matmul_mx(
+                        out=bank[:, e, :], lhsT=w2c[b][:, 2 * t * P : 2 * (t + 1) * P].bitcast(FP4X4),
+                        lhsT_scale=w2s[b][:, t * P : (t + 1) * P], rhs=rhs, rhs_scale=rhs_scale, start=True, stop=True,
+                    )
+                nc.vector.tensor_tensor(
+                    prod[:, u, :, :], bank[:].rearrange("p e n -> p n e"),
+                    rt_sb[(b, q)][:, 2 * u : 2 * u + 2, :].rearrange("p e n -> p n e"), MULT,
+                )
+            gated[(b, q)] = prod
+
+        h_bf = {}
+
+        def gate(b, q):
+            rhs, rhs_scale = v_operand(q)
+            act = work.tile([P, 2, Q, 2], F32, name="act")
+            for u in range(2):
+                bank = psum.tile([P, 2, Q], F32, name="bank_a")
+                for e in range(2):
+                    t = 2 * u + e
+                    nc.tensor.matmul_mx(
+                        out=bank[:, e, :], lhsT=w1c[b][:, t * P : (t + 1) * P].bitcast(FP8X4),
+                        lhsT_scale=w1s[b][:, t * P : (t + 1) * P], rhs=rhs, rhs_scale=rhs_scale, start=True, stop=True,
+                    )
+                nc.scalar.activation(act[:, u, :, :], bank[:].rearrange("p e n -> p n e"), ACT.Silu)
+            h = work.tile([P, Q, 2, 2], BF16, name="h", align_bytes=64)
+            nc.vector.tensor_tensor(
+                h[:], act[:].rearrange("p u n e -> p n u e"), gated[(b, q)][:].rearrange("p u n e -> p n u e"), MULT
+            )
+            h_bf[(b, q)] = h
+
+        hc, hs = {}, {}
+
+        def quantize_h(b, q):
+            hc[(b, q)] = held([P, Q], U32, "hc_%d_%d" % (b, q))
+            hs[(b, q)] = held([P, Q], U8, "hs_%d_%d" % (b, q))
+            nc.vector.quantize_mx(
+                out=hc[(b, q)][:].bitcast(FP8X4), scales=hs[(b, q)][:], in_=h_bf[(b, q)][:].rearrange("p n u e -> p (n u e)")
+            )
+
+        y_sb = {}
+
+        def down(q):
+            for pair in range(NT // 2):
+                bank = psum_y.tile([P, 2, Q], F32, name="bank_y")
+                for e in range(2):
+                    cols = slice((2 * pair + e) * P, (2 * pair + e + 1) * P)
+                    for b in range(NB):
+                        nc.tensor.matmul_mx(
+                            out=bank[:, e, :], lhsT=w3[b][:, cols].bitcast(FP8X4), lhsT_scale=w3_plane[4 * b : P, cols],
+                            rhs=hc[(b, q)][:].bitcast(FP8X4), rhs_scale=hs[(b, q)][:], start=(b == 0), stop=(b == NB - 1),
+                        )
+                y = work.tile([P, 2, Q], F32, name="y", bufs=4)
+                nc.scalar.copy(y[:], bank[:])
+                for e in range(2):
+                    y_sb[(q, 2 * pair + e)] = y[:, e, :]
+
+        page = [held([P, S], F32, "page%d" % i) for i in range(NT)]
+
+        def scatter(q, i):
+            nc.vector.tensor_tensor(
+                page[i][:].indirect(idx2[:, q * Q // 16 : (q + 1) * Q // 16]), y_sb[(q, i)], wgo_sb[:, q * Q : (q + 1) * Q], MULT
+            )
+
+        def finish(i):
+            for half in range(2):
+                cols = slice(half * HALF, (half + 1) * HALF)
+                pre = work.tile([P, HALF], F32, name="pre")
+                nc.vector.tensor_tensor(pre[:], page[i][:, cols], x0_sb[i][:, cols], ADD)
+                res = work.tile([P, HALF], F32, name="res")
+                nc.scalar.activation(res[:], pre[:], ACT.Tanh)
+                nc.sync.dma_start(out[i * P : (i + 1) * P, cols], res[:])
+
+        gather(v_plane, tab_plane, 0)
+        order_w2(0)
+        gather(v_words, tab, 0)
+        units = [(b, 2 * half + i) for half in range(2) for b in range(NB) for i in range(2)]
+        up(*units[0])
+        quantize_w1(0)
+        for step, (b, q) in enumerate(units):
+            if step + 1 < len(units):
+                nb, nq = units[step + 1]
+                if nq == 0:
+                    order_w2(nb)
+                    quantize_w1(nb)
+                if (nb, nq) == (2, 1):
+                    gather(v_plane, tab_plane, 1)
+                    gather(v_words, tab, 1)
+                up(nb, nq)
+            gate(b, q)
+            if step > 0:
+                quantize_h(*units[step - 1])
+                pb, pq = units[step - 1]
+                if pb == NB - 1:
+                    down(pq)
+            if step >= 8:
+                for i in range(2):
+                    scatter((step - 8) // 2, 2 * (step % 2) + i)
+        quantize_h(*units[-1])
+        down(NQ - 1)
+        for i in range(NT):
+            scatter(2, i)
+        for i in range(NT):
+            scatter(3, i)
+            if i > 0:
+                finish(i - 1)
+        finish(NT - 1)

@@ -26,6 +26,8 @@ NQ = S // Q
 HALF = 512
 NT = N // P
 M_SPLIT = 80
+FIRST_ON_GPSIMD = 3
+ADDS_ON_GPSIMD = 5
 
 
 def tile_list_email_expert_return_kernel(
@@ -36,7 +38,7 @@ def tile_list_email_expert_return_kernel(
         keep = ctx.enter_context(tc.tile_pool(name="keep", bufs=1))
         work = ctx.enter_context(tc.tile_pool(name="work", bufs=3))
         psum = ctx.enter_context(tc.psum_pool(name="psum", bufs=3))
-        psum_y = ctx.enter_context(tc.psum_pool(name="psum_y", bufs=2))
+        psum_a = ctx.enter_context(tc.psum_pool(name="psum_a", bufs=2))
 
         def held(shape, dtype, name):
             return keep.tile(shape, dtype, name=name, align_bytes=64)
@@ -69,12 +71,20 @@ def tile_list_email_expert_return_kernel(
                 w2_raw[first + i] = tile[:, 2 * i * PASS : 2 * (i + 1) * PASS]
 
         load_w2(0, 1)
-        nc.sync.dma_start(tab[:, T // 4 :].bitcast(I32), tab_src[:, T // 4 :])
+        w1_raw = {}
+
+        def load_w1(b):
+            tile = held([P, PACK, PASS], F32, "w1_raw%d" % b)
+            nc.sync.dma_start(tile[:], w1[:, b * PASS : (b + 1) * PASS].rearrange("(p j) c -> p j c", j=PACK))
+            w1_raw[b] = tile
+
+        load_w1(0)
         for quad in range(4):
             nc.sync.dma_start(
                 w2_plane_raw[32 * quad : 32 * quad + 4, :].bitcast(I32), w2_scales[0, 4 * quad : 4 * quad + 4, :].bitcast(I32)
             )
 
+        nc.sync.dma_start(tab[:, T // 4 :].bitcast(I32), tab_src[:, T // 4 :])
         rt_sb = {}
 
         def load_rt(b, first_q, count):
@@ -84,24 +94,15 @@ def tile_list_email_expert_return_kernel(
             for i in range(count):
                 rt_sb[(b, first_q + i)] = tile[:, :, i * Q : (i + 1) * Q]
 
-        w1_raw = {}
-
-        def load_w1(b):
-            tile = held([P, PACK, PASS], F32, "w1_raw%d" % b)
-            nc.sync.dma_start(tile[:], w1[:, b * PASS : (b + 1) * PASS].rearrange("(p j) c -> p j c", j=PACK))
-            w1_raw[b] = tile
-
         load_rt(0, 0, 1)
-        load_w1(0)
-        load_rt(0, 1, 1)
-        load_w2(1, 2)
         load_w1(1)
-        load_rt(1, 0, 2)
+        load_w2(1, 2)
+        load_rt(1, 0, 1)
         load_w1(2)
-        load_rt(2, 0, 2)
-        w3 = [held([P, N], U32, "w3_%d" % b) for b in range(NB)]
-        for b in range(NB):
-            nc.sync.dma_start(w3[b][:].bitcast(I32), w3_words[b].rearrange("p n i -> p (n i)").bitcast(I32))
+        load_rt(2, 0, 1)
+        load_rt(0, 1, 1)
+        w3 = held([P, NB, N], U32, "w3")
+        nc.sync.dma_start(w3[:].bitcast(I32), w3_words.rearrange("a p n i -> p a (n i)").bitcast(I32))
         for quad in range(4):
             nc.sync.dma_start(
                 w3_plane[32 * quad : 32 * quad + 4 * NB, :].bitcast(I32), w3_scales[:, 4 * quad : 4 * quad + 4, :].bitcast(I32)
@@ -109,6 +110,8 @@ def tile_list_email_expert_return_kernel(
         wgo_sb = held([P, S], F32, "wgo_sb")
         nc.sync.dma_start(wgo_sb[:], wgo)
         nc.sync.dma_start(idx2[:], offs2)
+        load_rt(1, 1, 1)
+        load_rt(2, 1, 1)
         for b in range(NB):
             load_rt(b, 2, 2)
         x0_sb = [held([P, S], F32, "x0_%d" % i) for i in range(NT)]
@@ -173,13 +176,13 @@ def tile_list_email_expert_return_kernel(
                 )
             gated[(b, q)] = prod
 
-        h_bf = {}
+        acts = {}
 
         def gate(b, q):
             rhs, rhs_scale = v_operand(q)
-            act = work.tile([P, 2, Q, 2], F32, name="act")
+            act = work.tile([P, 2, Q, 2], F32, name="act", bufs=2)
             for u in range(2):
-                bank = psum.tile([P, 2, Q], F32, name="bank_a")
+                bank = psum_a.tile([P, 2, Q], F32, name="bank_a")
                 for e in range(2):
                     t = 2 * u + e
                     nc.tensor.matmul_mx(
@@ -187,9 +190,18 @@ def tile_list_email_expert_return_kernel(
                         lhsT_scale=w1s[b][:, t * P : (t + 1) * P], rhs=rhs, rhs_scale=rhs_scale, start=True, stop=True,
                     )
                 nc.scalar.activation(act[:, u, :, :], bank[:].rearrange("p e n -> p n e"), ACT.Silu)
-            h = work.tile([P, Q, 2, 2], BF16, name="h", align_bytes=64)
-            nc.vector.tensor_tensor(
-                h[:], act[:].rearrange("p u n e -> p n u e"), gated[(b, q)][:].rearrange("p u n e -> p n u e"), MULT
+            acts[(b, q)] = act
+
+        h_bf = {}
+
+        def combine(b, q, on_gpsimd):
+            if on_gpsimd:
+                h = work.tile([P, Q, 2, 2], BF16, name="h_g", bufs=1, align_bytes=64)
+            else:
+                h = work.tile([P, Q, 2, 2], BF16, name="h_v", bufs=2, align_bytes=64)
+            engine = nc.gpsimd if on_gpsimd else nc.vector
+            engine.tensor_tensor(
+                h[:], acts[(b, q)][:].rearrange("p u n e -> p n u e"), gated[(b, q)][:].rearrange("p u n e -> p n u e"), MULT
             )
             h_bf[(b, q)] = h
 
@@ -202,70 +214,57 @@ def tile_list_email_expert_return_kernel(
                 out=hc[(b, q)][:].bitcast(FP8X4), scales=hs[(b, q)][:], in_=h_bf[(b, q)][:].rearrange("p n u e -> p (n u e)")
             )
 
-        y_sb = {}
-
-        def down(q):
-            for pair in range(NT // 2):
-                bank = psum_y.tile([P, 2, Q], F32, name="bank_y")
-                for e in range(2):
-                    cols = slice((2 * pair + e) * P, (2 * pair + e + 1) * P)
-                    for b in range(NB):
-                        nc.tensor.matmul_mx(
-                            out=bank[:, e, :], lhsT=w3[b][:, cols].bitcast(FP8X4), lhsT_scale=w3_plane[4 * b : P, cols],
-                            rhs=hc[(b, q)][:].bitcast(FP8X4), rhs_scale=hs[(b, q)][:], start=(b == 0), stop=(b == NB - 1),
-                        )
-                y = work.tile([P, 2, Q], F32, name="y", bufs=4)
-                nc.scalar.copy(y[:], bank[:])
-                for e in range(2):
-                    y_sb[(q, 2 * pair + e)] = y[:, e, :]
-
         page = [held([P, S], F32, "page%d" % i) for i in range(NT)]
 
-        def scatter(q, i):
-            nc.vector.tensor_tensor(
-                page[i][:].indirect(idx2[:, q * Q // 16 : (q + 1) * Q // 16]), y_sb[(q, i)], wgo_sb[:, q * Q : (q + 1) * Q], MULT
-            )
+        def down(q, i):
+            bank = psum_a.tile([P, 2, Q], F32, name="bank_a")
+            cols = slice(i * P, (i + 1) * P)
+            for b in range(NB):
+                nc.tensor.matmul_mx(
+                    out=bank[:, 0, :], lhsT=w3[:, b, cols].bitcast(FP8X4), lhsT_scale=w3_plane[4 * b : P, cols],
+                    rhs=hc[(b, q)][:].bitcast(FP8X4), rhs_scale=hs[(b, q)][:], start=(b == 0), stop=(b == NB - 1),
+                )
+            y = work.tile([P, Q], F32, name="y")
+            nc.vector.tensor_tensor(y[:], bank[:, 0, :], wgo_sb[:, q * Q : (q + 1) * Q], MULT)
+            nc.vector.tensor_copy(page[i][:].indirect(idx2[:, q * Q // 16 : (q + 1) * Q // 16]), y[:])
 
         def finish(i):
             for half in range(2):
                 cols = slice(half * HALF, (half + 1) * HALF)
                 pre = work.tile([P, HALF], F32, name="pre")
-                nc.vector.tensor_tensor(pre[:], page[i][:, cols], x0_sb[i][:, cols], ADD)
+                engine = nc.gpsimd if 2 * i + half < ADDS_ON_GPSIMD else nc.vector
+                engine.tensor_tensor(pre[:], page[i][:, cols], x0_sb[i][:, cols], ADD)
                 res = work.tile([P, HALF], F32, name="res")
                 nc.scalar.activation(res[:], pre[:], ACT.Tanh)
                 nc.sync.dma_start(out[i * P : (i + 1) * P, cols], res[:])
 
         gather(v_plane, tab_plane, 0)
         order_w2(0)
-        gather(v_words, tab, 0)
-        units = [(b, 2 * half + i) for half in range(2) for b in range(NB) for i in range(2)]
-        up(*units[0])
         quantize_w1(0)
+        gather(v_words, tab, 0)
+        units = [(b, q) for q in range(NQ) for b in range(NB)]
+        up(*units[0])
+        gate(*units[0])
         for step, (b, q) in enumerate(units):
+            if step > 0:
+                quantize_h(*units[step - 1])
+            combine(b, q, step >= FIRST_ON_GPSIMD)
             if step + 1 < len(units):
                 nb, nq = units[step + 1]
                 if nq == 0:
                     order_w2(nb)
                     quantize_w1(nb)
-                if (nb, nq) == (2, 1):
-                    gather(v_plane, tab_plane, 1)
-                    gather(v_words, tab, 1)
                 up(nb, nq)
-            gate(b, q)
-            if step > 0:
-                quantize_h(*units[step - 1])
-                pb, pq = units[step - 1]
-                if pb == NB - 1:
-                    down(pq)
-            if step >= 8:
-                for i in range(2):
-                    scatter((step - 8) // 2, 2 * (step % 2) + i)
+                gate(nb, nq)
+            if step == 0:
+                gather(v_plane, tab_plane, 1)
+                gather(v_words, tab, 1)
+            if q > 0:
+                for i in ((0, 1), (2,), (3,))[b]:
+                    down(q - 1, i)
         quantize_h(*units[-1])
-        down(NQ - 1)
         for i in range(NT):
-            scatter(2, i)
-        for i in range(NT):
-            scatter(3, i)
+            down(NQ - 1, i)
             if i > 0:
                 finish(i - 1)
         finish(NT - 1)

@@ -26,8 +26,9 @@ NQ = S // Q
 HALF = 512
 NT = N // P
 M_SPLIT = 80
+KB = 1024
+UNIT_BYTES = PACK * Q * 4
 FIRST_ON_GPSIMD = 3
-ADDS_ON_GPSIMD = 5
 
 
 def tile_list_email_expert_return_kernel(
@@ -37,8 +38,11 @@ def tile_list_email_expert_return_kernel(
     with ExitStack() as ctx:
         keep = ctx.enter_context(tc.tile_pool(name="keep", bufs=1))
         work = ctx.enter_context(tc.tile_pool(name="work", bufs=3))
+        stream = ctx.enter_context(tc.tile_pool(name="stream", bufs=1))
+        relay = ctx.enter_context(tc.tile_pool(name="relay", bufs=1))
         psum = ctx.enter_context(tc.psum_pool(name="psum", bufs=3))
-        psum_a = ctx.enter_context(tc.psum_pool(name="psum_a", bufs=2))
+        psum_a = ctx.enter_context(tc.psum_pool(name="psum_a", bufs=3))
+        psum_y = ctx.enter_context(tc.psum_pool(name="psum_y", bufs=2))
 
         def held(shape, dtype, name):
             return keep.tile(shape, dtype, name=name, align_bytes=64)
@@ -87,39 +91,44 @@ def tile_list_email_expert_return_kernel(
         nc.sync.dma_start(tab[:, T // 4 :].bitcast(I32), tab_src[:, T // 4 :])
         rt_sb = {}
 
-        def load_rt(b, first_q, count):
-            tile = held([P, PACK, count * Q], F32, "rt_%d_%d" % (b, first_q))
-            rows = rt[b * PASS : (b + 1) * PASS, first_q * Q : (first_q + count) * Q]
+        def load_rt(b, q):
+            tile = stream.tile([P, PACK, Q], F32, name="rt_%d_%d" % (b, q), offset=(NB * q + b) * UNIT_BYTES, align_bytes=64)
+            rows = rt[b * PASS : (b + 1) * PASS, q * Q : (q + 1) * Q]
             nc.sync.dma_start(tile[:], rows.rearrange("(p t) n -> p t n", t=PACK))
-            for i in range(count):
-                rt_sb[(b, first_q + i)] = tile[:, :, i * Q : (i + 1) * Q]
+            rt_sb[(b, q)] = tile
 
-        load_rt(0, 0, 1)
-        load_w1(1)
+        w3 = [held([P, NB, 2 * P], U32, "w3_%d" % pair) for pair in range(NT // 2)]
+        w3_src = w3_words.rearrange("a p n i -> p a (n i)").bitcast(I32)
+        wgo_sb = [held([P, Q], F32, "wgo_first"), held([P, S - Q], F32, "wgo_rest")]
+        load_rt(0, 0)
         load_w2(1, 2)
-        load_rt(1, 0, 1)
+        load_w1(1)
+        load_rt(1, 0)
         load_w1(2)
-        load_rt(2, 0, 1)
-        load_rt(0, 1, 1)
-        w3 = held([P, NB, N], U32, "w3")
-        nc.sync.dma_start(w3[:].bitcast(I32), w3_words.rearrange("a p n i -> p a (n i)").bitcast(I32))
+        load_rt(2, 0)
+        load_rt(0, 1)
+        nc.sync.dma_start(w3[0][:].bitcast(I32), w3_src[:, :, : 2 * P])
         for quad in range(4):
             nc.sync.dma_start(
                 w3_plane[32 * quad : 32 * quad + 4 * NB, :].bitcast(I32), w3_scales[:, 4 * quad : 4 * quad + 4, :].bitcast(I32)
             )
-        wgo_sb = held([P, S], F32, "wgo_sb")
-        nc.sync.dma_start(wgo_sb[:], wgo)
+        nc.sync.dma_start(wgo_sb[0][:], wgo[:, :Q])
         nc.sync.dma_start(idx2[:], offs2)
-        load_rt(1, 1, 1)
-        load_rt(2, 1, 1)
+        load_rt(1, 1)
+        load_rt(2, 1)
+        nc.sync.dma_start(w3[1][:].bitcast(I32), w3_src[:, :, 2 * P :])
+        load_rt(0, 2)
+        load_rt(1, 2)
+        nc.sync.dma_start(wgo_sb[1][:], wgo[:, Q:])
+        load_rt(2, 2)
         for b in range(NB):
-            load_rt(b, 2, 2)
+            load_rt(b, 3)
         x0_sb = [held([P, S], F32, "x0_%d" % i) for i in range(NT)]
         for i in range(NT):
             nc.sync.dma_start(x0_sb[i][:], x0[i * P : (i + 1) * P, :])
 
-        v_words = [held([P, HALF], U32, "v_words%d" % h) for h in range(2)]
-        v_plane = [held([P, HALF], U8, "v_plane%d" % h) for h in range(2)]
+        v_words = {0: held([P, HALF], U32, "v_words0")}
+        v_plane = {0: held([P, HALF], U8, "v_plane0")}
 
         def gather(dst, window, h):
             nc.vector.tensor_copy(dst[h][:], window[:].indirect(idx[:, h * HALF // 16 : (h + 1) * HALF // 16]))
@@ -144,7 +153,7 @@ def tile_list_email_expert_return_kernel(
             grouped = work.tile([P, PACK, P, PACK], BF16, name="w1_grouped", bufs=2, align_bytes=64)
             dst = grouped[:].rearrange("p t m j -> p m t j")
             src = w1_raw[b][:].rearrange("p j (m t) -> p m t j", t=PACK)
-            if b == 0:
+            if b in (0,):
                 nc.vector.tensor_copy(dst[:, :M_SPLIT], src[:, :M_SPLIT])
                 nc.scalar.copy(dst[:, M_SPLIT:], src[:, M_SPLIT:])
             else:
@@ -161,7 +170,7 @@ def tile_list_email_expert_return_kernel(
 
         def up(b, q):
             rhs, rhs_scale = v_operand(q)
-            prod = work.tile([P, 2, Q, 2], F32, name="prod")
+            prod = work.tile([P, 2, Q, 2], F32, name="prod", bufs=2)
             for u in range(2):
                 bank = psum.tile([P, 2, Q], F32, name="bank_b")
                 for e in range(2):
@@ -195,10 +204,8 @@ def tile_list_email_expert_return_kernel(
         h_bf = {}
 
         def combine(b, q, on_gpsimd):
-            if on_gpsimd:
-                h = work.tile([P, Q, 2, 2], BF16, name="h_g", bufs=1, align_bytes=64)
-            else:
-                h = work.tile([P, Q, 2, 2], BF16, name="h_v", bufs=2, align_bytes=64)
+            step = NB * q + b
+            h = relay.tile([P, Q, 2, 2], BF16, name="h_%d" % step, offset=(step % 2) * KB, align_bytes=64)
             engine = nc.gpsimd if on_gpsimd else nc.vector
             engine.tensor_tensor(
                 h[:], acts[(b, q)][:].rearrange("p u n e -> p n u e"), gated[(b, q)][:].rearrange("p u n e -> p n u e"), MULT
@@ -208,7 +215,9 @@ def tile_list_email_expert_return_kernel(
         hc, hs = {}, {}
 
         def quantize_h(b, q):
-            hc[(b, q)] = held([P, Q], U32, "hc_%d_%d" % (b, q))
+            hc[(b, q)] = stream.tile(
+                [P, Q], U32, name="hc_%d_%d" % (b, q), offset=(NB * q + b + 1) * UNIT_BYTES, align_bytes=64
+            )
             hs[(b, q)] = held([P, Q], U8, "hs_%d_%d" % (b, q))
             nc.vector.quantize_mx(
                 out=hc[(b, q)][:].bitcast(FP8X4), scales=hs[(b, q)][:], in_=h_bf[(b, q)][:].rearrange("p n u e -> p (n u e)")
@@ -216,27 +225,43 @@ def tile_list_email_expert_return_kernel(
 
         page = [held([P, S], F32, "page%d" % i) for i in range(NT)]
 
-        def down(q, i):
-            bank = psum_a.tile([P, 2, Q], F32, name="bank_a")
+        def down(i, quarters, on_gpsimd, paced):
+            width = len(quarters) * Q
+            if paced or i < 2:
+                bank = psum_y.tile([P, width], F32, name="bank_y")
+            else:
+                bank = psum_a.tile([P, width], F32, name="bank_a")
             cols = slice(i * P, (i + 1) * P)
-            for b in range(NB):
-                nc.tensor.matmul_mx(
-                    out=bank[:, 0, :], lhsT=w3[:, b, cols].bitcast(FP8X4), lhsT_scale=w3_plane[4 * b : P, cols],
-                    rhs=hc[(b, q)][:].bitcast(FP8X4), rhs_scale=hs[(b, q)][:], start=(b == 0), stop=(b == NB - 1),
-                )
-            y = work.tile([P, Q], F32, name="y")
-            nc.vector.tensor_tensor(y[:], bank[:, 0, :], wgo_sb[:, q * Q : (q + 1) * Q], MULT)
-            nc.vector.tensor_copy(page[i][:].indirect(idx2[:, q * Q // 16 : (q + 1) * Q // 16]), y[:])
+            for e, q in enumerate(quarters):
+                for b in range(NB):
+                    nc.tensor.matmul_mx(
+                        out=bank[:, e * Q : (e + 1) * Q], lhsT=w3[i // 2][:, b, (i % 2) * P : (i % 2 + 1) * P].bitcast(FP8X4),
+                        lhsT_scale=w3_plane[4 * b : P, cols],
+                        rhs=hc[(b, q)][:].bitcast(FP8X4), rhs_scale=hs[(b, q)][:], start=(b == 0), stop=(b == NB - 1),
+                    )
+            first = quarters[0] * Q
+            factor = wgo_sb[0][:] if first == 0 else wgo_sb[1][:, first - Q : first - Q + width]
+            if paced:
+                weighted = relay.tile([P, width], F32, name="weighted_%d" % paced, offset=(paced % 2) * 2 * KB, align_bytes=64)
+            else:
+                weighted = work.tile([P, width], F32, name="weighted", bufs=4)
+            if on_gpsimd:
+                y = work.tile([P, width], F32, name=("y", "stage_a", "stage_b")[i - 1], bufs=1)
+                nc.scalar.copy(y[:], bank[:])
+                nc.gpsimd.tensor_tensor(weighted[:], y[:], factor, MULT)
+            else:
+                nc.vector.tensor_tensor(weighted[:], bank[:], factor, MULT)
+            nc.vector.tensor_copy(page[i][:].indirect(idx2[:, first // 16 : (first + width) // 16]), weighted[:])
 
         def finish(i):
-            for half in range(2):
-                cols = slice(half * HALF, (half + 1) * HALF)
-                pre = work.tile([P, HALF], F32, name="pre")
-                engine = nc.gpsimd if 2 * i + half < ADDS_ON_GPSIMD else nc.vector
-                engine.tensor_tensor(pre[:], page[i][:, cols], x0_sb[i][:, cols], ADD)
-                res = work.tile([P, HALF], F32, name="res")
-                nc.scalar.activation(res[:], pre[:], ACT.Tanh)
-                nc.sync.dma_start(out[i * P : (i + 1) * P, cols], res[:])
+            pre = work.tile([P, S], F32, name="stage_b" if i == 1 else "stage_a", bufs=1)
+            width = Q if i == NT - 1 else HALF
+            for piece in range(S // width):
+                cols = slice(piece * width, (piece + 1) * width)
+                engine = nc.vector if i == NT - 1 else nc.gpsimd
+                engine.tensor_tensor(pre[:, cols], page[i][:, cols], x0_sb[i][:, cols], ADD)
+                nc.scalar.activation(x0_sb[i][:, cols], pre[:, cols], ACT.Tanh)
+                nc.sync.dma_start(out[i * P : (i + 1) * P, cols], x0_sb[i][:, cols])
 
         gather(v_plane, tab_plane, 0)
         order_w2(0)
@@ -246,9 +271,7 @@ def tile_list_email_expert_return_kernel(
         up(*units[0])
         gate(*units[0])
         for step, (b, q) in enumerate(units):
-            if step > 0:
-                quantize_h(*units[step - 1])
-            combine(b, q, step >= FIRST_ON_GPSIMD)
+            combine(b, q, step in range(3, 12))
             if step + 1 < len(units):
                 nb, nq = units[step + 1]
                 if nq == 0:
@@ -256,15 +279,15 @@ def tile_list_email_expert_return_kernel(
                     quantize_w1(nb)
                 up(nb, nq)
                 gate(nb, nq)
-            if step == 0:
-                gather(v_plane, tab_plane, 1)
+            quantize_h(b, q)
+            if step == NB - 1:
+                v_words[1] = stream.tile([P, HALF], U32, name="v_words1", offset=NB * UNIT_BYTES + KB, align_bytes=64)
+                v_plane[1] = stream.tile([P, HALF], U8, name="v_plane1", offset=NB * UNIT_BYTES + 3 * KB, align_bytes=64)
                 gather(v_words, tab, 1)
-            if q > 0:
-                for i in ((0, 1), (2,), (3,))[b]:
-                    down(q - 1, i)
-        quantize_h(*units[-1])
+                gather(v_plane, tab_plane, 1)
+            if NB <= step < NB + 2 * NT:
+                down((step - NB) % NT, [(step - NB) // NT], False, step)
         for i in range(NT):
-            down(NQ - 1, i)
-            if i > 0:
-                finish(i - 1)
-        finish(NT - 1)
+            down(i, [2, 3], i > 0, False)
+        for i in range(NT):
+            finish(i)

@@ -89,10 +89,11 @@ def tile_list_email_expert_return_kernel(
             )
 
         nc.sync.dma_start(tab[:, T // 4 :].bitcast(I32), tab_src[:, T // 4 :])
+        units = [(b, q) for q in range(NQ) for b in range(NB)]
         rt_sb = {}
 
         def load_rt(b, q):
-            tile = stream.tile([P, PACK, Q], F32, name="rt_%d_%d" % (b, q), offset=(NB * q + b) * UNIT_BYTES, align_bytes=64)
+            tile = stream.tile([P, PACK, Q], F32, name="rt_%d_%d" % (b, q), offset=units.index((b, q)) * UNIT_BYTES, align_bytes=64)
             rows = rt[b * PASS : (b + 1) * PASS, q * Q : (q + 1) * Q]
             nc.sync.dma_start(tile[:], rows.rearrange("(p t) n -> p t n", t=PACK))
             rt_sb[(b, q)] = tile
@@ -100,11 +101,11 @@ def tile_list_email_expert_return_kernel(
         w3 = [held([P, NB, 2 * P], U32, "w3_%d" % pair) for pair in range(NT // 2)]
         w3_src = w3_words.rearrange("a p n i -> p a (n i)").bitcast(I32)
         wgo_sb = [held([P, Q], F32, "wgo_first"), held([P, S - Q], F32, "wgo_rest")]
-        load_rt(0, 0)
         load_w2(1, 2)
         load_w1(1)
-        load_rt(1, 0)
+        load_rt(0, 0)
         load_w1(2)
+        load_rt(1, 0)
         load_rt(2, 0)
         load_rt(0, 1)
         nc.sync.dma_start(w3[0][:].bitcast(I32), w3_src[:, :, : 2 * P])
@@ -127,8 +128,8 @@ def tile_list_email_expert_return_kernel(
         for i in range(NT):
             nc.sync.dma_start(x0_sb[i][:], x0[i * P : (i + 1) * P, :])
 
-        v_words = {0: held([P, HALF], U32, "v_words0")}
-        v_plane = {0: held([P, HALF], U8, "v_plane0")}
+        v_words = [held([P, HALF], U32, "v_words%d" % h) for h in range(2)]
+        v_plane = [held([P, HALF], U8, "v_plane%d" % h) for h in range(2)]
 
         def gather(dst, window, h):
             nc.vector.tensor_copy(dst[h][:], window[:].indirect(idx[:, h * HALF // 16 : (h + 1) * HALF // 16]))
@@ -153,7 +154,7 @@ def tile_list_email_expert_return_kernel(
             grouped = work.tile([P, PACK, P, PACK], BF16, name="w1_grouped", bufs=2, align_bytes=64)
             dst = grouped[:].rearrange("p t m j -> p m t j")
             src = w1_raw[b][:].rearrange("p j (m t) -> p m t j", t=PACK)
-            if b in (0,):
+            if b in (0, 1, 2):
                 nc.vector.tensor_copy(dst[:, :M_SPLIT], src[:, :M_SPLIT])
                 nc.scalar.copy(dst[:, M_SPLIT:], src[:, M_SPLIT:])
             else:
@@ -204,7 +205,7 @@ def tile_list_email_expert_return_kernel(
         h_bf = {}
 
         def combine(b, q, on_gpsimd):
-            step = NB * q + b
+            step = units.index((b, q))
             h = relay.tile([P, Q, 2, 2], BF16, name="h_%d" % step, offset=(step % 2) * KB, align_bytes=64)
             engine = nc.gpsimd if on_gpsimd else nc.vector
             engine.tensor_tensor(
@@ -216,7 +217,7 @@ def tile_list_email_expert_return_kernel(
 
         def quantize_h(b, q):
             hc[(b, q)] = stream.tile(
-                [P, Q], U32, name="hc_%d_%d" % (b, q), offset=(NB * q + b + 1) * UNIT_BYTES, align_bytes=64
+                [P, Q], U32, name="hc_%d_%d" % (b, q), offset=(units.index((b, q)) + 1) * UNIT_BYTES, align_bytes=64
             )
             hs[(b, q)] = held([P, Q], U8, "hs_%d_%d" % (b, q))
             nc.vector.quantize_mx(
@@ -267,11 +268,10 @@ def tile_list_email_expert_return_kernel(
         order_w2(0)
         quantize_w1(0)
         gather(v_words, tab, 0)
-        units = [(b, q) for q in range(NQ) for b in range(NB)]
         up(*units[0])
         gate(*units[0])
         for step, (b, q) in enumerate(units):
-            combine(b, q, step in range(3, 12))
+            combine(b, q, step in range(3, 11))
             if step + 1 < len(units):
                 nb, nq = units[step + 1]
                 if nq == 0:
@@ -280,13 +280,11 @@ def tile_list_email_expert_return_kernel(
                 up(nb, nq)
                 gate(nb, nq)
             quantize_h(b, q)
-            if step == NB - 1:
-                v_words[1] = stream.tile([P, HALF], U32, name="v_words1", offset=NB * UNIT_BYTES + KB, align_bytes=64)
-                v_plane[1] = stream.tile([P, HALF], U8, name="v_plane1", offset=NB * UNIT_BYTES + 3 * KB, align_bytes=64)
+            if step == 0:
                 gather(v_words, tab, 1)
                 gather(v_plane, tab_plane, 1)
-            if NB <= step < NB + 2 * NT:
-                down((step - NB) % NT, [(step - NB) // NT], False, step)
+            if 2 <= step < 2 + 2 * NT:
+                down((step - 2) % NT, [(step - 2) // NT], False, step)
         for i in range(NT):
             down(i, [2, 3], i > 0, False)
         for i in range(NT):

@@ -21,14 +21,20 @@ P = 128
 PACK = 4
 PASS = P * PACK
 NB = H // PASS
-Q = 256
-NQ = S // Q
+UNIT = 128
+CHUNK = 2 * UNIT
+NC = S // CHUNK
 HALF = 512
 NT = N // P
-M_SPLIT = 80
+M_SPLIT = (64, 64, 80)
 KB = 1024
-UNIT_BYTES = PACK * Q * 4
-FIRST_ON_GPSIMD = 3
+UNIT_BYTES = NB * UNIT * PACK * 4
+ACT_AT = 0
+PROD_AT = 3 * UNIT_BYTES
+H_AT = 5 * UNIT_BYTES
+W1_AT = H_AT + 12 * KB
+TAB_AT = W1_AT + 24 * KB
+RT1_AT = TAB_AT + 16 * KB
 
 
 def tile_list_email_expert_return_kernel(
@@ -37,28 +43,28 @@ def tile_list_email_expert_return_kernel(
     nc = tc.nc
     with ExitStack() as ctx:
         keep = ctx.enter_context(tc.tile_pool(name="keep", bufs=1))
-        work = ctx.enter_context(tc.tile_pool(name="work", bufs=3))
-        stream = ctx.enter_context(tc.tile_pool(name="stream", bufs=1))
-        relay = ctx.enter_context(tc.tile_pool(name="relay", bufs=1))
-        psum = ctx.enter_context(tc.psum_pool(name="psum", bufs=3))
+        work = ctx.enter_context(tc.tile_pool(name="work", bufs=2))
+        arena = ctx.enter_context(tc.tile_pool(name="arena", bufs=1))
         psum_a = ctx.enter_context(tc.psum_pool(name="psum_a", bufs=3))
+        psum_b = ctx.enter_context(tc.psum_pool(name="psum_b", bufs=3))
         psum_y = ctx.enter_context(tc.psum_pool(name="psum_y", bufs=2))
 
         def held(shape, dtype, name):
             return keep.tile(shape, dtype, name=name, align_bytes=64)
 
+        def placed(shape, dtype, name, offset):
+            return arena.tile(shape, dtype, name=name, offset=offset, align_bytes=64)
+
         idx = keep.tile([P, S // 16], U16, name="idx")
         idx2 = keep.tile([P, S // 16], U16, name="idx2")
-        tab_plane = held([P, T], U8, "tab_plane")
         w2_plane_raw = held([P, H], U8, "w2_plane_raw")
-        w3_plane = held([P, N], U8, "w3_plane")
+        tab_plane = held([P, T], U8, "tab_plane")
+        w3_plane = held([P, NB, N], U8, "w3_plane")
         nc.vector.memset(tab_plane[:].bitcast(I32), 0)
         nc.vector.memset(w2_plane_raw[:].bitcast(I32), 0)
-        nc.gpsimd.memset(w3_plane[:].bitcast(I32), 0)
-        warm = held([P, 2], F32, "warm")
-        nc.gpsimd.memset(warm[:, 0:1], 0.0)
-        nc.scalar.activation(warm[:, 1:2], warm[:, 0:1], ACT.Silu)
-        tab = held([P, T], U32, "tab")
+        nc.gpsimd.memset(w3_plane[:].rearrange("p a n -> p (a n)").bitcast(I32), 0)
+
+        tab = placed([P, T], U32, "tab", TAB_AT)
         tab_src = tab_words[0].rearrange("p t i -> p (t i)").bitcast(I32)
         nc.sync.dma_start(tab[:, : T // 4].bitcast(I32), tab_src[:, : T // 4])
         for quad in range(4):
@@ -66,67 +72,55 @@ def tile_list_email_expert_return_kernel(
                 tab_plane[32 * quad : 32 * quad + 4, :].bitcast(I32), tab_scales[0, 4 * quad : 4 * quad + 4, :].bitcast(I32)
             )
         nc.sync.dma_start(idx[:], offs)
-        w2_raw = {}
-
-        def load_w2(first, count):
-            tile = held([P, 2 * count * PASS], U8, "w2_raw%d" % first)
-            nc.sync.dma_start(tile[:].bitcast(I32), w2_words[0, :, 2 * first * PASS : 2 * (first + count) * PASS].bitcast(I32))
-            for i in range(count):
-                w2_raw[first + i] = tile[:, 2 * i * PASS : 2 * (i + 1) * PASS]
-
-        load_w2(0, 1)
-        w1_raw = {}
-
-        def load_w1(b):
-            tile = held([P, PACK, PASS], F32, "w1_raw%d" % b)
-            nc.sync.dma_start(tile[:], w1[:, b * PASS : (b + 1) * PASS].rearrange("(p j) c -> p j c", j=PACK))
-            w1_raw[b] = tile
-
-        load_w1(0)
+        w2_raw = held([P, 2 * H], U8, "w2_raw")
+        nc.sync.dma_start(w2_raw[:].bitcast(I32), w2_words[0].bitcast(I32))
         for quad in range(4):
             nc.sync.dma_start(
                 w2_plane_raw[32 * quad : 32 * quad + 4, :].bitcast(I32), w2_scales[0, 4 * quad : 4 * quad + 4, :].bitcast(I32)
             )
-
         nc.sync.dma_start(tab[:, T // 4 :].bitcast(I32), tab_src[:, T // 4 :])
-        units = [(b, q) for q in range(NQ) for b in range(NB)]
-        rt_sb = {}
 
-        def load_rt(b, q):
-            tile = stream.tile([P, PACK, Q], F32, name="rt_%d_%d" % (b, q), offset=units.index((b, q)) * UNIT_BYTES, align_bytes=64)
-            rows = rt[b * PASS : (b + 1) * PASS, q * Q : (q + 1) * Q]
-            nc.sync.dma_start(tile[:], rows.rearrange("(p t) n -> p t n", t=PACK))
-            rt_sb[(b, q)] = tile
+        w1_raw, rt_sb = {}, {}
+
+        def load_w1(b):
+            tile = placed([P, PACK, PASS], F32, "w1_raw%d" % b, W1_AT + b * 8 * KB)
+            nc.sync.dma_start(tile[:], w1[:, b * PASS : (b + 1) * PASS].rearrange("(p j) c -> p j c", j=PACK))
+            w1_raw[b] = tile
+
+        def load_rt(c, b):
+            name = "rt_%d_%d" % (c, b)
+            if c == 1:
+                tile = placed([P, PACK, CHUNK], F32, name, RT1_AT + b * 4 * KB)
+            elif c == 3:
+                tile = placed([P, PACK, CHUNK], F32, name, TAB_AT + b * 4 * KB)
+            else:
+                tile = held([P, PACK, CHUNK], F32, name)
+            queue = nc.scalar if c == 3 else nc.sync
+            rows = rt[b * PASS : (b + 1) * PASS, c * CHUNK : (c + 1) * CHUNK]
+            queue.dma_start(tile[:], rows.rearrange("(p t) n -> p t n", t=PACK))
+            rt_sb[(c, b)] = tile
 
         w3 = [held([P, NB, 2 * P], U32, "w3_%d" % pair) for pair in range(NT // 2)]
         w3_src = w3_words.rearrange("a p n i -> p a (n i)").bitcast(I32)
-        wgo_sb = [held([P, Q], F32, "wgo_first"), held([P, S - Q], F32, "wgo_rest")]
-        load_w2(1, 2)
-        load_w1(1)
-        load_rt(0, 0)
-        load_w1(2)
-        load_rt(1, 0)
-        load_rt(2, 0)
-        load_rt(0, 1)
+        wgo_first = held([P, CHUNK], F32, "wgo_first")
+        wgo_rest = held([P, S - CHUNK], F32, "wgo_rest")
+        for b in range(NB):
+            load_w1(b)
+            load_rt(0, b)
         nc.sync.dma_start(w3[0][:].bitcast(I32), w3_src[:, :, : 2 * P])
         for quad in range(4):
             nc.sync.dma_start(
-                w3_plane[32 * quad : 32 * quad + 4 * NB, :].bitcast(I32), w3_scales[:, 4 * quad : 4 * quad + 4, :].bitcast(I32)
+                w3_plane[32 * quad : 32 * quad + 4].bitcast(I32),
+                w3_scales[:, 4 * quad : 4 * quad + 4, :].rearrange("a r n -> r a n").bitcast(I32),
             )
-        nc.sync.dma_start(wgo_sb[0][:], wgo[:, :Q])
+        nc.sync.dma_start(wgo_first[:], wgo[:, :CHUNK])
         nc.sync.dma_start(idx2[:], offs2)
-        load_rt(1, 1)
-        load_rt(2, 1)
-        nc.sync.dma_start(w3[1][:].bitcast(I32), w3_src[:, :, 2 * P :])
-        load_rt(0, 2)
-        load_rt(1, 2)
-        nc.sync.dma_start(wgo_sb[1][:], wgo[:, Q:])
-        load_rt(2, 2)
         for b in range(NB):
-            load_rt(b, 3)
-        x0_sb = [held([P, S], F32, "x0_%d" % i) for i in range(NT)]
-        for i in range(NT):
-            nc.sync.dma_start(x0_sb[i][:], x0[i * P : (i + 1) * P, :])
+            load_rt(1, b)
+        nc.sync.dma_start(w3[1][:].bitcast(I32), w3_src[:, :, 2 * P :])
+        for b in range(NB):
+            load_rt(2, b)
+        nc.sync.dma_start(wgo_rest[:], wgo[:, CHUNK:])
 
         v_words = [held([P, HALF], U32, "v_words%d" % h) for h in range(2)]
         v_plane = [held([P, HALF], U8, "v_plane%d" % h) for h in range(2)]
@@ -140,7 +134,7 @@ def tile_list_email_expert_return_kernel(
         def order_w2(b):
             nc.vector.tensor_copy(
                 w2c[b][:].bitcast(U16).rearrange("p (t m) -> p t m", t=PACK),
-                w2_raw[b].bitcast(U16).rearrange("p (m t) -> p t m", t=PACK),
+                w2_raw[:, 2 * b * PASS : 2 * (b + 1) * PASS].bitcast(U16).rearrange("p (m t) -> p t m", t=PACK),
             )
             nc.vector.tensor_copy(
                 w2s[b][:].rearrange("p (t m) -> p t m", t=PACK),
@@ -151,141 +145,206 @@ def tile_list_email_expert_return_kernel(
         w1s = [held([P, PASS], U8, "w1s%d" % b) for b in range(NB)]
 
         def quantize_w1(b):
-            grouped = work.tile([P, PACK, P, PACK], BF16, name="w1_grouped", bufs=2, align_bytes=64)
+            grouped = work.tile([P, PACK, P, PACK], BF16, name="w1_grouped", align_bytes=64)
             dst = grouped[:].rearrange("p t m j -> p m t j")
             src = w1_raw[b][:].rearrange("p j (m t) -> p m t j", t=PACK)
-            if b in (0, 1, 2):
-                nc.vector.tensor_copy(dst[:, :M_SPLIT], src[:, :M_SPLIT])
-                nc.scalar.copy(dst[:, M_SPLIT:], src[:, M_SPLIT:])
+            low, high = slice(0, M_SPLIT[b]), slice(M_SPLIT[b], P)
+            if b == 1:
+                nc.gpsimd.tensor_scalar(dst[:, low], src[:, low], 1.0, 0.0, op0=MULT, op1=ADD)
             else:
-                nc.scalar.copy(dst, src)
+                nc.vector.tensor_copy(dst[:, low], src[:, low])
+            if b == 0:
+                nc.gpsimd.tensor_scalar(dst[:, high], src[:, high], 1.0, 0.0, op0=MULT, op1=ADD)
+            else:
+                nc.scalar.copy(dst[:, high], src[:, high])
             nc.vector.quantize_mx(
                 out=w1c[b][:].bitcast(FP8X4), scales=w1s[b][:], in_=grouped[:].rearrange("p t m j -> p (t m j)")
             )
 
-        def v_operand(q):
-            cols = slice((q % 2) * Q, (q % 2 + 1) * Q)
-            return v_words[q // 2][:, cols].bitcast(FP8X4), v_plane[q // 2][:, cols]
-
-        gated = {}
-
-        def up(b, q):
-            rhs, rhs_scale = v_operand(q)
-            prod = work.tile([P, 2, Q, 2], F32, name="prod", bufs=2)
-            for u in range(2):
-                bank = psum.tile([P, 2, Q], F32, name="bank_b")
-                for e in range(2):
-                    t = 2 * u + e
-                    nc.tensor.matmul_mx(
-                        out=bank[:, e, :], lhsT=w2c[b][:, 2 * t * P : 2 * (t + 1) * P].bitcast(FP4X4),
-                        lhsT_scale=w2s[b][:, t * P : (t + 1) * P], rhs=rhs, rhs_scale=rhs_scale, start=True, stop=True,
-                    )
-                nc.vector.tensor_tensor(
-                    prod[:, u, :, :], bank[:].rearrange("p e n -> p n e"),
-                    rt_sb[(b, q)][:, 2 * u : 2 * u + 2, :].rearrange("p e n -> p n e"), MULT,
+        def four_slots(pool, codes, plane, dtype, width, j):
+            cols = slice((j * UNIT) % HALF, (j * UNIT) % HALF + UNIT)
+            rhs, rhs_scale = v_words[j * UNIT // HALF][:, cols].bitcast(FP8X4), v_plane[j * UNIT // HALF][:, cols]
+            bank = pool.tile([P, PACK, UNIT], F32, name="bank")
+            for t in range(PACK):
+                nc.tensor.matmul_mx(
+                    out=bank[:, t, :], lhsT=codes[:, width * t * P : width * (t + 1) * P].bitcast(dtype),
+                    lhsT_scale=plane[:, t * P : (t + 1) * P], rhs=rhs, rhs_scale=rhs_scale, start=True, stop=True,
                 )
-            gated[(b, q)] = prod
+            return bank
 
-        acts = {}
+        def routed(j, b, dst):
+            bank = four_slots(psum_b, w2c[b], w2s[b], FP4X4, 2, j)
+            factor = rt_sb[(j // 2, b)][:, :, (j % 2) * UNIT : (j % 2 + 1) * UNIT]
+            nc.vector.tensor_tensor(
+                dst.rearrange("p (c i) t -> p c t i", i=2), bank[:].rearrange("p t (c i) -> p c t i", i=2),
+                factor.rearrange("p t (c i) -> p c t i", i=2), MULT,
+            )
 
-        def gate(b, q):
-            rhs, rhs_scale = v_operand(q)
-            act = work.tile([P, 2, Q, 2], F32, name="act", bufs=2)
-            for u in range(2):
-                bank = psum_a.tile([P, 2, Q], F32, name="bank_a")
-                for e in range(2):
-                    t = 2 * u + e
+        def gate(j, b, dst):
+            bank = four_slots(psum_a, w1c[b], w1s[b], FP8X4, 1, j)
+            nc.scalar.activation(dst, bank[:].rearrange("p t n -> p n t"), ACT.Silu)
+
+        h, hc, hs = {}, {}, {}
+
+        def new_h(c):
+            h[c] = placed([P, NB, CHUNK, PACK], BF16, "h%d" % c, H_AT + c * 2 * KB)
+
+        acts, prods = {}, {}
+
+        def prepare(j):
+            acts[j] = placed([P, NB, UNIT, PACK], F32, "act%d" % j, ACT_AT + (j % 3) * UNIT_BYTES)
+            prods[j] = placed([P, NB, UNIT, PACK], F32, "prod%d" % j, PROD_AT + (j % 2) * UNIT_BYTES)
+            for b in range(NB):
+                routed(j, b, prods[j][:, b])
+                gate(j, b, acts[j][:, b])
+
+        def combine(j):
+            if j % 2 == 0:
+                new_h(j // 2)
+            dst = h[j // 2][:, :, (j % 2) * UNIT : (j % 2 + 1) * UNIT, :].rearrange("p b n t -> p b (n t)")
+            nc.gpsimd.tensor_tensor(
+                dst, acts[j][:].rearrange("p b n t -> p b (n t)"), prods[j][:].rearrange("p b n t -> p b (n t)"), MULT
+            )
+
+        def quantize_h(c):
+            hc[c] = work.tile([P, NB * CHUNK], U32, name="hc", align_bytes=64)
+            hs[c] = work.tile([P, NB * CHUNK], U8, name="hs", align_bytes=64)
+            flat = h[c][:].rearrange("p b n t -> p (b n t)")
+            for first, last in ((2 * CHUNK, 3 * CHUNK), (0, 2 * CHUNK)):
+                nc.vector.quantize_mx(
+                    out=hc[c][:, first:last].bitcast(FP8X4), scales=hs[c][:, first:last], in_=flat[:, PACK * first : PACK * last]
+                )
+
+        def down(c, pair):
+            bank = psum_y.tile([P, 2, CHUNK], F32, name="bank_y")
+            for e in range(2):
+                i = 2 * pair + e
+                for b in range(NB):
+                    cols = slice(b * CHUNK, (b + 1) * CHUNK)
                     nc.tensor.matmul_mx(
-                        out=bank[:, e, :], lhsT=w1c[b][:, t * P : (t + 1) * P].bitcast(FP8X4),
-                        lhsT_scale=w1s[b][:, t * P : (t + 1) * P], rhs=rhs, rhs_scale=rhs_scale, start=True, stop=True,
+                        out=bank[:, e, :], lhsT=w3[pair][:, b, e * P : (e + 1) * P].bitcast(FP8X4),
+                        lhsT_scale=w3_plane[:, b, i * P : (i + 1) * P],
+                        rhs=hc[c][:, cols].bitcast(FP8X4), rhs_scale=hs[c][:, cols], start=(b == 0), stop=(b == NB - 1),
                     )
-                nc.scalar.activation(act[:, u, :, :], bank[:].rearrange("p e n -> p n e"), ACT.Silu)
-            acts[(b, q)] = act
+            return bank
 
-        h_bf = {}
+        def factor_of(c):
+            cols = wgo_first[:] if c == 0 else wgo_rest[:, (c - 1) * CHUNK : c * CHUNK]
+            return cols.unsqueeze(1).to_broadcast([P, 2, CHUNK])
 
-        def combine(b, q, on_gpsimd):
-            step = units.index((b, q))
-            h = relay.tile([P, Q, 2, 2], BF16, name="h_%d" % step, offset=(step % 2) * KB, align_bytes=64)
-            engine = nc.gpsimd if on_gpsimd else nc.vector
-            engine.tensor_tensor(
-                h[:], acts[(b, q)][:].rearrange("p u n e -> p n u e"), gated[(b, q)][:].rearrange("p u n e -> p n u e"), MULT
-            )
-            h_bf[(b, q)] = h
+        y_sb = {}
 
-        hc, hs = {}, {}
-
-        def quantize_h(b, q):
-            hc[(b, q)] = stream.tile(
-                [P, Q], U32, name="hc_%d_%d" % (b, q), offset=(units.index((b, q)) + 1) * UNIT_BYTES, align_bytes=64
-            )
-            hs[(b, q)] = held([P, Q], U8, "hs_%d_%d" % (b, q))
-            nc.vector.quantize_mx(
-                out=hc[(b, q)][:].bitcast(FP8X4), scales=hs[(b, q)][:], in_=h_bf[(b, q)][:].rearrange("p n u e -> p (n u e)")
-            )
+        def down_to_sbuf(c, pair):
+            bank = down(c, pair)
+            y_sb[(c, pair)] = work.tile([P, 2, CHUNK], F32, name="y%d" % pair)
+            nc.scalar.copy(y_sb[(c, pair)][:], bank[:])
 
         page = [held([P, S], F32, "page%d" % i) for i in range(NT)]
+        weighted = {}
 
-        def down(i, quarters, on_gpsimd, paced):
-            width = len(quarters) * Q
-            if paced or i < 2:
-                bank = psum_y.tile([P, width], F32, name="bank_y")
+        def weigh(c, pair):
+            if pair == 0:
+                offset = ACT_AT + ((2 * c + 2) % 3) * UNIT_BYTES
             else:
-                bank = psum_a.tile([P, width], F32, name="bank_a")
-            cols = slice(i * P, (i + 1) * P)
-            for e, q in enumerate(quarters):
-                for b in range(NB):
-                    nc.tensor.matmul_mx(
-                        out=bank[:, e * Q : (e + 1) * Q], lhsT=w3[i // 2][:, b, (i % 2) * P : (i % 2 + 1) * P].bitcast(FP8X4),
-                        lhsT_scale=w3_plane[4 * b : P, cols],
-                        rhs=hc[(b, q)][:].bitcast(FP8X4), rhs_scale=hs[(b, q)][:], start=(b == 0), stop=(b == NB - 1),
-                    )
-            first = quarters[0] * Q
-            factor = wgo_sb[0][:] if first == 0 else wgo_sb[1][:, first - Q : first - Q + width]
-            if paced:
-                weighted = relay.tile([P, width], F32, name="weighted_%d" % paced, offset=(paced % 2) * 2 * KB, align_bytes=64)
-            else:
-                weighted = work.tile([P, width], F32, name="weighted", bufs=4)
-            if on_gpsimd:
-                y = work.tile([P, width], F32, name=("y", "stage_a", "stage_b")[i - 1], bufs=1)
-                nc.scalar.copy(y[:], bank[:])
-                nc.gpsimd.tensor_tensor(weighted[:], y[:], factor, MULT)
-            else:
-                nc.vector.tensor_tensor(weighted[:], bank[:], factor, MULT)
-            nc.vector.tensor_copy(page[i][:].indirect(idx2[:, first // 16 : (first + width) // 16]), weighted[:])
+                offset = H_AT + (c + 1) * 2 * KB
+            weighted[(c, pair)] = placed([P, 2, CHUNK], F32, "weighted_%d_%d" % (c, pair), offset)
+            nc.gpsimd.tensor_tensor(weighted[(c, pair)][:], y_sb[(c, pair)][:], factor_of(c), MULT)
+
+        def scatter(c, pair):
+            for e in range(2):
+                offsets = idx2[:, c * CHUNK // 16 : (c + 1) * CHUNK // 16]
+                nc.vector.tensor_copy(page[2 * pair + e][:].indirect(offsets), weighted[(c, pair)][:, e, :])
 
         def finish(i):
-            pre = work.tile([P, S], F32, name="stage_b" if i == 1 else "stage_a", bufs=1)
-            width = Q if i == NT - 1 else HALF
+            last = i == NT - 1
+            width = CHUNK if last else HALF
+            if not last:
+                nc.gpsimd.tensor_tensor(x0_sb[i][:], page[i][:], x0_sb[i][:], ADD)
             for piece in range(S // width):
                 cols = slice(piece * width, (piece + 1) * width)
-                engine = nc.vector if i == NT - 1 else nc.gpsimd
-                engine.tensor_tensor(pre[:, cols], page[i][:, cols], x0_sb[i][:, cols], ADD)
-                nc.scalar.activation(x0_sb[i][:, cols], pre[:, cols], ACT.Tanh)
+                if last:
+                    nc.vector.tensor_tensor(x0_sb[i][:, cols], page[i][:, cols], x0_sb[i][:, cols], ADD)
+                nc.scalar.activation(x0_sb[i][:, cols], x0_sb[i][:, cols], ACT.Tanh)
                 nc.sync.dma_start(out[i * P : (i + 1) * P, cols], x0_sb[i][:, cols])
 
         gather(v_plane, tab_plane, 0)
-        order_w2(0)
-        quantize_w1(0)
+        gather(v_plane, tab_plane, 1)
+        for b in range(NB):
+            order_w2(b)
         gather(v_words, tab, 0)
-        up(*units[0])
-        gate(*units[0])
-        for step, (b, q) in enumerate(units):
-            combine(b, q, step in range(3, 11))
-            if step + 1 < len(units):
-                nb, nq = units[step + 1]
-                if nq == 0:
-                    order_w2(nb)
-                    quantize_w1(nb)
-                up(nb, nq)
-                gate(nb, nq)
-            quantize_h(b, q)
-            if step == 0:
-                gather(v_words, tab, 1)
-                gather(v_plane, tab_plane, 1)
-            if 2 <= step < 2 + 2 * NT:
-                down((step - 2) % NT, [(step - 2) // NT], False, step)
-        for i in range(NT):
-            down(i, [2, 3], i > 0, False)
+        gather(v_words, tab, 1)
+        act_first = placed([P, NB, CHUNK, PACK], F32, "act_first", ACT_AT)
+        prod_first = placed([P, NB, CHUNK, PACK], F32, "prod_first", TAB_AT)
+        new_h(0)
+        for b in range(NB):
+            quantize_w1(b)
+            for j in range(2):
+                routed(j, b, prod_first[:, b, j * UNIT : (j + 1) * UNIT, :])
+                gate(j, b, act_first[:, b, j * UNIT : (j + 1) * UNIT, :])
+            engine = nc.vector if b == NB - 1 else nc.gpsimd
+            engine.tensor_tensor(h[0][:, b], act_first[:, b], prod_first[:, b], MULT)
+        for b in range(NB):
+            load_rt(3, b)
+
+        y_late = held([P, 2 * CHUNK], F32, "y_late")
+        for c in range(NC - 1):
+            quantize_h(c)
+            if c == 0:
+                prepare(2)
+                bank_first = down(0, 0)
+            else:
+                down_to_sbuf(c, 0)
+                weigh(c - 1, 1)
+            if c < NC - 2:
+                down_to_sbuf(c, 1)
+            else:
+                bank = down(c, 1)
+                y_sb[(c, 1)] = work.tile([P, CHUNK], F32, name="y1")
+                nc.scalar.copy(y_sb[(c, 1)][:], bank[:, 0, :])
+                nc.scalar.copy(y_late[:, :CHUNK], bank[:, 1, :])
+            combine(2 * c + 2)
+            prepare(2 * c + 3)
+            if c > 0:
+                scatter(c - 1, 1)
+                weigh(c, 0)
+            else:
+                weighted[(0, 0)] = placed([P, 2, CHUNK], F32, "weighted_first", RT1_AT + (NB - 1) * 4 * KB)
+                nc.vector.tensor_tensor(weighted[(0, 0)][:], bank_first[:], factor_of(0), MULT)
+            combine(2 * c + 3)
+            if c == 0:
+                scatter(c, 0)
+                x0_sb = [placed([P, S], F32, "x0_%d" % i, RT1_AT + i * 4 * KB) for i in range(NT)]
+                for i in range(NT):
+                    nc.sync.dma_start(x0_sb[i][:], x0[i * P : (i + 1) * P, :])
+            if c + 2 < NC:
+                prepare(2 * c + 4)
+            if c > 0:
+                scatter(c, 0)
+
+        last = NC - 1
+        quantize_h(last)
+
+        def weigh_page(name, offset, y, first, width):
+            tile = placed([P, width], F32, name, offset)
+            nc.gpsimd.tensor_tensor(tile[:], y, wgo_rest[:, first - CHUNK : first - CHUNK + width], MULT)
+            return tile
+
+        def scatter_page(i, values, first, width):
+            nc.vector.tensor_copy(page[i][:].indirect(idx2[:, first // 16 : (first + width) // 16]), values)
+
+        held_back = weigh_page("held_back", H_AT + last * 2 * KB, y_sb[(last - 1, 1)][:], (last - 1) * CHUNK, CHUNK)
+        bank = down(last, 0)
+        weighted[(last, 0)] = placed([P, 2, CHUNK], F32, "weighted_last", PROD_AT)
+        nc.vector.tensor_tensor(weighted[(last, 0)][:], bank[:], factor_of(last), MULT)
+        scatter(last, 0)
+        bank = down(last, 1)
+        y_third = work.tile([P, CHUNK], F32, name="y1")
+        nc.scalar.copy(y_third[:], bank[:, 0, :])
+        nc.scalar.copy(y_late[:, CHUNK:], bank[:, 1, :])
+        third = weigh_page("third", ACT_AT, y_third[:], last * CHUNK, CHUNK)
+        fourth = weigh_page("fourth", ACT_AT + UNIT_BYTES, y_late[:], (last - 1) * CHUNK, 2 * CHUNK)
+        scatter_page(2, held_back[:], (last - 1) * CHUNK, CHUNK)
+        scatter_page(2, third[:], last * CHUNK, CHUNK)
+        scatter_page(3, fourth[:], (last - 1) * CHUNK, 2 * CHUNK)
         for i in range(NT):
             finish(i)

@@ -26,15 +26,16 @@ CHUNK = 2 * UNIT
 NC = S // CHUNK
 HALF = 512
 NT = N // P
-M_SPLIT = (64, 64, 80)
 KB = 1024
+RT_ORDER = (2, 0, 1)
 UNIT_BYTES = NB * UNIT * PACK * 4
 ACT_AT = 0
-PROD_AT = 3 * UNIT_BYTES
-H_AT = 5 * UNIT_BYTES
-W1_AT = H_AT + 12 * KB
+PROD_AT = 4 * UNIT_BYTES
+H_AT = PROD_AT + 2 * UNIT_BYTES
+W1_AT = H_AT + 6 * KB
 TAB_AT = W1_AT + 24 * KB
 RT1_AT = TAB_AT + 16 * KB
+RT_AT = (None, RT1_AT, RT1_AT + 12 * KB, RT1_AT + 24 * KB)
 
 
 def tile_list_email_expert_return_kernel(
@@ -89,24 +90,26 @@ def tile_list_email_expert_return_kernel(
 
         def load_rt(c, b):
             name = "rt_%d_%d" % (c, b)
-            if c == 1:
-                tile = placed([P, PACK, CHUNK], F32, name, RT1_AT + b * 4 * KB)
-            elif c == 3:
-                tile = placed([P, PACK, CHUNK], F32, name, TAB_AT + b * 4 * KB)
-            else:
+            if c == 0:
                 tile = held([P, PACK, CHUNK], F32, name)
-            queue = nc.scalar if c == 3 else nc.sync
+            else:
+                tile = placed([P, PACK, CHUNK], F32, name, RT_AT[c] + b * 4 * KB)
             rows = rt[b * PASS : (b + 1) * PASS, c * CHUNK : (c + 1) * CHUNK]
-            queue.dma_start(tile[:], rows.rearrange("(p t) n -> p t n", t=PACK))
+            nc.sync.dma_start(tile[:], rows.rearrange("(p t) n -> p t n", t=PACK))
             rt_sb[(c, b)] = tile
 
         w3 = [held([P, NB, 2 * P], U32, "w3_%d" % pair) for pair in range(NT // 2)]
         w3_src = w3_words.rearrange("a p n i -> p a (n i)").bitcast(I32)
         wgo_first = held([P, CHUNK], F32, "wgo_first")
         wgo_rest = held([P, S - CHUNK], F32, "wgo_rest")
-        for b in range(NB):
-            load_w1(b)
-            load_rt(0, b)
+        load_w1(0)
+        load_rt(0, 0)
+        load_w1(1)
+        load_rt(0, 1)
+        load_w1(2)
+        load_rt(0, 2)
+        load_rt(1, 0)
+        load_rt(1, 1)
         nc.sync.dma_start(w3[0][:].bitcast(I32), w3_src[:, :, : 2 * P])
         for quad in range(4):
             nc.sync.dma_start(
@@ -115,12 +118,13 @@ def tile_list_email_expert_return_kernel(
             )
         nc.sync.dma_start(wgo_first[:], wgo[:, :CHUNK])
         nc.sync.dma_start(idx2[:], offs2)
-        for b in range(NB):
-            load_rt(1, b)
+        load_rt(1, 2)
         nc.sync.dma_start(w3[1][:].bitcast(I32), w3_src[:, :, 2 * P :])
         for b in range(NB):
             load_rt(2, b)
         nc.sync.dma_start(wgo_rest[:], wgo[:, CHUNK:])
+        for b in range(NB):
+            load_rt(3, b)
 
         v_words = [held([P, HALF], U32, "v_words%d" % h) for h in range(2)]
         v_plane = [held([P, HALF], U8, "v_plane%d" % h) for h in range(2)]
@@ -148,15 +152,14 @@ def tile_list_email_expert_return_kernel(
             grouped = work.tile([P, PACK, P, PACK], BF16, name="w1_grouped", align_bytes=64)
             dst = grouped[:].rearrange("p t m j -> p m t j")
             src = w1_raw[b][:].rearrange("p j (m t) -> p m t j", t=PACK)
-            low, high = slice(0, M_SPLIT[b]), slice(M_SPLIT[b], P)
-            if b == 1:
-                nc.gpsimd.tensor_scalar(dst[:, low], src[:, low], 1.0, 0.0, op0=MULT, op1=ADD)
+            if b == NB - 1:
+                nc.vector.tensor_copy(dst, src)
             else:
-                nc.vector.tensor_copy(dst[:, low], src[:, low])
-            if b == 0:
-                nc.gpsimd.tensor_scalar(dst[:, high], src[:, high], 1.0, 0.0, op0=MULT, op1=ADD)
-            else:
-                nc.scalar.copy(dst[:, high], src[:, high])
+                nc.gpsimd.tensor_scalar(dst[:, : P // 2], src[:, : P // 2], 1.0, 0.0, op0=MULT, op1=ADD)
+                if b == 0:
+                    nc.scalar.copy(dst[:, P // 2 :], src[:, P // 2 :])
+                else:
+                    nc.vector.tensor_copy(dst[:, P // 2 :], src[:, P // 2 :])
             nc.vector.quantize_mx(
                 out=w1c[b][:].bitcast(FP8X4), scales=w1s[b][:], in_=grouped[:].rearrange("p t m j -> p (t m j)")
             )
@@ -187,27 +190,29 @@ def tile_list_email_expert_return_kernel(
         h, hc, hs = {}, {}, {}
 
         def new_h(c):
-            h[c] = placed([P, NB, CHUNK, PACK], BF16, "h%d" % c, H_AT + c * 2 * KB)
+            h[c] = placed([P, NB, CHUNK, PACK], BF16, "h%d" % c, H_AT)
 
         acts, prods = {}, {}
 
-        def prepare(j):
-            acts[j] = placed([P, NB, UNIT, PACK], F32, "act%d" % j, ACT_AT + (j % 3) * UNIT_BYTES)
-            prods[j] = placed([P, NB, UNIT, PACK], F32, "prod%d" % j, PROD_AT + (j % 2) * UNIT_BYTES)
-            for b in range(NB):
-                routed(j, b, prods[j][:, b])
-                gate(j, b, acts[j][:, b])
+        def prepare(c, b):
+            if b == 0:
+                acts[c] = placed([P, NB, CHUNK, PACK], F32, "act%d" % c, (ACT_AT if c < 2 else W1_AT) + (c % 2) * 2 * UNIT_BYTES)
+                prods[c] = placed([P, NB, CHUNK, PACK], F32, "prod%d" % c, PROD_AT if c % 2 else TAB_AT)
+            for u in range(2):
+                routed(2 * c + u, b, prods[c][:, b, u * UNIT : (u + 1) * UNIT, :])
+                gate(2 * c + u, b, acts[c][:, b, u * UNIT : (u + 1) * UNIT, :])
 
-        def combine(j):
-            if j % 2 == 0:
-                new_h(j // 2)
-            dst = h[j // 2][:, :, (j % 2) * UNIT : (j % 2 + 1) * UNIT, :].rearrange("p b n t -> p b (n t)")
-            nc.gpsimd.tensor_tensor(
-                dst, acts[j][:].rearrange("p b n t -> p b (n t)"), prods[j][:].rearrange("p b n t -> p b (n t)"), MULT
-            )
+        def combine(c, u):
+            if u == 0:
+                new_h(c)
+            parts = [t[c][:, :, u * UNIT : (u + 1) * UNIT, :].rearrange("p b n t -> p b (n t)") for t in (h, acts, prods)]
+            nc.gpsimd.tensor_tensor(parts[0], parts[1], parts[2], MULT)
 
         def quantize_h(c):
-            hc[c] = work.tile([P, NB * CHUNK], U32, name="hc", align_bytes=64)
+            if c + 1 < NC:
+                hc[c] = placed([P, NB * CHUNK], U32, "hc%d" % c, RT_AT[c + 1] + 4 * KB)
+            else:
+                hc[c] = held([P, NB * CHUNK], U32, "hc%d" % c)
             hs[c] = work.tile([P, NB * CHUNK], U8, name="hs", align_bytes=64)
             flat = h[c][:].rearrange("p b n t -> p (b n t)")
             for first, last in ((2 * CHUNK, 3 * CHUNK), (0, 2 * CHUNK)):
@@ -216,15 +221,18 @@ def tile_list_email_expert_return_kernel(
                 )
 
         def down(c, pair):
-            bank = psum_y.tile([P, 2, CHUNK], F32, name="bank_y")
-            for e in range(2):
-                i = 2 * pair + e
-                for b in range(NB):
+            if c == 0 and pair == 1:
+                bank = psum_a.tile([P, 2, CHUNK], F32, name="bank")
+            else:
+                bank = psum_y.tile([P, 2, CHUNK], F32, name="bank_y")
+            for b in RT_ORDER:
+                for e in range(2):
+                    i = 2 * pair + e
                     cols = slice(b * CHUNK, (b + 1) * CHUNK)
                     nc.tensor.matmul_mx(
                         out=bank[:, e, :], lhsT=w3[pair][:, b, e * P : (e + 1) * P].bitcast(FP8X4),
                         lhsT_scale=w3_plane[:, b, i * P : (i + 1) * P],
-                        rhs=hc[c][:, cols].bitcast(FP8X4), rhs_scale=hs[c][:, cols], start=(b == 0), stop=(b == NB - 1),
+                        rhs=hc[c][:, cols].bitcast(FP8X4), rhs_scale=hs[c][:, cols], start=(b == 2 and e == 0), stop=(b == 1 and e == 1),
                     )
             return bank
 
@@ -242,13 +250,14 @@ def tile_list_email_expert_return_kernel(
         page = [held([P, S], F32, "page%d" % i) for i in range(NT)]
         weighted = {}
 
-        def weigh(c, pair):
-            if pair == 0:
-                offset = ACT_AT + ((2 * c + 2) % 3) * UNIT_BYTES
-            else:
-                offset = H_AT + (c + 1) * 2 * KB
-            weighted[(c, pair)] = placed([P, 2, CHUNK], F32, "weighted_%d_%d" % (c, pair), offset)
-            nc.gpsimd.tensor_tensor(weighted[(c, pair)][:], y_sb[(c, pair)][:], factor_of(c), MULT)
+        def weigh_first_pair(c, offset):
+            bank = down(c, 0)
+            weighted[(c, 0)] = placed([P, 2, CHUNK], F32, "weighted_%d_0" % c, offset)
+            nc.vector.tensor_tensor(weighted[(c, 0)][:], bank[:], factor_of(c), MULT)
+
+        def weigh_second_pair(c):
+            weighted[(c, 1)] = placed([P, 2, CHUNK], F32, "weighted_%d_1" % c, RT_AT[c + 2] + 10 * KB)
+            nc.gpsimd.tensor_tensor(weighted[(c, 1)][:], y_sb[(c, 1)][:], factor_of(c), MULT)
 
         def scatter(c, pair):
             for e in range(2):
@@ -258,13 +267,14 @@ def tile_list_email_expert_return_kernel(
         def finish(i):
             last = i == NT - 1
             width = CHUNK if last else HALF
+            pre = placed([P, S], F32, "pre%d" % i, TAB_AT + (1 if last else i) * 4 * KB)
             if not last:
-                nc.gpsimd.tensor_tensor(x0_sb[i][:], page[i][:], x0_sb[i][:], ADD)
+                nc.gpsimd.tensor_tensor(pre[:], page[i][:], x0_sb[i][:], ADD)
             for piece in range(S // width):
                 cols = slice(piece * width, (piece + 1) * width)
                 if last:
-                    nc.vector.tensor_tensor(x0_sb[i][:, cols], page[i][:, cols], x0_sb[i][:, cols], ADD)
-                nc.scalar.activation(x0_sb[i][:, cols], x0_sb[i][:, cols], ACT.Tanh)
+                    nc.vector.tensor_tensor(pre[:, cols], page[i][:, cols], x0_sb[i][:, cols], ADD)
+                nc.scalar.activation(x0_sb[i][:, cols], pre[:, cols], ACT.Tanh)
                 nc.sync.dma_start(out[i * P : (i + 1) * P, cols], x0_sb[i][:, cols])
 
         gather(v_plane, tab_plane, 0)
@@ -273,77 +283,59 @@ def tile_list_email_expert_return_kernel(
             order_w2(b)
         gather(v_words, tab, 0)
         gather(v_words, tab, 1)
-        act_first = placed([P, NB, CHUNK, PACK], F32, "act_first", ACT_AT)
-        prod_first = placed([P, NB, CHUNK, PACK], F32, "prod_first", TAB_AT)
         new_h(0)
         for b in range(NB):
             quantize_w1(b)
-            for j in range(2):
-                routed(j, b, prod_first[:, b, j * UNIT : (j + 1) * UNIT, :])
-                gate(j, b, act_first[:, b, j * UNIT : (j + 1) * UNIT, :])
-            engine = nc.vector if b == NB - 1 else nc.gpsimd
-            engine.tensor_tensor(h[0][:, b], act_first[:, b], prod_first[:, b], MULT)
-        for b in range(NB):
-            load_rt(3, b)
+            prepare(0, b)
+            for part in (slice(0, UNIT), slice(UNIT, CHUNK)) if b == NB - 1 else (slice(0, CHUNK),):
+                nc.gpsimd.tensor_tensor(h[0][:, b, part], acts[0][:, b, part], prods[0][:, b, part], MULT)
+        prepare(1, 0)
+        prepare(1, 1)
 
         y_late = held([P, 2 * CHUNK], F32, "y_late")
-        for c in range(NC - 1):
-            quantize_h(c)
-            if c == 0:
-                prepare(2)
-                bank_first = down(0, 0)
-            else:
-                down_to_sbuf(c, 0)
-                weigh(c - 1, 1)
-            if c < NC - 2:
-                down_to_sbuf(c, 1)
-            else:
-                bank = down(c, 1)
-                y_sb[(c, 1)] = work.tile([P, CHUNK], F32, name="y1")
-                nc.scalar.copy(y_sb[(c, 1)][:], bank[:, 0, :])
-                nc.scalar.copy(y_late[:, :CHUNK], bank[:, 1, :])
-            combine(2 * c + 2)
-            prepare(2 * c + 3)
-            if c > 0:
-                scatter(c - 1, 1)
-                weigh(c, 0)
-            else:
-                weighted[(0, 0)] = placed([P, 2, CHUNK], F32, "weighted_first", RT1_AT + (NB - 1) * 4 * KB)
-                nc.vector.tensor_tensor(weighted[(0, 0)][:], bank_first[:], factor_of(0), MULT)
-            combine(2 * c + 3)
-            if c == 0:
-                scatter(c, 0)
-                x0_sb = [placed([P, S], F32, "x0_%d" % i, RT1_AT + i * 4 * KB) for i in range(NT)]
-                for i in range(NT):
-                    nc.sync.dma_start(x0_sb[i][:], x0[i * P : (i + 1) * P, :])
-            if c + 2 < NC:
-                prepare(2 * c + 4)
-            if c > 0:
-                scatter(c, 0)
 
-        last = NC - 1
-        quantize_h(last)
-
-        def weigh_page(name, offset, y, first, width):
-            tile = placed([P, width], F32, name, offset)
-            nc.gpsimd.tensor_tensor(tile[:], y, wgo_rest[:, first - CHUNK : first - CHUNK + width], MULT)
+        def third_page(c):
+            bank = down(c, 1)
+            tile = work.tile([P, CHUNK], F32, name="third")
+            nc.scalar.copy(y_late[:, (c - NC + 2) * CHUNK : (c - NC + 3) * CHUNK], bank[:, 1, :])
+            nc.vector.tensor_tensor(tile[:], bank[:, 0, :], wgo_rest[:, (c - 1) * CHUNK : c * CHUNK], MULT)
             return tile
 
         def scatter_page(i, values, first, width):
             nc.vector.tensor_copy(page[i][:].indirect(idx2[:, first // 16 : (first + width) // 16]), values)
 
-        held_back = weigh_page("held_back", H_AT + last * 2 * KB, y_sb[(last - 1, 1)][:], (last - 1) * CHUNK, CHUNK)
-        bank = down(last, 0)
-        weighted[(last, 0)] = placed([P, 2, CHUNK], F32, "weighted_last", PROD_AT)
-        nc.vector.tensor_tensor(weighted[(last, 0)][:], bank[:], factor_of(last), MULT)
+        for c in range(NC - 1):
+            quantize_h(c)
+            prepare(c + 1, 2)
+            combine(c + 1, 0)
+            weigh_first_pair(c, RT_AT[c + 1] + (NB - 1) * 4 * KB)
+            if c > 0:
+                weigh_second_pair(c - 1)
+            if c < NC - 2:
+                down_to_sbuf(c, 1)
+            else:
+                third = third_page(c)
+            combine(c + 1, 1)
+            if c == 0:
+                x0_sb = [placed([P, S], F32, "x0_%d" % i, ACT_AT + i * 4 * KB) for i in range(NT)]
+                for i in range(NT):
+                    nc.sync.dma_start(x0_sb[i][:], x0[i * P : (i + 1) * P, :])
+            scatter(c, 0)
+            if c > 0:
+                scatter(c - 1, 1)
+            if c == NC - 2:
+                scatter_page(2, third[:], c * CHUNK, CHUNK)
+            if c + 2 < NC:
+                prepare(c + 2, 0)
+                prepare(c + 2, 1)
+
+        last = NC - 1
+        quantize_h(last)
+        weigh_first_pair(last, PROD_AT)
+        third = third_page(last)
+        fourth = placed([P, 2 * CHUNK], F32, "fourth", H_AT)
+        nc.gpsimd.tensor_tensor(fourth[:], y_late[:], wgo_rest[:, CHUNK:], MULT)
         scatter(last, 0)
-        bank = down(last, 1)
-        y_third = work.tile([P, CHUNK], F32, name="y1")
-        nc.scalar.copy(y_third[:], bank[:, 0, :])
-        nc.scalar.copy(y_late[:, CHUNK:], bank[:, 1, :])
-        third = weigh_page("third", ACT_AT, y_third[:], last * CHUNK, CHUNK)
-        fourth = weigh_page("fourth", ACT_AT + UNIT_BYTES, y_late[:], (last - 1) * CHUNK, 2 * CHUNK)
-        scatter_page(2, held_back[:], (last - 1) * CHUNK, CHUNK)
         scatter_page(2, third[:], last * CHUNK, CHUNK)
         scatter_page(3, fourth[:], (last - 1) * CHUNK, 2 * CHUNK)
         for i in range(NT):

@@ -32,7 +32,7 @@ UNIT_BYTES = NB * UNIT * PACK * 4
 ACT_AT = 0
 PROD_AT = 4 * UNIT_BYTES
 H_AT = PROD_AT + 2 * UNIT_BYTES
-W1_AT = H_AT + 6 * KB
+W1_AT = H_AT + 8 * KB
 TAB_AT = W1_AT + 24 * KB
 RT1_AT = TAB_AT + 16 * KB
 RT_AT = (None, RT1_AT, RT1_AT + 12 * KB, RT1_AT + 24 * KB)
@@ -103,10 +103,10 @@ def tile_list_email_expert_return_kernel(
         wgo_first = held([P, CHUNK], F32, "wgo_first")
         wgo_rest = held([P, S - CHUNK], F32, "wgo_rest")
         load_w1(0)
-        load_rt(0, 0)
         load_w1(1)
-        load_rt(0, 1)
+        load_rt(0, 0)
         load_w1(2)
+        load_rt(0, 1)
         load_rt(0, 2)
         load_rt(1, 0)
         load_rt(1, 1)
@@ -149,17 +149,13 @@ def tile_list_email_expert_return_kernel(
         w1s = [held([P, PASS], U8, "w1s%d" % b) for b in range(NB)]
 
         def quantize_w1(b):
-            grouped = work.tile([P, PACK, P, PACK], BF16, name="w1_grouped", align_bytes=64)
+            grouped = placed([P, PACK, P, PACK], BF16, "w1_grouped%d" % b, H_AT + (b % 2) * 4 * KB)
             dst = grouped[:].rearrange("p t m j -> p m t j")
             src = w1_raw[b][:].rearrange("p j (m t) -> p m t j", t=PACK)
-            if b == NB - 1:
-                nc.vector.tensor_copy(dst, src)
+            if b == 0:
+                nc.scalar.copy(dst, src)
             else:
-                nc.gpsimd.tensor_scalar(dst[:, : P // 2], src[:, : P // 2], 1.0, 0.0, op0=MULT, op1=ADD)
-                if b == 0:
-                    nc.scalar.copy(dst[:, P // 2 :], src[:, P // 2 :])
-                else:
-                    nc.vector.tensor_copy(dst[:, P // 2 :], src[:, P // 2 :])
+                nc.vector.tensor_copy(dst, src)
             nc.vector.quantize_mx(
                 out=w1c[b][:].bitcast(FP8X4), scales=w1s[b][:], in_=grouped[:].rearrange("p t m j -> p (t m j)")
             )
@@ -283,12 +279,13 @@ def tile_list_email_expert_return_kernel(
             order_w2(b)
         gather(v_words, tab, 0)
         gather(v_words, tab, 1)
-        new_h(0)
         for b in range(NB):
             quantize_w1(b)
+        new_h(0)
+        for b in range(NB):
             prepare(0, b)
-            for part in (slice(0, UNIT), slice(UNIT, CHUNK)) if b == NB - 1 else (slice(0, CHUNK),):
-                nc.gpsimd.tensor_tensor(h[0][:, b, part], acts[0][:, b, part], prods[0][:, b, part], MULT)
+            engine = nc.vector if b == NB - 1 else nc.gpsimd
+            engine.tensor_tensor(h[0][:, b], acts[0][:, b], prods[0][:, b], MULT)
         prepare(1, 0)
         prepare(1, 1)
 

@@ -1,6 +1,7 @@
 from contextlib import ExitStack
 
 import concourse.mybir as mybir
+from concourse.masks import make_identity
 
 K, T, S, H, N = 512, 4096, 1024, 1536, 512
 FLOPS = 2 * (2 * K * H * S + H * N * S)
@@ -64,6 +65,9 @@ def tile_list_email_expert_return_kernel(
         nc.vector.memset(tab_plane[:].bitcast(I32), 0)
         nc.vector.memset(w2_plane_raw[:].bitcast(I32), 0)
         nc.gpsimd.memset(w3_plane[:].rearrange("p a n -> p (a n)").bitcast(I32), 0)
+
+        identity = held([P, P], F32, "identity")
+        make_identity(nc, identity[:])
 
         tab = placed([P, T], U32, "tab", TAB_AT)
         tab_src = tab_words[0].rearrange("p t i -> p (t i)").bitcast(I32)
@@ -260,16 +264,37 @@ def tile_list_email_expert_return_kernel(
                 offsets = idx2[:, c * CHUNK // 16 : (c + 1) * CHUNK // 16]
                 nc.vector.tensor_copy(page[2 * pair + e][:].indirect(offsets), weighted[(c, pair)][:, e, :])
 
-        def finish(i):
-            last = i == NT - 1
-            width = CHUNK if last else HALF
-            pre = placed([P, S], F32, "pre%d" % i, TAB_AT + (1 if last else i) * 4 * KB)
-            if not last:
-                nc.gpsimd.tensor_tensor(pre[:], page[i][:], x0_sb[i][:], ADD)
-            for piece in range(S // width):
-                cols = slice(piece * width, (piece + 1) * width)
-                if last:
-                    nc.vector.tensor_tensor(pre[:, cols], page[i][:, cols], x0_sb[i][:, cols], ADD)
+        sums = {}
+
+        def add_turned(i, half, source, opens):
+            if opens:
+                sums[(i, half)] = (psum_a, psum_b)[half].tile([P, PACK, P], F32, name="bank")
+            for k in range(PACK):
+                cols = slice(half * HALF + k * P, half * HALF + (k + 1) * P)
+                nc.tensor.matmul(
+                    sums[(i, half)][:, k, :], source[:, cols], identity[:], is_transpose=True,
+                    start=(opens and k == 0), stop=(not opens and k == PACK - 1),
+                )
+
+        def finish_turned(i):
+            turned = placed([P, 2, PACK, P], F32, "turned%d" % i, TAB_AT + i * 4 * KB)
+            for half in range(2):
+                add_turned(i, half, page[i], False)
+                nc.scalar.activation(turned[:, half], sums[(i, half)][:], ACT.Tanh)
+            for half in range(2):
+                bank = psum_y.tile([P, PACK, P], F32, name="bank_y")
+                for k in range(PACK):
+                    nc.tensor.transpose(bank[:, k, :], turned[:, half, k, :], identity[:])
+                cols = slice(half * HALF, (half + 1) * HALF)
+                nc.scalar.copy(x0_sb[i][:, cols], bank[:].rearrange("p k m -> p (k m)"))
+                nc.sync.dma_start(out[i * P : (i + 1) * P, cols], x0_sb[i][:, cols])
+
+        def finish_last():
+            i = NT - 1
+            pre = placed([P, S], F32, "pre", TAB_AT + 4 * KB)
+            for piece in range(S // CHUNK):
+                cols = slice(piece * CHUNK, (piece + 1) * CHUNK)
+                nc.vector.tensor_tensor(pre[:, cols], page[i][:, cols], x0_sb[i][:, cols], ADD)
                 nc.scalar.activation(x0_sb[i][:, cols], pre[:, cols], ACT.Tanh)
                 nc.sync.dma_start(out[i * P : (i + 1) * P, cols], x0_sb[i][:, cols])
 
@@ -327,6 +352,9 @@ def tile_list_email_expert_return_kernel(
                 prepare(c + 2, 1)
 
         last = NC - 1
+        for i in range(NT - 1):
+            for half in range(2):
+                add_turned(i, half, x0_sb[i], True)
         quantize_h(last)
         weigh_first_pair(last, PROD_AT)
         third = third_page(last)
@@ -335,5 +363,6 @@ def tile_list_email_expert_return_kernel(
         scatter(last, 0)
         scatter_page(2, third[:], last * CHUNK, CHUNK)
         scatter_page(3, fourth[:], (last - 1) * CHUNK, 2 * CHUNK)
-        for i in range(NT):
-            finish(i)
+        for i in range(NT - 1):
+            finish_turned(i)
+        finish_last()

@@ -72,17 +72,13 @@ def tile_list_email_expert_return_kernel(
         tab = placed([P, T], U32, "tab", TAB_AT)
         tab_src = tab_words[0].rearrange("p t i -> p (t i)").bitcast(I32)
         nc.sync.dma_start(tab[:, : T // 4].bitcast(I32), tab_src[:, : T // 4])
-        for quad in range(4):
-            nc.sync.dma_start(
-                tab_plane[32 * quad : 32 * quad + 4, :].bitcast(I32), tab_scales[0, 4 * quad : 4 * quad + 4, :].bitcast(I32)
-            )
+        for r in range(4):
+            nc.sync.dma_start(tab_plane[r:P:32, :].bitcast(I32), tab_scales[0, r:16:4, :].bitcast(I32))
         nc.sync.dma_start(idx[:], offs)
         w2_raw = held([P, 2 * H], U8, "w2_raw")
         nc.sync.dma_start(w2_raw[:].bitcast(I32), w2_words[0].bitcast(I32))
-        for quad in range(4):
-            nc.sync.dma_start(
-                w2_plane_raw[32 * quad : 32 * quad + 4, :].bitcast(I32), w2_scales[0, 4 * quad : 4 * quad + 4, :].bitcast(I32)
-            )
+        for r in range(4):
+            nc.sync.dma_start(w2_plane_raw[r:P:32, :].bitcast(I32), w2_scales[0, r:16:4, :].bitcast(I32))
         nc.sync.dma_start(tab[:, T // 4 :].bitcast(I32), tab_src[:, T // 4 :])
 
         w1_raw, rt_sb = {}, {}
@@ -106,7 +102,11 @@ def tile_list_email_expert_return_kernel(
         w3_src = w3_words.rearrange("a p n i -> p a (n i)").bitcast(I32)
         wgo_first = held([P, CHUNK], F32, "wgo_first")
         wgo_rest = held([P, S - CHUNK], F32, "wgo_rest")
+        for r in range(4):
+            nc.sync.dma_start(w3_plane[r:P:32].bitcast(I32), w3_scales[:, r:16:4, :].rearrange("a q n -> q a n").bitcast(I32))
         load_w1(0)
+        nc.sync.dma_start(idx2[:], offs2)
+        nc.sync.dma_start(wgo_first[:], wgo[:, :CHUNK])
         load_w1(1)
         load_rt(0, 0)
         load_w1(2)
@@ -115,13 +115,6 @@ def tile_list_email_expert_return_kernel(
         load_rt(1, 0)
         load_rt(1, 1)
         nc.sync.dma_start(w3[0][:].bitcast(I32), w3_src[:, :, : 2 * P])
-        for quad in range(4):
-            nc.sync.dma_start(
-                w3_plane[32 * quad : 32 * quad + 4].bitcast(I32),
-                w3_scales[:, 4 * quad : 4 * quad + 4, :].rearrange("a r n -> r a n").bitcast(I32),
-            )
-        nc.sync.dma_start(wgo_first[:], wgo[:, :CHUNK])
-        nc.sync.dma_start(idx2[:], offs2)
         load_rt(1, 2)
         nc.sync.dma_start(w3[1][:].bitcast(I32), w3_src[:, :, 2 * P :])
         for b in range(NB):
@@ -136,17 +129,19 @@ def tile_list_email_expert_return_kernel(
         def gather(dst, window, h):
             nc.vector.tensor_copy(dst[h][:], window[:].indirect(idx[:, h * HALF // 16 : (h + 1) * HALF // 16]))
 
-        w2c = [held([P, 2 * PASS], U8, "w2c%d" % b) for b in range(NB)]
-        w2s = [held([P, PASS], U8, "w2s%d" % b) for b in range(NB)]
+        w2_codes = held([P, NB, 2 * PASS], U8, "w2_codes")
+        w2_plane = held([P, NB, PASS], U8, "w2_plane")
+        w2c = [w2_codes[:, b] for b in range(NB)]
+        w2s = [w2_plane[:, b] for b in range(NB)]
 
-        def order_w2(b):
+        def order_w2():
             nc.vector.tensor_copy(
-                w2c[b][:].bitcast(U16).rearrange("p (t m) -> p t m", t=PACK),
-                w2_raw[:, 2 * b * PASS : 2 * (b + 1) * PASS].bitcast(U16).rearrange("p (m t) -> p t m", t=PACK),
+                w2_codes[:].bitcast(U16).rearrange("p b (t m) -> p t b m", t=PACK),
+                w2_raw[:].bitcast(U16).rearrange("p (b m t) -> p t b m", b=NB, t=PACK),
             )
             nc.vector.tensor_copy(
-                w2s[b][:].rearrange("p (t m) -> p t m", t=PACK),
-                w2_plane_raw[:, b * PASS : (b + 1) * PASS].rearrange("p (m t) -> p t m", t=PACK),
+                w2_plane[:].rearrange("p b (t m) -> p t b m", t=PACK),
+                w2_plane_raw[:].rearrange("p (b m t) -> p t b m", b=NB, t=PACK),
             )
 
         w1c = [held([P, PASS], U32, "w1c%d" % b) for b in range(NB)]
@@ -156,7 +151,7 @@ def tile_list_email_expert_return_kernel(
             grouped = placed([P, PACK, P, PACK], BF16, "w1_grouped%d" % b, H_AT + (b % 2) * 4 * KB)
             dst = grouped[:].rearrange("p t m j -> p m t j")
             src = w1_raw[b][:].rearrange("p j (m t) -> p m t j", t=PACK)
-            if b == 0:
+            if b < NB - 1:
                 nc.scalar.copy(dst, src)
             else:
                 nc.vector.tensor_copy(dst, src)
@@ -289,19 +284,26 @@ def tile_list_email_expert_return_kernel(
                 nc.scalar.copy(x0_sb[i][:, cols], bank[:].rearrange("p k m -> p (k m)"))
                 nc.sync.dma_start(out[i * P : (i + 1) * P, cols], x0_sb[i][:, cols])
 
+        def finish_summed(i):
+            for half in range(2):
+                cols = slice(half * HALF, (half + 1) * HALF)
+                pre = placed([P, HALF], F32, "pre%d_%d" % (i, half), TAB_AT + i * 4 * KB + half * 2 * KB)
+                nc.gpsimd.tensor_tensor(pre[:], page[i][:, cols], x0_sb[i][:, cols], ADD)
+                nc.scalar.activation(x0_sb[i][:, cols], pre[:], ACT.Tanh)
+                nc.sync.dma_start(out[i * P : (i + 1) * P, cols], x0_sb[i][:, cols])
+
         def finish_last():
             i = NT - 1
-            pre = placed([P, S], F32, "pre", TAB_AT + 4 * KB)
+            pre = placed([P, S], F32, "pre", TAB_AT + 6 * KB)
             for piece in range(S // CHUNK):
                 cols = slice(piece * CHUNK, (piece + 1) * CHUNK)
                 nc.vector.tensor_tensor(pre[:, cols], page[i][:, cols], x0_sb[i][:, cols], ADD)
                 nc.scalar.activation(x0_sb[i][:, cols], pre[:, cols], ACT.Tanh)
-                nc.sync.dma_start(out[i * P : (i + 1) * P, cols], x0_sb[i][:, cols])
+                nc.scalar.dma_start(out[i * P : (i + 1) * P, cols], x0_sb[i][:, cols])
 
         gather(v_plane, tab_plane, 0)
         gather(v_plane, tab_plane, 1)
-        for b in range(NB):
-            order_w2(b)
+        order_w2()
         gather(v_words, tab, 0)
         gather(v_words, tab, 1)
         for b in range(NB):
@@ -352,9 +354,8 @@ def tile_list_email_expert_return_kernel(
                 prepare(c + 2, 1)
 
         last = NC - 1
-        for i in range(NT - 1):
-            for half in range(2):
-                add_turned(i, half, x0_sb[i], True)
+        for half in range(2):
+            add_turned(1, half, x0_sb[1], True)
         quantize_h(last)
         weigh_first_pair(last, PROD_AT)
         third = third_page(last)
@@ -363,6 +364,7 @@ def tile_list_email_expert_return_kernel(
         scatter(last, 0)
         scatter_page(2, third[:], last * CHUNK, CHUNK)
         scatter_page(3, fourth[:], (last - 1) * CHUNK, 2 * CHUNK)
-        for i in range(NT - 1):
-            finish_turned(i)
+        finish_summed(0)
+        finish_turned(1)
+        finish_summed(2)
         finish_last()

@@ -75,11 +75,9 @@ def tile_list_email_expert_return_kernel(
         for r in range(4):
             nc.sync.dma_start(tab_plane[r:P:32, :].bitcast(I32), tab_scales[0, r:16:4, :].bitcast(I32))
         nc.sync.dma_start(idx[:], offs)
+        nc.sync.dma_start(tab[:, T // 4 :].bitcast(I32), tab_src[:, T // 4 :])
         w2_raw = held([P, 2 * H], U8, "w2_raw")
         nc.sync.dma_start(w2_raw[:].bitcast(I32), w2_words[0].bitcast(I32))
-        for r in range(4):
-            nc.sync.dma_start(w2_plane_raw[r:P:32, :].bitcast(I32), w2_scales[0, r:16:4, :].bitcast(I32))
-        nc.sync.dma_start(tab[:, T // 4 :].bitcast(I32), tab_src[:, T // 4 :])
 
         w1_raw, rt_sb = {}, {}
 
@@ -102,17 +100,24 @@ def tile_list_email_expert_return_kernel(
         w3_src = w3_words.rearrange("a p n i -> p a (n i)").bitcast(I32)
         wgo_first = held([P, CHUNK], F32, "wgo_first")
         wgo_rest = held([P, S - CHUNK], F32, "wgo_rest")
-        for r in range(4):
-            nc.sync.dma_start(w3_plane[r:P:32].bitcast(I32), w3_scales[:, r:16:4, :].rearrange("a q n -> q a n").bitcast(I32))
+
+        def load_w3_rows(rows):
+            for r in rows:
+                nc.sync.dma_start(w3_plane[r:P:32].bitcast(I32), w3_scales[:, r:16:4, :].rearrange("a q n -> q a n").bitcast(I32))
+
         load_w1(0)
-        nc.sync.dma_start(idx2[:], offs2)
-        nc.sync.dma_start(wgo_first[:], wgo[:, :CHUNK])
+        for r in range(4):
+            nc.sync.dma_start(w2_plane_raw[r:P:32, :].bitcast(I32), w2_scales[0, r:16:4, :].bitcast(I32))
         load_w1(1)
         load_rt(0, 0)
         load_w1(2)
+        load_w3_rows((0, 1))
         load_rt(0, 1)
+        load_w3_rows((2, 3))
         load_rt(0, 2)
+        nc.sync.dma_start(idx2[:], offs2)
         load_rt(1, 0)
+        nc.sync.dma_start(wgo_first[:], wgo[:, :CHUNK])
         load_rt(1, 1)
         nc.sync.dma_start(w3[0][:].bitcast(I32), w3_src[:, :, : 2 * P])
         load_rt(1, 2)
@@ -215,19 +220,17 @@ def tile_list_email_expert_return_kernel(
                     out=hc[c][:, first:last].bitcast(FP8X4), scales=hs[c][:, first:last], in_=flat[:, PACK * first : PACK * last]
                 )
 
-        def down(c, pair):
-            if c == 0 and pair == 1:
-                bank = psum_a.tile([P, 2, CHUNK], F32, name="bank")
-            else:
-                bank = psum_y.tile([P, 2, CHUNK], F32, name="bank_y")
+        def down(c, first, count, pool):
+            bank = pool.tile([P, count, CHUNK], F32, name="bank_y" if pool is psum_y else "bank")
             for b in RT_ORDER:
-                for e in range(2):
-                    i = 2 * pair + e
+                for e in range(count):
+                    i = first + e
                     cols = slice(b * CHUNK, (b + 1) * CHUNK)
                     nc.tensor.matmul_mx(
-                        out=bank[:, e, :], lhsT=w3[pair][:, b, e * P : (e + 1) * P].bitcast(FP8X4),
+                        out=bank[:, e, :], lhsT=w3[i // 2][:, b, (i % 2) * P : (i % 2 + 1) * P].bitcast(FP8X4),
                         lhsT_scale=w3_plane[:, b, i * P : (i + 1) * P],
-                        rhs=hc[c][:, cols].bitcast(FP8X4), rhs_scale=hs[c][:, cols], start=(b == 2 and e == 0), stop=(b == 1 and e == 1),
+                        rhs=hc[c][:, cols].bitcast(FP8X4), rhs_scale=hs[c][:, cols],
+                        start=(b == 2 and e == 0), stop=(b == 1 and e == count - 1),
                     )
             return bank
 
@@ -238,7 +241,7 @@ def tile_list_email_expert_return_kernel(
         y_sb = {}
 
         def down_to_sbuf(c, pair):
-            bank = down(c, pair)
+            bank = down(c, 2, 2, psum_a)
             y_sb[(c, pair)] = work.tile([P, 2, CHUNK], F32, name="y%d" % pair)
             nc.scalar.copy(y_sb[(c, pair)][:], bank[:])
 
@@ -246,9 +249,10 @@ def tile_list_email_expert_return_kernel(
         weighted = {}
 
         def weigh_first_pair(c, offset):
-            bank = down(c, 0)
+            banks = [down(c, i, 1, psum_y) for i in range(2)]
             weighted[(c, 0)] = placed([P, 2, CHUNK], F32, "weighted_%d_0" % c, offset)
-            nc.vector.tensor_tensor(weighted[(c, 0)][:], bank[:], factor_of(c), MULT)
+            for i in range(2):
+                nc.vector.tensor_tensor(weighted[(c, 0)][:, i : i + 1], banks[i][:], factor_of(c)[:, :1], MULT)
 
         def weigh_second_pair(c):
             weighted[(c, 1)] = placed([P, 2, CHUNK], F32, "weighted_%d_1" % c, RT_AT[c + 2] + 10 * KB)
@@ -319,7 +323,7 @@ def tile_list_email_expert_return_kernel(
         y_late = held([P, 2 * CHUNK], F32, "y_late")
 
         def third_page(c):
-            bank = down(c, 1)
+            bank = down(c, 2, 2, psum_a)
             tile = work.tile([P, CHUNK], F32, name="third")
             nc.scalar.copy(y_late[:, (c - NC + 2) * CHUNK : (c - NC + 3) * CHUNK], bank[:, 1, :])
             nc.vector.tensor_tensor(tile[:], bank[:, 0, :], wgo_rest[:, (c - 1) * CHUNK : c * CHUNK], MULT)
@@ -357,12 +361,14 @@ def tile_list_email_expert_return_kernel(
         for half in range(2):
             add_turned(1, half, x0_sb[1], True)
         quantize_h(last)
-        weigh_first_pair(last, PROD_AT)
-        third = third_page(last)
+        banks = [down(last, i, 1, (psum_y, psum_y, psum_a, psum_b)[i])[:, 0] for i in range(NT)]
+        nc.scalar.copy(y_late[:, CHUNK:], banks[3])
         fourth = placed([P, 2 * CHUNK], F32, "fourth", H_AT)
         nc.gpsimd.tensor_tensor(fourth[:], y_late[:], wgo_rest[:, CHUNK:], MULT)
-        scatter(last, 0)
-        scatter_page(2, third[:], last * CHUNK, CHUNK)
+        for i in range(NT - 1):
+            values = placed([P, CHUNK], F32, "weighted_last%d" % i, PROD_AT + i * KB)
+            nc.vector.tensor_tensor(values[:], banks[i], wgo_rest[:, (last - 1) * CHUNK :], MULT)
+            scatter_page(i, values[:], last * CHUNK, CHUNK)
         scatter_page(3, fourth[:], (last - 1) * CHUNK, 2 * CHUNK)
         finish_summed(0)
         finish_turned(1)

@@ -75,9 +75,11 @@ def tile_list_email_expert_return_kernel(
         for r in range(4):
             nc.sync.dma_start(tab_plane[r:P:32, :].bitcast(I32), tab_scales[0, r:16:4, :].bitcast(I32))
         nc.sync.dma_start(idx[:], offs)
-        nc.sync.dma_start(tab[:, T // 4 :].bitcast(I32), tab_src[:, T // 4 :])
         w2_raw = held([P, 2 * H], U8, "w2_raw")
         nc.sync.dma_start(w2_raw[:].bitcast(I32), w2_words[0].bitcast(I32))
+        for r in range(4):
+            nc.sync.dma_start(w2_plane_raw[r:P:32, :].bitcast(I32), w2_scales[0, r:16:4, :].bitcast(I32))
+        nc.sync.dma_start(tab[:, T // 4 :].bitcast(I32), tab_src[:, T // 4 :])
 
         w1_raw, rt_sb = {}, {}
 
@@ -100,24 +102,17 @@ def tile_list_email_expert_return_kernel(
         w3_src = w3_words.rearrange("a p n i -> p a (n i)").bitcast(I32)
         wgo_first = held([P, CHUNK], F32, "wgo_first")
         wgo_rest = held([P, S - CHUNK], F32, "wgo_rest")
-
-        def load_w3_rows(rows):
-            for r in rows:
-                nc.sync.dma_start(w3_plane[r:P:32].bitcast(I32), w3_scales[:, r:16:4, :].rearrange("a q n -> q a n").bitcast(I32))
-
-        load_w1(0)
         for r in range(4):
-            nc.sync.dma_start(w2_plane_raw[r:P:32, :].bitcast(I32), w2_scales[0, r:16:4, :].bitcast(I32))
+            nc.sync.dma_start(w3_plane[r:P:32].bitcast(I32), w3_scales[:, r:16:4, :].rearrange("a q n -> q a n").bitcast(I32))
+        load_w1(0)
+        nc.sync.dma_start(idx2[:], offs2)
+        nc.sync.dma_start(wgo_first[:], wgo[:, :CHUNK])
         load_w1(1)
         load_rt(0, 0)
         load_w1(2)
-        load_w3_rows((0, 1))
         load_rt(0, 1)
-        load_w3_rows((2, 3))
         load_rt(0, 2)
-        nc.sync.dma_start(idx2[:], offs2)
         load_rt(1, 0)
-        nc.sync.dma_start(wgo_first[:], wgo[:, :CHUNK])
         load_rt(1, 1)
         nc.sync.dma_start(w3[0][:].bitcast(I32), w3_src[:, :, : 2 * P])
         load_rt(1, 2)

@@ -185,7 +185,7 @@ def tile_list_email_expert_return_kernel(
         h, hc, hs = {}, {}, {}
 
         def new_h(c):
-            h[c] = placed([P, NB, CHUNK, PACK], BF16, "h%d" % c, H_AT)
+            h[c] = placed([P, NB, CHUNK, PACK], BF16, "h%d" % c, H_AT + max(c - 1, 0) * 2 * KB)
 
         acts, prods = {}, {}
 
@@ -246,11 +246,16 @@ def tile_list_email_expert_return_kernel(
         def weigh_first_pair(c, offset):
             banks = [down(c, i, 1, psum_y) for i in range(2)]
             weighted[(c, 0)] = placed([P, 2, CHUNK], F32, "weighted_%d_0" % c, offset)
-            for i in range(2):
-                nc.vector.tensor_tensor(weighted[(c, 0)][:, i : i + 1], banks[i][:], factor_of(c)[:, :1], MULT)
+            nc.vector.tensor_tensor(weighted[(c, 0)][:, :1], banks[0][:], factor_of(c)[:, :1], MULT)
+            if c == 1:
+                y_second = work.tile([P, 1, CHUNK], F32, name="y_second")
+                nc.scalar.copy(y_second[:], banks[1][:])
+                nc.gpsimd.tensor_tensor(weighted[(c, 0)][:, 1:], y_second[:], factor_of(c)[:, :1], MULT)
+            else:
+                nc.vector.tensor_tensor(weighted[(c, 0)][:, 1:], banks[1][:], factor_of(c)[:, :1], MULT)
 
         def weigh_second_pair(c):
-            weighted[(c, 1)] = placed([P, 2, CHUNK], F32, "weighted_%d_1" % c, RT_AT[c + 2] + 10 * KB)
+            weighted[(c, 1)] = placed([P, 2, CHUNK], F32, "weighted_%d_1" % c, H_AT + c * 2 * KB)
             nc.gpsimd.tensor_tensor(weighted[(c, 1)][:], y_sb[(c, 1)][:], factor_of(c), MULT)
 
         def scatter(c, pair):
@@ -330,10 +335,10 @@ def tile_list_email_expert_return_kernel(
         for c in range(NC - 1):
             quantize_h(c)
             prepare(c + 1, 2)
-            combine(c + 1, 0)
-            weigh_first_pair(c, RT_AT[c + 1] + (NB - 1) * 4 * KB)
             if c > 0:
                 weigh_second_pair(c - 1)
+            combine(c + 1, 0)
+            weigh_first_pair(c, RT_AT[c + 1] + (NB - 1) * 4 * KB)
             if c < NC - 2:
                 down_to_sbuf(c, 1)
             else:
@@ -358,7 +363,7 @@ def tile_list_email_expert_return_kernel(
         quantize_h(last)
         banks = [down(last, i, 1, (psum_y, psum_y, psum_a, psum_b)[i])[:, 0] for i in range(NT)]
         nc.scalar.copy(y_late[:, CHUNK:], banks[3])
-        fourth = placed([P, 2 * CHUNK], F32, "fourth", H_AT)
+        fourth = placed([P, 2 * CHUNK], F32, "fourth", H_AT + 4 * KB)
         nc.gpsimd.tensor_tensor(fourth[:], y_late[:], wgo_rest[:, CHUNK:], MULT)
         for i in range(NT - 1):
             values = placed([P, CHUNK], F32, "weighted_last%d" % i, PROD_AT + i * KB)

@@ -28,15 +28,19 @@ NC = S // CHUNK
 HALF = 512
 NT = N // P
 KB = 1024
-RT_ORDER = (2, 0, 1)
-UNIT_BYTES = NB * UNIT * PACK * 4
-ACT_AT = 0
-PROD_AT = 4 * UNIT_BYTES
-H_AT = PROD_AT + 2 * UNIT_BYTES
-W1_AT = H_AT + 8 * KB
+CAST_VECTOR = 84
+
+W1_AT = 0
+ACT0_AT = W1_AT + 16 * KB
 TAB_AT = W1_AT + 24 * KB
-RT1_AT = TAB_AT + 16 * KB
-RT_AT = (None, RT1_AT, RT1_AT + 12 * KB, RT1_AT + 24 * KB)
+GROUPED_AT = TAB_AT + 16 * KB
+H0_AT = GROUPED_AT + 8 * KB
+H12_AT = H0_AT + 4 * KB
+ACT12_AT = H12_AT + 4 * KB
+PROD0_AT = ACT12_AT + 16 * KB
+PROD12_AT = PROD0_AT + 8 * KB
+RT12_AT = PROD12_AT + 16 * KB
+ACT0_PLACES = (ACT0_AT, RT12_AT + 4 * KB)
 
 
 def tile_list_email_expert_return_kernel(
@@ -47,15 +51,16 @@ def tile_list_email_expert_return_kernel(
         keep = ctx.enter_context(tc.tile_pool(name="keep", bufs=1))
         work = ctx.enter_context(tc.tile_pool(name="work", bufs=2))
         arena = ctx.enter_context(tc.tile_pool(name="arena", bufs=1))
-        psum_a = ctx.enter_context(tc.psum_pool(name="psum_a", bufs=3))
-        psum_b = ctx.enter_context(tc.psum_pool(name="psum_b", bufs=3))
-        psum_y = ctx.enter_context(tc.psum_pool(name="psum_y", bufs=2))
+        psum = ctx.enter_context(tc.psum_pool(name="psum", bufs=1))
 
         def held(shape, dtype, name):
             return keep.tile(shape, dtype, name=name, align_bytes=64)
 
         def placed(shape, dtype, name, offset):
             return arena.tile(shape, dtype, name=name, offset=offset, align_bytes=64)
+
+        def in_bank(shape, name, bank):
+            return psum.tile(shape, F32, name=name, offset=bank * 2 * KB)
 
         idx = keep.tile([P, S // 16], U16, name="idx")
         idx2 = keep.tile([P, S // 16], U16, name="idx2")
@@ -69,17 +74,8 @@ def tile_list_email_expert_return_kernel(
         identity = held([P, P], F32, "identity")
         make_identity(nc, identity[:])
 
-        tab = placed([P, T], U32, "tab", TAB_AT)
-        tab_src = tab_words[0].rearrange("p t i -> p (t i)").bitcast(I32)
-        nc.sync.dma_start(tab[:, : T // 4].bitcast(I32), tab_src[:, : T // 4])
-        for r in range(4):
-            nc.sync.dma_start(tab_plane[r:P:32, :].bitcast(I32), tab_scales[0, r:16:4, :].bitcast(I32))
-        nc.sync.dma_start(idx[:], offs)
-        w2_raw = held([P, 2 * H], U8, "w2_raw")
-        nc.sync.dma_start(w2_raw[:].bitcast(I32), w2_words[0].bitcast(I32))
-        for r in range(4):
-            nc.sync.dma_start(w2_plane_raw[r:P:32, :].bitcast(I32), w2_scales[0, r:16:4, :].bitcast(I32))
-        nc.sync.dma_start(tab[:, T // 4 :].bitcast(I32), tab_src[:, T // 4 :])
+        warm = held([P, 1], F32, "warm")
+        nc.scalar.activation(warm[:], identity[:, :1], ACT.Silu)
 
         w1_raw, rt_sb = {}, {}
 
@@ -90,38 +86,47 @@ def tile_list_email_expert_return_kernel(
 
         def load_rt(c, b):
             name = "rt_%d_%d" % (c, b)
-            if c == 0:
-                tile = held([P, PACK, CHUNK], F32, name)
+            if (c, b) == (1, 2):
+                tile = placed([P, PACK, CHUNK], F32, name, RT12_AT)
             else:
-                tile = placed([P, PACK, CHUNK], F32, name, RT_AT[c] + b * 4 * KB)
+                tile = held([P, PACK, CHUNK], F32, name)
             rows = rt[b * PASS : (b + 1) * PASS, c * CHUNK : (c + 1) * CHUNK]
             nc.sync.dma_start(tile[:], rows.rearrange("(p t) n -> p t n", t=PACK))
             rt_sb[(c, b)] = tile
 
-        w3 = [held([P, NB, 2 * P], U32, "w3_%d" % pair) for pair in range(NT // 2)]
-        w3_src = w3_words.rearrange("a p n i -> p a (n i)").bitcast(I32)
-        wgo_first = held([P, CHUNK], F32, "wgo_first")
-        wgo_rest = held([P, S - CHUNK], F32, "wgo_rest")
+        tab = placed([P, T], U32, "tab", TAB_AT)
+        w2_raw = held([P, 2 * H], U8, "w2_raw")
+        w3 = held([P, NB, N], U32, "w3")
+        wgo_sb = [held([P, width], F32, "wgo%d" % c) for c, width in enumerate((CHUNK, CHUNK, 2 * CHUNK))]
+
+        load_w1(0)
+        for r in range(4):
+            nc.sync.dma_start(tab_plane[r:P:32, :].bitcast(I32), tab_scales[0, r:16:4, :].bitcast(I32))
+        nc.sync.dma_start(idx[:], offs)
+        nc.sync.dma_start(w2_raw[:].bitcast(I32), w2_words[0].bitcast(I32))
+        load_w1(1)
+        for r in range(4):
+            nc.sync.dma_start(w2_plane_raw[r:P:32, :].bitcast(I32), w2_scales[0, r:16:4, :].bitcast(I32))
+        nc.sync.dma_start(tab[:].bitcast(I32), tab_words[0].rearrange("p t i -> p (t i)").bitcast(I32))
+        load_w1(2)
         for r in range(4):
             nc.sync.dma_start(w3_plane[r:P:32].bitcast(I32), w3_scales[:, r:16:4, :].rearrange("a q n -> q a n").bitcast(I32))
-        load_w1(0)
         nc.sync.dma_start(idx2[:], offs2)
-        nc.sync.dma_start(wgo_first[:], wgo[:, :CHUNK])
-        load_w1(1)
-        load_rt(0, 0)
-        load_w1(2)
-        load_rt(0, 1)
-        load_rt(0, 2)
+        for b in range(NB):
+            load_rt(0, b)
         load_rt(1, 0)
         load_rt(1, 1)
-        nc.sync.dma_start(w3[0][:].bitcast(I32), w3_src[:, :, : 2 * P])
+        nc.sync.dma_start(w3[:].bitcast(I32), w3_words.rearrange("a p n i -> p a (n i)").bitcast(I32))
         load_rt(1, 2)
-        nc.sync.dma_start(w3[1][:].bitcast(I32), w3_src[:, :, 2 * P :])
-        for b in range(NB):
-            load_rt(2, b)
-        nc.sync.dma_start(wgo_rest[:], wgo[:, CHUNK:])
-        for b in range(NB):
-            load_rt(3, b)
+        load_rt(2, 0)
+        nc.sync.dma_start(wgo_sb[0][:], wgo[:, :CHUNK])
+        load_rt(2, 1)
+        load_rt(2, 2)
+        load_rt(3, 0)
+        nc.sync.dma_start(wgo_sb[1][:], wgo[:, CHUNK : 2 * CHUNK])
+        load_rt(3, 1)
+        load_rt(3, 2)
+        nc.sync.dma_start(wgo_sb[2][:], wgo[:, 2 * CHUNK :])
 
         v_words = [held([P, HALF], U32, "v_words%d" % h) for h in range(2)]
         v_plane = [held([P, HALF], U8, "v_plane%d" % h) for h in range(2)]
@@ -131,8 +136,6 @@ def tile_list_email_expert_return_kernel(
 
         w2_codes = held([P, NB, 2 * PASS], U8, "w2_codes")
         w2_plane = held([P, NB, PASS], U8, "w2_plane")
-        w2c = [w2_codes[:, b] for b in range(NB)]
-        w2s = [w2_plane[:, b] for b in range(NB)]
 
         def order_w2():
             nc.vector.tensor_copy(
@@ -148,21 +151,22 @@ def tile_list_email_expert_return_kernel(
         w1s = [held([P, PASS], U8, "w1s%d" % b) for b in range(NB)]
 
         def quantize_w1(b):
-            grouped = placed([P, PACK, P, PACK], BF16, "w1_grouped%d" % b, H_AT + (b % 2) * 4 * KB)
+            grouped = placed([P, PACK, P, PACK], BF16, "w1_grouped%d" % b, GROUPED_AT + b * 4 * KB)
             dst = grouped[:].rearrange("p t m j -> p m t j")
             src = w1_raw[b][:].rearrange("p j (m t) -> p m t j", t=PACK)
             if b < NB - 1:
                 nc.scalar.copy(dst, src)
             else:
-                nc.vector.tensor_copy(dst, src)
+                nc.vector.tensor_copy(dst[:, :CAST_VECTOR], src[:, :CAST_VECTOR])
+                nc.scalar.copy(dst[:, CAST_VECTOR:], src[:, CAST_VECTOR:])
             nc.vector.quantize_mx(
                 out=w1c[b][:].bitcast(FP8X4), scales=w1s[b][:], in_=grouped[:].rearrange("p t m j -> p (t m j)")
             )
 
-        def four_slots(pool, codes, plane, dtype, width, j):
+        def four_slots(name, at, codes, plane, dtype, width, j):
             cols = slice((j * UNIT) % HALF, (j * UNIT) % HALF + UNIT)
             rhs, rhs_scale = v_words[j * UNIT // HALF][:, cols].bitcast(FP8X4), v_plane[j * UNIT // HALF][:, cols]
-            bank = pool.tile([P, PACK, UNIT], F32, name="bank")
+            bank = in_bank([P, PACK, UNIT], name, at)
             for t in range(PACK):
                 nc.tensor.matmul_mx(
                     out=bank[:, t, :], lhsT=codes[:, width * t * P : width * (t + 1) * P].bitcast(dtype),
@@ -170,118 +174,222 @@ def tile_list_email_expert_return_kernel(
                 )
             return bank
 
-        def routed(j, b, dst):
-            bank = four_slots(psum_b, w2c[b], w2s[b], FP4X4, 2, j)
-            factor = rt_sb[(j // 2, b)][:, :, (j % 2) * UNIT : (j % 2 + 1) * UNIT]
-            nc.vector.tensor_tensor(
-                dst.rearrange("p (c i) t -> p c t i", i=2), bank[:].rearrange("p t (c i) -> p c t i", i=2),
-                factor.rearrange("p t (c i) -> p c t i", i=2), MULT,
-            )
-
-        def gate(j, b, dst):
-            bank = four_slots(psum_a, w1c[b], w1s[b], FP8X4, 1, j)
-            nc.scalar.activation(dst, bank[:].rearrange("p t n -> p n t"), ACT.Silu)
-
-        h, hc, hs = {}, {}, {}
-
-        def new_h(c):
-            h[c] = placed([P, NB, CHUNK, PACK], BF16, "h%d" % c, H_AT + max(c - 1, 0) * 2 * KB)
-
         acts, prods = {}, {}
 
-        def prepare(c, b):
+        def new_part(store, name, c, b, first_at, rest_at):
             if b == 0:
-                acts[c] = placed([P, NB, CHUNK, PACK], F32, "act%d" % c, (ACT_AT if c < 2 else W1_AT) + (c % 2) * 2 * UNIT_BYTES)
-                prods[c] = placed([P, NB, CHUNK, PACK], F32, "prod%d" % c, PROD_AT if c % 2 else TAB_AT)
+                store[(c, 0)] = placed([P, 1, CHUNK, PACK], F32, "%s_%d_0" % (name, c), first_at)[:]
+            elif c == 0:
+                store[(c, b)] = placed([P, 1, CHUNK, PACK], F32, "%s_%d_%d" % (name, c, b), rest_at + (b - 1) * 4 * KB)[:]
+            elif b == 1:
+                both = placed([P, 2, CHUNK, PACK], F32, "%s_%d_12" % (name, c), rest_at)
+                store[(c, 12)] = both[:]
+                store[(c, 1)] = both[:, :1]
+                store[(c, 2)] = both[:, 1:]
+            return store[(c, b)]
+
+        def routed(c, b, banks):
+            part = new_part(prods, "prod", c, b, PROD0_AT + (c % 2) * 4 * KB, PROD12_AT + min(c, 1) * 8 * KB)
             for u in range(2):
-                routed(2 * c + u, b, prods[c][:, b, u * UNIT : (u + 1) * UNIT, :])
-                gate(2 * c + u, b, acts[c][:, b, u * UNIT : (u + 1) * UNIT, :])
-
-        def combine(c, u):
-            if u == 0:
-                new_h(c)
-            parts = [t[c][:, :, u * UNIT : (u + 1) * UNIT, :].rearrange("p b n t -> p b (n t)") for t in (h, acts, prods)]
-            nc.gpsimd.tensor_tensor(parts[0], parts[1], parts[2], MULT)
-
-        def quantize_h(c):
-            if c + 1 < NC:
-                hc[c] = placed([P, NB * CHUNK], U32, "hc%d" % c, RT_AT[c + 1] + 4 * KB)
-            else:
-                hc[c] = held([P, NB * CHUNK], U32, "hc%d" % c)
-            hs[c] = work.tile([P, NB * CHUNK], U8, name="hs", align_bytes=64)
-            flat = h[c][:].rearrange("p b n t -> p (b n t)")
-            for first, last in ((2 * CHUNK, 3 * CHUNK), (0, 2 * CHUNK)):
-                nc.vector.quantize_mx(
-                    out=hc[c][:, first:last].bitcast(FP8X4), scales=hs[c][:, first:last], in_=flat[:, PACK * first : PACK * last]
+                bank = four_slots("b_%d_%d_%d" % (c, b, u), banks[u], w2_codes[:, b], w2_plane[:, b], FP4X4, 2, 2 * c + u)
+                cols = slice(u * UNIT, (u + 1) * UNIT)
+                nc.vector.tensor_tensor(
+                    part[:, 0, cols, :].rearrange("p (c i) t -> p c t i", i=2),
+                    bank[:].rearrange("p t (c i) -> p c t i", i=2),
+                    rt_sb[(c, b)][:, :, cols].rearrange("p t (c i) -> p c t i", i=2), MULT,
                 )
 
-        def down(c, first, count, pool):
-            bank = pool.tile([P, count, CHUNK], F32, name="bank_y" if pool is psum_y else "bank")
-            for b in RT_ORDER:
+        def gate(c, b, banks):
+            rest_at = ACT0_AT + 4 * KB if (c, b) == (0, 1) else ACT12_AT + (c % 2) * 8 * KB
+            part = new_part(acts, "act", c, b, ACT0_PLACES[c % 2], rest_at)
+            for u in range(2):
+                bank = four_slots("a_%d_%d_%d" % (c, b, u), banks[u], w1c[b], w1s[b], FP8X4, 1, 2 * c + u)
+                nc.scalar.activation(part[:, 0, u * UNIT : (u + 1) * UNIT, :], bank[:].rearrange("p t n -> p n t"), ACT.Silu)
+
+        h0, h12 = {}, {}
+
+        def flat(ap):
+            return ap.rearrange("p b n t -> p (b n t)")
+
+        def combine_first(c):
+            h0[c] = placed([P, 1, CHUNK, PACK], BF16, "h0_%d" % c, H0_AT)
+            nc.gpsimd.tensor_tensor(flat(h0[c][:]), flat(acts[(c, 0)]), flat(prods[(c, 0)]), MULT)
+
+        def combine_rest(c):
+            h12[c] = placed([P, 2, CHUNK, PACK], BF16, "h12_%d" % c, H12_AT)
+            if c == 0:
+                for b in (1, 2):
+                    nc.gpsimd.tensor_tensor(flat(h12[c][:, b - 1 : b]), flat(acts[(c, b)]), flat(prods[(c, b)]), MULT)
+            else:
+                nc.gpsimd.tensor_tensor(flat(h12[c][:]), flat(acts[(c, 12)]), flat(prods[(c, 12)]), MULT)
+
+        codes, planes = {}, {}
+
+        def quantize_rest(c):
+            if c == 0:
+                tile = placed([P, 2 * CHUNK], U32, "hc12_0", RT12_AT)
+            else:
+                tile = work.tile([P, 2 * CHUNK], U32, name="hc12", align_bytes=64)
+            plane = work.tile([P, 2 * CHUNK], U8, name="hs12", align_bytes=64)
+            nc.vector.quantize_mx(out=tile[:].bitcast(FP8X4), scales=plane[:], in_=flat(h12[c][:]))
+            for b in (1, 2):
+                codes[(c, b)] = tile[:, (b - 1) * CHUNK : b * CHUNK]
+                planes[(c, b)] = plane[:, (b - 1) * CHUNK : b * CHUNK]
+
+        def quantize_first(c):
+            tile = placed([P, CHUNK], U32, "hc0_%d" % c, RT12_AT + 2 * KB if c == 0 else ACT12_AT + (c % 2) * 8 * KB)
+            plane = work.tile([P, CHUNK], U8, name="hs0", align_bytes=64)
+            nc.vector.quantize_mx(out=tile[:].bitcast(FP8X4), scales=plane[:], in_=flat(h0[c][:]))
+            codes[(c, 0)], planes[(c, 0)] = tile[:], plane[:]
+
+        def down(c, first, count, at):
+            bank = in_bank([P, count, CHUNK], "y_bank_%d_%d" % (c, first), at)
+            for b in (1, 2, 0):
                 for e in range(count):
-                    i = first + e
-                    cols = slice(b * CHUNK, (b + 1) * CHUNK)
+                    cols = slice((first + e) * P, (first + e + 1) * P)
                     nc.tensor.matmul_mx(
-                        out=bank[:, e, :], lhsT=w3[i // 2][:, b, (i % 2) * P : (i % 2 + 1) * P].bitcast(FP8X4),
-                        lhsT_scale=w3_plane[:, b, i * P : (i + 1) * P],
-                        rhs=hc[c][:, cols].bitcast(FP8X4), rhs_scale=hs[c][:, cols],
-                        start=(b == 2 and e == 0), stop=(b == 1 and e == count - 1),
+                        out=bank[:, e, :], lhsT=w3[:, b, cols].bitcast(FP8X4), lhsT_scale=w3_plane[:, b, cols],
+                        rhs=codes[(c, b)].bitcast(FP8X4), rhs_scale=planes[(c, b)],
+                        start=(b == 1 and e == 0), stop=(b == 0 and e == count - 1),
                     )
             return bank
 
-        def factor_of(c):
-            cols = wgo_first[:] if c == 0 else wgo_rest[:, (c - 1) * CHUNK : c * CHUNK]
-            return cols.unsqueeze(1).to_broadcast([P, 2, CHUNK])
+        def factor(c):
+            return wgo_sb[c][:] if c < 2 else wgo_sb[2][:, (c - 2) * CHUNK : (c - 1) * CHUNK]
 
-        y_sb = {}
+        def factor_pair(c):
+            return factor(c).unsqueeze(1).to_broadcast([P, 2, CHUNK])
 
-        def down_to_sbuf(c, pair):
-            bank = down(c, 2, 2, psum_a)
-            y_sb[(c, pair)] = work.tile([P, 2, CHUNK], F32, name="y%d" % pair)
-            nc.scalar.copy(y_sb[(c, pair)][:], bank[:])
+        def to_sbuf(c, pair, bank):
+            tile = placed([P, 2, CHUNK], F32, "y_%d_%d" % (c, pair), H12_AT + pair * 2 * KB)
+            nc.scalar.copy(tile[:], bank[:])
+            return tile
+
+        def weigh_pair(engine, c, pair, y):
+            tile = held([P, 2, CHUNK], F32, "weighted_%d_%d" % (c, pair))
+            engine.tensor_tensor(tile[:], y[:], factor_pair(c), MULT)
+            return tile
 
         page = [held([P, S], F32, "page%d" % i) for i in range(NT)]
-        weighted = {}
 
-        def weigh_first_pair(c, offset):
-            banks = [down(c, i, 1, psum_y) for i in range(2)]
-            weighted[(c, 0)] = placed([P, 2, CHUNK], F32, "weighted_%d_0" % c, offset)
-            nc.vector.tensor_tensor(weighted[(c, 0)][:, :1], banks[0][:], factor_of(c)[:, :1], MULT)
-            if c == 1:
-                y_second = work.tile([P, 1, CHUNK], F32, name="y_second")
-                nc.scalar.copy(y_second[:], banks[1][:])
-                nc.gpsimd.tensor_tensor(weighted[(c, 0)][:, 1:], y_second[:], factor_of(c)[:, :1], MULT)
-            else:
-                nc.vector.tensor_tensor(weighted[(c, 0)][:, 1:], banks[1][:], factor_of(c)[:, :1], MULT)
+        def scatter(i, values, first, width):
+            nc.vector.tensor_copy(page[i][:].indirect(idx2[:, first // 16 : (first + width) // 16]), values)
 
-        def weigh_second_pair(c):
-            weighted[(c, 1)] = placed([P, 2, CHUNK], F32, "weighted_%d_1" % c, H_AT + c * 2 * KB)
-            nc.gpsimd.tensor_tensor(weighted[(c, 1)][:], y_sb[(c, 1)][:], factor_of(c), MULT)
-
-        def scatter(c, pair):
+        def scatter_pair(c, pair, weighted):
             for e in range(2):
-                offsets = idx2[:, c * CHUNK // 16 : (c + 1) * CHUNK // 16]
-                nc.vector.tensor_copy(page[2 * pair + e][:].indirect(offsets), weighted[(c, pair)][:, e, :])
+                scatter(2 * pair + e, weighted[:, e, :], c * CHUNK, CHUNK)
+
+        gather(v_plane, tab_plane, 0)
+        gather(v_plane, tab_plane, 1)
+        quantize_w1(0)
+        order_w2()
+        quantize_w1(1)
+        gather(v_words, tab, 0)
+        gather(v_words, tab, 1)
+        quantize_w1(2)
+        x0_sb = [placed([P, S], F32, "x0_%d" % i, W1_AT + i * 4 * KB) for i in range(NT)]
+        for i in range(NT):
+            nc.sync.dma_start(x0_sb[i][:], x0[i * P : (i + 1) * P, :])
+        gate(0, 0, (0, 1))
+        routed(0, 0, (2, 3))
+        gate(0, 1, (4, 5))
+        routed(0, 1, (6, 7))
+        gate(0, 2, (0, 1))
+        routed(0, 2, (2, 3))
+        combine_first(0)
+        combine_rest(0)
+        routed(1, 0, (4, 5))
+        routed(1, 1, (6, 7))
+        routed(1, 2, (0, 1))
+        gate(1, 0, (2, 3))
+        gate(1, 1, (4, 5))
+        gate(1, 2, (6, 7))
+
+        quantize_rest(0)
+        quantize_first(0)
+        low = down(0, 0, 2, 0)
+        high = to_sbuf(0, 1, down(0, 2, 2, 1))
+        combine_first(1)
+        routed(2, 0, (2, 3))
+        low = weigh_pair(nc.vector, 0, 0, low)
+        high = weigh_pair(nc.gpsimd, 0, 1, high)
+        for b in range(NB):
+            gate(2, b, (1, 0))
+        scatter_pair(0, 0, low)
+        combine_rest(1)
+        scatter_pair(0, 1, high)
+
+        quantize_rest(1)
+        quantize_first(1)
+        low = to_sbuf(1, 0, down(1, 0, 2, 2))
+        combine_first(2)
+        routed(2, 1, (4, 5))
+        routed(2, 2, (6, 7))
+        routed(3, 0, (1, 0))
+        high = to_sbuf(1, 1, down(1, 2, 2, 3))
+        low = weigh_pair(nc.gpsimd, 1, 0, low)
+        high = weigh_pair(nc.gpsimd, 1, 1, high)
+        gate(3, 0, (2, 3))
+        gate(3, 1, (1, 0))
+        gate(3, 2, (2, 3))
+        scatter_pair(1, 0, low)
+        combine_rest(2)
+        scatter_pair(1, 1, high)
+
+        quantize_rest(2)
+        quantize_first(2)
+        low = down(2, 0, 2, 4)
+        combine_first(3)
+        routed(3, 1, (1, 0))
+        routed(3, 2, (2, 3))
+        high = down(2, 2, 2, 5)
+        y_late = held([P, 2 * CHUNK], F32, "y_late")
+        nc.scalar.copy(y_late[:, :CHUNK], high[:, 1, :])
+        low = weigh_pair(nc.vector, 2, 0, low)
+        scatter_pair(2, 0, low)
+        combine_rest(3)
 
         sums = {}
 
-        def add_turned(i, half, source, opens):
+        def add_turned(half, source, opens):
             if opens:
-                sums[(i, half)] = (psum_a, psum_b)[half].tile([P, PACK, P], F32, name="bank")
+                sums[half] = in_bank([P, PACK, P], "sums%d" % half, (4, 3)[half])
             for k in range(PACK):
                 cols = slice(half * HALF + k * P, half * HALF + (k + 1) * P)
                 nc.tensor.matmul(
-                    sums[(i, half)][:, k, :], source[:, cols], identity[:], is_transpose=True,
+                    sums[half][:, k, :], source[:, cols], identity[:], is_transpose=True,
                     start=(opens and k == 0), stop=(not opens and k == PACK - 1),
                 )
 
+        for half in range(2):
+            add_turned(half, x0_sb[1], True)
+        last = NC - 1
+        quantize_rest(last)
+        third = placed([P, CHUNK], F32, "third", PROD12_AT + 8 * KB)
+        nc.vector.tensor_tensor(third[:], high[:, 0, :], factor(2), MULT)
+        quantize_first(last)
+        scatter(2, third[:], 2 * CHUNK, CHUNK)
+        banks = [down(last, i, 1, (6, 7, 1, 0)[i])[:, 0] for i in range(NT)]
+        values = [held([P, CHUNK], F32, "weighted_last%d" % i) for i in range(NT - 1)]
+        nc.vector.tensor_tensor(values[0][:], banks[0], factor(last), MULT)
+        for i in (1, 2):
+            y = held([P, CHUNK], F32, "y_last%d" % i)
+            nc.scalar.copy(y[:], banks[i])
+            nc.gpsimd.tensor_tensor(values[i][:], y[:], factor(last), MULT)
+        nc.scalar.copy(y_late[:, CHUNK:], banks[3])
+        fourth = held([P, 2 * CHUNK], F32, "fourth")
+        nc.gpsimd.tensor_tensor(fourth[:], y_late[:], wgo_sb[2][:], MULT)
+        for i in range(NT - 1):
+            scatter(i, values[i][:], last * CHUNK, CHUNK)
+        scatter(3, fourth[:], 2 * CHUNK, 2 * CHUNK)
+
         def finish_turned(i):
-            turned = placed([P, 2, PACK, P], F32, "turned%d" % i, TAB_AT + i * 4 * KB)
+            turned = placed([P, 2, PACK, P], F32, "turned", TAB_AT + i * 4 * KB)
             for half in range(2):
-                add_turned(i, half, page[i], False)
-                nc.scalar.activation(turned[:, half], sums[(i, half)][:], ACT.Tanh)
+                add_turned(half, page[i], False)
+                nc.scalar.activation(turned[:, half], sums[half][:], ACT.Tanh)
             for half in range(2):
-                bank = psum_y.tile([P, PACK, P], F32, name="bank_y")
+                bank = in_bank([P, PACK, P], "back%d" % half, (2, 5)[half])
                 for k in range(PACK):
                     nc.tensor.transpose(bank[:, k, :], turned[:, half, k, :], identity[:])
                 cols = slice(half * HALF, (half + 1) * HALF)
@@ -305,71 +413,6 @@ def tile_list_email_expert_return_kernel(
                 nc.scalar.activation(x0_sb[i][:, cols], pre[:, cols], ACT.Tanh)
                 nc.scalar.dma_start(out[i * P : (i + 1) * P, cols], x0_sb[i][:, cols])
 
-        gather(v_plane, tab_plane, 0)
-        gather(v_plane, tab_plane, 1)
-        order_w2()
-        gather(v_words, tab, 0)
-        gather(v_words, tab, 1)
-        for b in range(NB):
-            quantize_w1(b)
-        new_h(0)
-        for b in range(NB):
-            prepare(0, b)
-            engine = nc.vector if b == NB - 1 else nc.gpsimd
-            engine.tensor_tensor(h[0][:, b], acts[0][:, b], prods[0][:, b], MULT)
-        prepare(1, 0)
-        prepare(1, 1)
-
-        y_late = held([P, 2 * CHUNK], F32, "y_late")
-
-        def third_page(c):
-            bank = down(c, 2, 2, psum_a)
-            tile = work.tile([P, CHUNK], F32, name="third")
-            nc.scalar.copy(y_late[:, (c - NC + 2) * CHUNK : (c - NC + 3) * CHUNK], bank[:, 1, :])
-            nc.vector.tensor_tensor(tile[:], bank[:, 0, :], wgo_rest[:, (c - 1) * CHUNK : c * CHUNK], MULT)
-            return tile
-
-        def scatter_page(i, values, first, width):
-            nc.vector.tensor_copy(page[i][:].indirect(idx2[:, first // 16 : (first + width) // 16]), values)
-
-        for c in range(NC - 1):
-            quantize_h(c)
-            prepare(c + 1, 2)
-            if c > 0:
-                weigh_second_pair(c - 1)
-            combine(c + 1, 0)
-            weigh_first_pair(c, RT_AT[c + 1] + (NB - 1) * 4 * KB)
-            if c < NC - 2:
-                down_to_sbuf(c, 1)
-            else:
-                third = third_page(c)
-            combine(c + 1, 1)
-            if c == 0:
-                x0_sb = [placed([P, S], F32, "x0_%d" % i, ACT_AT + i * 4 * KB) for i in range(NT)]
-                for i in range(NT):
-                    nc.sync.dma_start(x0_sb[i][:], x0[i * P : (i + 1) * P, :])
-            scatter(c, 0)
-            if c > 0:
-                scatter(c - 1, 1)
-            if c == NC - 2:
-                scatter_page(2, third[:], c * CHUNK, CHUNK)
-            if c + 2 < NC:
-                prepare(c + 2, 0)
-                prepare(c + 2, 1)
-
-        last = NC - 1
-        for half in range(2):
-            add_turned(1, half, x0_sb[1], True)
-        quantize_h(last)
-        banks = [down(last, i, 1, (psum_y, psum_y, psum_a, psum_b)[i])[:, 0] for i in range(NT)]
-        nc.scalar.copy(y_late[:, CHUNK:], banks[3])
-        fourth = placed([P, 2 * CHUNK], F32, "fourth", H_AT + 4 * KB)
-        nc.gpsimd.tensor_tensor(fourth[:], y_late[:], wgo_rest[:, CHUNK:], MULT)
-        for i in range(NT - 1):
-            values = placed([P, CHUNK], F32, "weighted_last%d" % i, PROD_AT + i * KB)
-            nc.vector.tensor_tensor(values[:], banks[i], wgo_rest[:, (last - 1) * CHUNK :], MULT)
-            scatter_page(i, values[:], last * CHUNK, CHUNK)
-        scatter_page(3, fourth[:], (last - 1) * CHUNK, 2 * CHUNK)
         finish_summed(0)
         finish_turned(1)
         finish_summed(2)

@@ -28,19 +28,19 @@ NC = S // CHUNK
 HALF = 512
 NT = N // P
 KB = 1024
-CAST_VECTOR = 84
+CAST_VECTOR = (0, 84, 63)
 
 W1_AT = 0
-ACT0_AT = W1_AT + 16 * KB
 TAB_AT = W1_AT + 24 * KB
 GROUPED_AT = TAB_AT + 16 * KB
-H0_AT = GROUPED_AT + 8 * KB
+FIRST_ACT_AT = W1_AT + 8 * KB
+H0_AT = GROUPED_AT + 4 * KB
 H12_AT = H0_AT + 4 * KB
 ACT12_AT = H12_AT + 4 * KB
 PROD0_AT = ACT12_AT + 16 * KB
 PROD12_AT = PROD0_AT + 8 * KB
 RT12_AT = PROD12_AT + 16 * KB
-ACT0_PLACES = (ACT0_AT, RT12_AT + 4 * KB)
+ACT0_AT = RT12_AT + 4 * KB
 
 
 def tile_list_email_expert_return_kernel(
@@ -99,25 +99,25 @@ def tile_list_email_expert_return_kernel(
         w3 = held([P, NB, N], U32, "w3")
         wgo_sb = [held([P, width], F32, "wgo%d" % c) for c, width in enumerate((CHUNK, CHUNK, 2 * CHUNK))]
 
-        load_w1(0)
+        nc.sync.dma_start(idx[:], offs)
+        nc.sync.dma_start(idx2[:], offs2)
+        nc.sync.dma_start(w2_raw[:].bitcast(I32), w2_words[0].bitcast(I32))
         for r in range(4):
             nc.sync.dma_start(tab_plane[r:P:32, :].bitcast(I32), tab_scales[0, r:16:4, :].bitcast(I32))
-        nc.sync.dma_start(idx[:], offs)
-        nc.sync.dma_start(w2_raw[:].bitcast(I32), w2_words[0].bitcast(I32))
-        load_w1(1)
+        load_w1(0)
         for r in range(4):
             nc.sync.dma_start(w2_plane_raw[r:P:32, :].bitcast(I32), w2_scales[0, r:16:4, :].bitcast(I32))
         nc.sync.dma_start(tab[:].bitcast(I32), tab_words[0].rearrange("p t i -> p (t i)").bitcast(I32))
+        load_w1(1)
+        load_rt(0, 0)
         load_w1(2)
+        load_rt(0, 1)
+        load_rt(0, 2)
         for r in range(4):
             nc.sync.dma_start(w3_plane[r:P:32].bitcast(I32), w3_scales[:, r:16:4, :].rearrange("a q n -> q a n").bitcast(I32))
-        nc.sync.dma_start(idx2[:], offs2)
         for b in range(NB):
-            load_rt(0, b)
-        load_rt(1, 0)
-        load_rt(1, 1)
+            load_rt(1, b)
         nc.sync.dma_start(w3[:].bitcast(I32), w3_words.rearrange("a p n i -> p a (n i)").bitcast(I32))
-        load_rt(1, 2)
         load_rt(2, 0)
         nc.sync.dma_start(wgo_sb[0][:], wgo[:, :CHUNK])
         load_rt(2, 1)
@@ -147,18 +147,18 @@ def tile_list_email_expert_return_kernel(
                 w2_plane_raw[:].rearrange("p (b m t) -> p t b m", b=NB, t=PACK),
             )
 
-        w1c = [held([P, PASS], U32, "w1c%d" % b) for b in range(NB)]
+        w1c = {}
         w1s = [held([P, PASS], U8, "w1s%d" % b) for b in range(NB)]
 
         def quantize_w1(b):
-            grouped = placed([P, PACK, P, PACK], BF16, "w1_grouped%d" % b, GROUPED_AT + b * 4 * KB)
+            grouped = placed([P, PACK, P, PACK], BF16, "w1_grouped%d" % b, (GROUPED_AT, H0_AT, H12_AT)[b])
+            w1c[b] = held([P, PASS], U32, "w1c%d" % b) if b < NB - 1 else placed([P, PASS], U32, "w1c%d" % b, FIRST_ACT_AT)
             dst = grouped[:].rearrange("p t m j -> p m t j")
             src = w1_raw[b][:].rearrange("p j (m t) -> p m t j", t=PACK)
-            if b < NB - 1:
-                nc.scalar.copy(dst, src)
-            else:
-                nc.vector.tensor_copy(dst[:, :CAST_VECTOR], src[:, :CAST_VECTOR])
-                nc.scalar.copy(dst[:, CAST_VECTOR:], src[:, CAST_VECTOR:])
+            share = CAST_VECTOR[b]
+            if share:
+                nc.vector.tensor_copy(dst[:, :share], src[:, :share])
+            nc.scalar.copy(dst[:, share:], src[:, share:])
             nc.vector.quantize_mx(
                 out=w1c[b][:].bitcast(FP8X4), scales=w1s[b][:], in_=grouped[:].rearrange("p t m j -> p (t m j)")
             )
@@ -189,7 +189,8 @@ def tile_list_email_expert_return_kernel(
             return store[(c, b)]
 
         def routed(c, b, banks):
-            part = new_part(prods, "prod", c, b, PROD0_AT + (c % 2) * 4 * KB, PROD12_AT + min(c, 1) * 8 * KB)
+            first_at = PROD12_AT + 4 * KB if c == 2 else PROD0_AT + (c % 2) * 4 * KB
+            part = new_part(prods, "prod", c, b, first_at, PROD12_AT + min(c, 1) * 8 * KB)
             for u in range(2):
                 bank = four_slots("b_%d_%d_%d" % (c, b, u), banks[u], w2_codes[:, b], w2_plane[:, b], FP4X4, 2, 2 * c + u)
                 cols = slice(u * UNIT, (u + 1) * UNIT)
@@ -200,8 +201,8 @@ def tile_list_email_expert_return_kernel(
                 )
 
         def gate(c, b, banks):
-            rest_at = ACT0_AT + 4 * KB if (c, b) == (0, 1) else ACT12_AT + (c % 2) * 8 * KB
-            part = new_part(acts, "act", c, b, ACT0_PLACES[c % 2], rest_at)
+            first_at = FIRST_ACT_AT if c == 0 else ACT0_AT + (c % 2) * 4 * KB
+            part = new_part(acts, "act", c, b, first_at, ACT12_AT + (c % 2) * 8 * KB)
             for u in range(2):
                 bank = four_slots("a_%d_%d_%d" % (c, b, u), banks[u], w1c[b], w1s[b], FP8X4, 1, 2 * c + u)
                 nc.scalar.activation(part[:, 0, u * UNIT : (u + 1) * UNIT, :], bank[:].rearrange("p t n -> p n t"), ACT.Silu)
@@ -281,36 +282,36 @@ def tile_list_email_expert_return_kernel(
 
         gather(v_plane, tab_plane, 0)
         gather(v_plane, tab_plane, 1)
-        quantize_w1(0)
         order_w2()
-        quantize_w1(1)
+        quantize_w1(0)
         gather(v_words, tab, 0)
         gather(v_words, tab, 1)
-        quantize_w1(2)
-        x0_sb = [placed([P, S], F32, "x0_%d" % i, W1_AT + i * 4 * KB) for i in range(NT)]
-        for i in range(NT):
-            nc.sync.dma_start(x0_sb[i][:], x0[i * P : (i + 1) * P, :])
+        quantize_w1(1)
         gate(0, 0, (0, 1))
         routed(0, 0, (2, 3))
         gate(0, 1, (4, 5))
+        combine_first(0)
         routed(0, 1, (6, 7))
+        quantize_w1(2)
+        x0_sb = [placed([P, S], F32, "x0_%d" % i, W1_AT + (i // 2) * 16 * KB + (i % 2) * 4 * KB) for i in range(NT)]
+        for i in range(NT):
+            nc.sync.dma_start(x0_sb[i][:], x0[i * P : (i + 1) * P, :])
         gate(0, 2, (0, 1))
         routed(0, 2, (2, 3))
-        combine_first(0)
         combine_rest(0)
         routed(1, 0, (4, 5))
         routed(1, 1, (6, 7))
         routed(1, 2, (0, 1))
         gate(1, 0, (2, 3))
-        gate(1, 1, (4, 5))
-        gate(1, 2, (6, 7))
+        gate(1, 1, (2, 3))
+        gate(1, 2, (2, 3))
 
         quantize_rest(0)
         quantize_first(0)
         low = down(0, 0, 2, 0)
         high = to_sbuf(0, 1, down(0, 2, 2, 1))
         combine_first(1)
-        routed(2, 0, (2, 3))
+        routed(2, 0, (4, 5))
         low = weigh_pair(nc.vector, 0, 0, low)
         high = weigh_pair(nc.gpsimd, 0, 1, high)
         for b in range(NB):
@@ -323,8 +324,8 @@ def tile_list_email_expert_return_kernel(
         quantize_first(1)
         low = to_sbuf(1, 0, down(1, 0, 2, 2))
         combine_first(2)
-        routed(2, 1, (4, 5))
-        routed(2, 2, (6, 7))
+        routed(2, 1, (6, 7))
+        routed(2, 2, (4, 5))
         routed(3, 0, (1, 0))
         high = to_sbuf(1, 1, down(1, 2, 2, 3))
         low = weigh_pair(nc.gpsimd, 1, 0, low)
@@ -338,11 +339,11 @@ def tile_list_email_expert_return_kernel(
 
         quantize_rest(2)
         quantize_first(2)
-        low = down(2, 0, 2, 4)
+        low = down(2, 0, 2, 6)
         combine_first(3)
         routed(3, 1, (1, 0))
         routed(3, 2, (2, 3))
-        high = down(2, 2, 2, 5)
+        high = down(2, 2, 2, 7)
         y_late = held([P, 2 * CHUNK], F32, "y_late")
         nc.scalar.copy(y_late[:, :CHUNK], high[:, 1, :])
         low = weigh_pair(nc.vector, 2, 0, low)
@@ -353,7 +354,7 @@ def tile_list_email_expert_return_kernel(
 
         def add_turned(half, source, opens):
             if opens:
-                sums[half] = in_bank([P, PACK, P], "sums%d" % half, (4, 3)[half])
+                sums[half] = in_bank([P, PACK, P], "sums%d" % half, (6, 3)[half])
             for k in range(PACK):
                 cols = slice(half * HALF + k * P, half * HALF + (k + 1) * P)
                 nc.tensor.matmul(
@@ -369,7 +370,7 @@ def tile_list_email_expert_return_kernel(
         nc.vector.tensor_tensor(third[:], high[:, 0, :], factor(2), MULT)
         quantize_first(last)
         scatter(2, third[:], 2 * CHUNK, CHUNK)
-        banks = [down(last, i, 1, (6, 7, 1, 0)[i])[:, 0] for i in range(NT)]
+        banks = [down(last, i, 1, (4, 5, 1, 0)[i])[:, 0] for i in range(NT)]
         values = [held([P, CHUNK], F32, "weighted_last%d" % i) for i in range(NT - 1)]
         nc.vector.tensor_tensor(values[0][:], banks[0], factor(last), MULT)
         for i in (1, 2):
@@ -389,7 +390,7 @@ def tile_list_email_expert_return_kernel(
                 add_turned(half, page[i], False)
                 nc.scalar.activation(turned[:, half], sums[half][:], ACT.Tanh)
             for half in range(2):
-                bank = in_bank([P, PACK, P], "back%d" % half, (2, 5)[half])
+                bank = in_bank([P, PACK, P], "back%d" % half, (2, 7)[half])
                 for k in range(PACK):
                     nc.tensor.transpose(bank[:, k, :], turned[:, half, k, :], identity[:])
                 cols = slice(half * HALF, (half + 1) * HALF)

@@ -113,10 +113,10 @@ def tile_list_email_expert_return_kernel(
         load_w1(2)
         load_rt(0, 1)
         load_rt(0, 2)
-        for r in range(4):
-            nc.sync.dma_start(w3_plane[r:P:32].bitcast(I32), w3_scales[:, r:16:4, :].rearrange("a q n -> q a n").bitcast(I32))
         for b in range(NB):
             load_rt(1, b)
+        for r in range(4):
+            nc.sync.dma_start(w3_plane[r:P:32].bitcast(I32), w3_scales[:, r:16:4, :].rearrange("a q n -> q a n").bitcast(I32))
         nc.sync.dma_start(w3[:].bitcast(I32), w3_words.rearrange("a p n i -> p a (n i)").bitcast(I32))
         load_rt(2, 0)
         nc.sync.dma_start(wgo_sb[0][:], wgo[:, :CHUNK])
@@ -205,7 +205,10 @@ def tile_list_email_expert_return_kernel(
             part = new_part(acts, "act", c, b, first_at, ACT12_AT + (c % 2) * 8 * KB)
             for u in range(2):
                 bank = four_slots("a_%d_%d_%d" % (c, b, u), banks[u], w1c[b], w1s[b], FP8X4, 1, 2 * c + u)
-                nc.scalar.activation(part[:, 0, u * UNIT : (u + 1) * UNIT, :], bank[:].rearrange("p t n -> p n t"), ACT.Silu)
+                nc.scalar.activation(
+                    part[:, 0, u * UNIT : (u + 1) * UNIT, :].rearrange("p (c i) t -> p c t i", i=2),
+                    bank[:].rearrange("p t (c i) -> p c t i", i=2), ACT.Silu,
+                )
 
         h0, h12 = {}, {}
 
@@ -344,8 +347,6 @@ def tile_list_email_expert_return_kernel(
         routed(3, 1, (1, 0))
         routed(3, 2, (2, 3))
         high = down(2, 2, 2, 7)
-        y_late = held([P, 2 * CHUNK], F32, "y_late")
-        nc.scalar.copy(y_late[:, :CHUNK], high[:, 1, :])
         low = weigh_pair(nc.vector, 2, 0, low)
         scatter_pair(2, 0, low)
         combine_rest(3)
@@ -366,10 +367,11 @@ def tile_list_email_expert_return_kernel(
             add_turned(half, x0_sb[1], True)
         last = NC - 1
         quantize_rest(last)
-        third = placed([P, CHUNK], F32, "third", PROD12_AT + 8 * KB)
-        nc.vector.tensor_tensor(third[:], high[:, 0, :], factor(2), MULT)
         quantize_first(last)
-        scatter(2, third[:], 2 * CHUNK, CHUNK)
+        y_late = placed([P, 3, CHUNK], F32, "y_late", PROD12_AT + 8 * KB)
+        nc.scalar.copy(y_late[:, :2], high[:])
+        offsets = idx2[:, 2 * CHUNK // 16 : 3 * CHUNK // 16]
+        nc.vector.tensor_tensor(page[2][:].indirect(offsets), y_late[:, 0, :], factor(2), MULT)
         banks = [down(last, i, 1, (4, 5, 1, 0)[i])[:, 0] for i in range(NT)]
         values = [held([P, CHUNK], F32, "weighted_last%d" % i) for i in range(NT - 1)]
         nc.vector.tensor_tensor(values[0][:], banks[0], factor(last), MULT)
@@ -377,9 +379,9 @@ def tile_list_email_expert_return_kernel(
             y = held([P, CHUNK], F32, "y_last%d" % i)
             nc.scalar.copy(y[:], banks[i])
             nc.gpsimd.tensor_tensor(values[i][:], y[:], factor(last), MULT)
-        nc.scalar.copy(y_late[:, CHUNK:], banks[3])
+        nc.scalar.copy(y_late[:, 2, :], banks[3])
         fourth = held([P, 2 * CHUNK], F32, "fourth")
-        nc.gpsimd.tensor_tensor(fourth[:], y_late[:], wgo_sb[2][:], MULT)
+        nc.gpsimd.tensor_tensor(fourth[:], y_late[:, 1:].rearrange("p c n -> p (c n)"), wgo_sb[2][:], MULT)
         for i in range(NT - 1):
             scatter(i, values[i][:], last * CHUNK, CHUNK)
         scatter(3, fourth[:], 2 * CHUNK, 2 * CHUNK)
@@ -412,7 +414,7 @@ def tile_list_email_expert_return_kernel(
                 cols = slice(piece * CHUNK, (piece + 1) * CHUNK)
                 nc.vector.tensor_tensor(pre[:, cols], page[i][:, cols], x0_sb[i][:, cols], ADD)
                 nc.scalar.activation(x0_sb[i][:, cols], pre[:, cols], ACT.Tanh)
-                nc.scalar.dma_start(out[i * P : (i + 1) * P, cols], x0_sb[i][:, cols])
+                nc.sync.dma_start(out[i * P : (i + 1) * P, cols], x0_sb[i][:, cols])
 
         finish_summed(0)
         finish_turned(1)

@@ -69,6 +69,8 @@ def tile_list_email_expert_return_kernel(
         w3_plane = held([P, NB, N], U8, "w3_plane")
         nc.vector.memset(tab_plane[:].bitcast(I32), 0)
         nc.vector.memset(w2_plane_raw[:].bitcast(I32), 0)
+        plane_all = held([P, S], U8, "plane_all")
+        nc.vector.memset(plane_all[:].bitcast(I32), 0)
         nc.gpsimd.memset(w3_plane[:].rearrange("p a n -> p (a n)").bitcast(I32), 0)
 
         identity = held([P, P], F32, "identity")
@@ -102,12 +104,15 @@ def tile_list_email_expert_return_kernel(
         nc.sync.dma_start(idx[:], offs)
         nc.sync.dma_start(idx2[:], offs2)
         nc.sync.dma_start(w2_raw[:].bitcast(I32), w2_words[0].bitcast(I32))
-        for r in range(4):
-            nc.sync.dma_start(tab_plane[r:P:32, :].bitcast(I32), tab_scales[0, r:16:4, :].bitcast(I32))
+        nc.sync.dma_start(tab_plane[0:P:8, :].bitcast(I32), tab_scales[0].bitcast(I32))
         load_w1(0)
         for r in range(4):
             nc.sync.dma_start(w2_plane_raw[r:P:32, :].bitcast(I32), w2_scales[0, r:16:4, :].bitcast(I32))
         nc.sync.dma_start(tab[:].bitcast(I32), tab_words[0].rearrange("p t i -> p (t i)").bitcast(I32))
+        picked = held([P, S], U8, "picked")
+        nc.vector.tensor_copy(picked[:], tab_plane[:].indirect(idx[:]))
+        for r in range(4):
+            nc.sync.dma_start(plane_all[r:P:32, :].bitcast(I32), picked[8 * r : P : 32, :].bitcast(I32))
         load_w1(1)
         load_rt(0, 0)
         load_w1(2)
@@ -129,7 +134,7 @@ def tile_list_email_expert_return_kernel(
         nc.sync.dma_start(wgo_sb[2][:], wgo[:, 2 * CHUNK :])
 
         v_words = [held([P, HALF], U32, "v_words%d" % h) for h in range(2)]
-        v_plane = [held([P, HALF], U8, "v_plane%d" % h) for h in range(2)]
+        v_plane = [plane_all[:, h * HALF : (h + 1) * HALF] for h in range(2)]
 
         def gather(dst, window, h):
             nc.vector.tensor_copy(dst[h][:], window[:].indirect(idx[:, h * HALF // 16 : (h + 1) * HALF // 16]))
@@ -283,8 +288,6 @@ def tile_list_email_expert_return_kernel(
             for e in range(2):
                 scatter(2 * pair + e, weighted[:, e, :], c * CHUNK, CHUNK)
 
-        gather(v_plane, tab_plane, 0)
-        gather(v_plane, tab_plane, 1)
         order_w2()
         quantize_w1(0)
         gather(v_words, tab, 0)

@@ -29,6 +29,7 @@ HALF = 512
 NT = N // P
 KB = 1024
 CAST_VECTOR = (0, 84, 63)
+W3_ROW = 4
 
 W1_AT = 0
 TAB_AT = W1_AT + 24 * KB
@@ -86,15 +87,16 @@ def tile_list_email_expert_return_kernel(
             nc.sync.dma_start(tile[:], w1[:, b * PASS : (b + 1) * PASS].rearrange("(p j) c -> p j c", j=PACK))
             w1_raw[b] = tile
 
-        def load_rt(c, b):
+        def load_rt(c, b, chunks=1):
             name = "rt_%d_%d" % (c, b)
-            if (c, b) == (1, 2):
+            if (c, b) == (1, 1):
                 tile = placed([P, PACK, CHUNK], F32, name, RT12_AT)
             else:
-                tile = held([P, PACK, CHUNK], F32, name)
-            rows = rt[b * PASS : (b + 1) * PASS, c * CHUNK : (c + 1) * CHUNK]
+                tile = held([P, PACK, chunks * CHUNK], F32, name)
+            rows = rt[b * PASS : (b + 1) * PASS, c * CHUNK : (c + chunks) * CHUNK]
             nc.sync.dma_start(tile[:], rows.rearrange("(p t) n -> p t n", t=PACK))
-            rt_sb[(c, b)] = tile
+            for e in range(chunks):
+                rt_sb[(c + e, b)] = tile[:, :, e * CHUNK : (e + 1) * CHUNK]
 
         tab = placed([P, T], U32, "tab", TAB_AT)
         w2_raw = held([P, 2 * H], U8, "w2_raw")
@@ -117,11 +119,11 @@ def tile_list_email_expert_return_kernel(
         load_rt(0, 0)
         load_w1(2)
         load_rt(0, 1)
-        load_rt(0, 2)
-        for b in range(NB):
-            load_rt(1, b)
+        load_rt(0, 2, 2)
+        load_rt(1, 0)
+        load_rt(1, 1)
         for r in range(4):
-            nc.sync.dma_start(w3_plane[r:P:32].bitcast(I32), w3_scales[:, r:16:4, :].rearrange("a q n -> q a n").bitcast(I32))
+            nc.sync.dma_start(w3_plane[W3_ROW + r : P : 32].bitcast(I32), w3_scales[:, r:16:4, :].rearrange("a q n -> q a n").bitcast(I32))
         nc.sync.dma_start(w3[:].bitcast(I32), w3_words.rearrange("a p n i -> p a (n i)").bitcast(I32))
         load_rt(2, 0)
         nc.sync.dma_start(wgo_sb[0][:], wgo[:, :CHUNK])
@@ -186,7 +188,7 @@ def tile_list_email_expert_return_kernel(
                 store[(c, 0)] = placed([P, 1, CHUNK, PACK], F32, "%s_%d_0" % (name, c), first_at)[:]
             elif c == 0:
                 store[(c, b)] = placed([P, 1, CHUNK, PACK], F32, "%s_%d_%d" % (name, c, b), rest_at + (b - 1) * 4 * KB)[:]
-            elif b == 1:
+            elif (c, 12) not in store:
                 both = placed([P, 2, CHUNK, PACK], F32, "%s_%d_12" % (name, c), rest_at)
                 store[(c, 12)] = both[:]
                 store[(c, 1)] = both[:, :1]
@@ -257,7 +259,7 @@ def tile_list_email_expert_return_kernel(
                 for e in range(count):
                     cols = slice((first + e) * P, (first + e + 1) * P)
                     nc.tensor.matmul_mx(
-                        out=bank[:, e, :], lhsT=w3[:, b, cols].bitcast(FP8X4), lhsT_scale=w3_plane[:, b, cols],
+                        out=bank[:, e, :], lhsT=w3[:, b, cols].bitcast(FP8X4), lhsT_scale=w3_plane[W3_ROW:, b, cols],
                         rhs=codes[(c, b)].bitcast(FP8X4), rhs_scale=planes[(c, b)],
                         start=(b == 1 and e == 0), stop=(b == 0 and e == count - 1),
                     )
@@ -305,40 +307,39 @@ def tile_list_email_expert_return_kernel(
         gate(0, 2, (0, 1))
         routed(0, 2, (2, 3))
         combine_rest(0)
-        routed(1, 0, (4, 5))
-        routed(1, 1, (6, 7))
-        routed(1, 2, (0, 1))
-        gate(1, 0, (2, 3))
-        gate(1, 1, (2, 3))
-        gate(1, 2, (2, 3))
+        routed(1, 2, (4, 5))
+        routed(1, 0, (6, 7))
+        routed(1, 1, (2, 3))
+        for b in range(NB):
+            gate(1, b, (0, 1))
 
         quantize_rest(0)
         quantize_first(0)
-        low = down(0, 0, 2, 0)
-        high = to_sbuf(0, 1, down(0, 2, 2, 1))
+        low = down(0, 0, 2, 2)
+        high = to_sbuf(0, 1, down(0, 2, 2, 3))
         combine_first(1)
         routed(2, 0, (4, 5))
         low = weigh_pair(nc.vector, 0, 0, low)
         high = weigh_pair(nc.gpsimd, 0, 1, high)
         for b in range(NB):
-            gate(2, b, (1, 0))
+            gate(2, b, (3, 2))
         scatter_pair(0, 0, low)
         combine_rest(1)
         scatter_pair(0, 1, high)
 
         quantize_rest(1)
         quantize_first(1)
-        low = to_sbuf(1, 0, down(1, 0, 2, 2))
+        low = to_sbuf(1, 0, down(1, 0, 2, 0))
         combine_first(2)
         routed(2, 1, (6, 7))
         routed(2, 2, (4, 5))
-        routed(3, 0, (1, 0))
-        high = to_sbuf(1, 1, down(1, 2, 2, 3))
+        routed(3, 0, (3, 2))
+        high = to_sbuf(1, 1, down(1, 2, 2, 1))
         low = weigh_pair(nc.gpsimd, 1, 0, low)
         high = weigh_pair(nc.gpsimd, 1, 1, high)
-        gate(3, 0, (2, 3))
-        gate(3, 1, (1, 0))
-        gate(3, 2, (2, 3))
+        gate(3, 0, (0, 1))
+        gate(3, 1, (3, 2))
+        gate(3, 2, (0, 1))
         scatter_pair(1, 0, low)
         combine_rest(2)
         scatter_pair(1, 1, high)
@@ -347,8 +348,8 @@ def tile_list_email_expert_return_kernel(
         quantize_first(2)
         low = down(2, 0, 2, 6)
         combine_first(3)
-        routed(3, 1, (1, 0))
-        routed(3, 2, (2, 3))
+        routed(3, 1, (3, 2))
+        routed(3, 2, (0, 1))
         high = down(2, 2, 2, 7)
         low = weigh_pair(nc.vector, 2, 0, low)
         scatter_pair(2, 0, low)
@@ -358,7 +359,7 @@ def tile_list_email_expert_return_kernel(
 
         def add_turned(half, source, opens):
             if opens:
-                sums[half] = in_bank([P, PACK, P], "sums%d" % half, (6, 3)[half])
+                sums[half] = in_bank([P, PACK, P], "sums%d" % half, (6, 1)[half])
             for k in range(PACK):
                 cols = slice(half * HALF + k * P, half * HALF + (k + 1) * P)
                 nc.tensor.matmul(
@@ -375,7 +376,7 @@ def tile_list_email_expert_return_kernel(
         nc.scalar.copy(y_late[:, :2], high[:])
         offsets = idx2[:, 2 * CHUNK // 16 : 3 * CHUNK // 16]
         nc.vector.tensor_tensor(page[2][:].indirect(offsets), y_late[:, 0, :], factor(2), MULT)
-        banks = [down(last, i, 1, (4, 5, 1, 0)[i])[:, 0] for i in range(NT)]
+        banks = [down(last, i, 1, (4, 5, 3, 2)[i])[:, 0] for i in range(NT)]
         values = [held([P, CHUNK], F32, "weighted_last%d" % i) for i in range(NT - 1)]
         nc.vector.tensor_tensor(values[0][:], banks[0], factor(last), MULT)
         for i in (1, 2):
@@ -395,7 +396,7 @@ def tile_list_email_expert_return_kernel(
                 add_turned(half, page[i], False)
                 nc.scalar.activation(turned[:, half], sums[half][:], ACT.Tanh)
             for half in range(2):
-                bank = in_bank([P, PACK, P], "back%d" % half, (2, 7)[half])
+                bank = in_bank([P, PACK, P], "back%d" % half, (0, 7)[half])
                 for k in range(PACK):
                     nc.tensor.transpose(bank[:, k, :], turned[:, half, k, :], identity[:])
                 cols = slice(half * HALF, (half + 1) * HALF)

@@ -195,16 +195,35 @@ def tile_list_email_expert_return_kernel(
                 store[(c, 2)] = both[:, 1:]
             return store[(c, b)]
 
+        def new_prod(c, b):
+            name = "prod_%d_%d" % (c, b)
+            if b == 0:
+                at = PROD12_AT + 4 * KB if c == 2 else PROD0_AT + (c % 2) * 4 * KB
+                prods[(c, 0)] = placed([P, 2, CHUNK, 2], F32, name, at)[:]
+            elif c == 0:
+                prods[(c, b)] = placed([P, 2, CHUNK, 2], F32, name, PROD12_AT + (b - 1) * 4 * KB)[:]
+            elif (c, 12) not in prods:
+                both = placed([P, 2, 2 * CHUNK, 2], F32, name, PROD12_AT + 8 * KB)
+                prods[(c, 12)] = both[:]
+                prods[(c, 1)] = both[:, :, :CHUNK]
+                prods[(c, 2)] = both[:, :, CHUNK:]
+            return prods[(c, b)]
+
         def routed(c, b, banks):
-            first_at = PROD12_AT + 4 * KB if c == 2 else PROD0_AT + (c % 2) * 4 * KB
-            part = new_part(prods, "prod", c, b, first_at, PROD12_AT + min(c, 1) * 8 * KB)
-            for u in range(2):
-                bank = four_slots("b_%d_%d_%d" % (c, b, u), banks[u], w2_codes[:, b], w2_plane[:, b], FP4X4, 2, 2 * c + u)
-                cols = slice(u * UNIT, (u + 1) * UNIT)
+            part = new_prod(c, b)
+            cols = slice((c * CHUNK) % HALF, (c * CHUNK) % HALF + CHUNK)
+            rhs, rhs_scale = v_words[c // 2][:, cols].bitcast(FP8X4), v_plane[c // 2][:, cols]
+            for g in range(2):
+                bank = in_bank([P, 2, CHUNK], "b_%d_%d_%d" % (c, b, g), banks[g])
+                for e in range(2):
+                    t = 2 * g + e
+                    nc.tensor.matmul_mx(
+                        out=bank[:, e, :], lhsT=w2_codes[:, b, 2 * t * P : 2 * (t + 1) * P].bitcast(FP4X4),
+                        lhsT_scale=w2_plane[:, b, t * P : (t + 1) * P], rhs=rhs, rhs_scale=rhs_scale, start=True, stop=True,
+                    )
                 nc.vector.tensor_tensor(
-                    part[:, 0, cols, :].rearrange("p (c i) t -> p c t i", i=2),
-                    bank[:].rearrange("p t (c i) -> p c t i", i=2),
-                    rt_sb[(c, b)][:, :, cols].rearrange("p t (c i) -> p c t i", i=2), MULT,
+                    part[:, g], bank[:].rearrange("p e n -> p n e"),
+                    rt_sb[(c, b)][:, 2 * g : 2 * g + 2, :].rearrange("p e n -> p n e"), MULT,
                 )
 
         def gate(c, b, banks):
@@ -222,17 +241,23 @@ def tile_list_email_expert_return_kernel(
         def flat(ap):
             return ap.rearrange("p b n t -> p (b n t)")
 
+        def combine(h, act, prod):
+            nc.gpsimd.tensor_tensor(
+                h.rearrange("p b n (g e) -> p (b n) g e", e=2), act.rearrange("p b n (g e) -> p (b n) g e", e=2),
+                prod.rearrange("p g n e -> p n g e"), MULT,
+            )
+
         def combine_first(c):
             h0[c] = placed([P, 1, CHUNK, PACK], BF16, "h0_%d" % c, H0_AT)
-            nc.gpsimd.tensor_tensor(flat(h0[c][:]), flat(acts[(c, 0)]), flat(prods[(c, 0)]), MULT)
+            combine(h0[c][:], acts[(c, 0)], prods[(c, 0)])
 
         def combine_rest(c):
             h12[c] = placed([P, 2, CHUNK, PACK], BF16, "h12_%d" % c, H12_AT)
             if c == 0:
                 for b in (1, 2):
-                    nc.gpsimd.tensor_tensor(flat(h12[c][:, b - 1 : b]), flat(acts[(c, b)]), flat(prods[(c, b)]), MULT)
+                    combine(h12[c][:, b - 1 : b], acts[(c, b)], prods[(c, b)])
             else:
-                nc.gpsimd.tensor_tensor(flat(h12[c][:]), flat(acts[(c, 12)]), flat(prods[(c, 12)]), MULT)
+                combine(h12[c][:], acts[(c, 12)], prods[(c, 12)])
 
         codes, planes = {}, {}
 

@@ -72,10 +72,11 @@ def tile_list_email_expert_return_kernel(
         nc.vector.memset(w2_plane_raw[:].bitcast(I32), 0)
         plane_all = held([P, S], U8, "plane_all")
         nc.vector.memset(plane_all[:].bitcast(I32), 0)
-        nc.gpsimd.memset(w3_plane[:].rearrange("p a n -> p (a n)").bitcast(I32), 0)
+        nc.vector.memset(w3_plane[:].rearrange("p a n -> p (a n)").bitcast(I32), 0)
 
         identity = held([P, P], F32, "identity")
-        make_identity(nc, identity[:])
+        nc.vector.memset(identity[:], 0.0)
+        make_identity(nc, identity[:], nomemset=True)
 
         warm = held([P, 1], F32, "warm")
         nc.scalar.activation(warm[:], identity[:, :1], ACT.Silu)

from contextlib import ExitStack

import concourse.mybir as mybir
from concourse.masks import make_identity

K, T, S, H, N = 512, 4096, 1024, 1536, 512
FLOPS = 2 * (2 * K * H * S + H * N * S)

F32 = mybir.dt.float32
BF16 = mybir.dt.bfloat16
I32 = mybir.dt.int32
U32 = mybir.dt.uint32
U16 = mybir.dt.uint16
U8 = mybir.dt.uint8
FP8X4 = mybir.dt.float8_e4m3fn_x4
FP4X4 = mybir.dt.float4_e2m1fn_x4
MULT = mybir.AluOpType.mult
ADD = mybir.AluOpType.add
ACT = mybir.ActivationFunctionType

P = 128
PACK = 4
PASS = P * PACK
NB = H // PASS
UNIT = 128
CHUNK = 2 * UNIT
NC = S // CHUNK
HALF = 512
NT = N // P
KB = 1024
CAST_VECTOR = (0, 84, 63)
W3_ROW = 4

W1_AT = 0
TAB_AT = W1_AT + 24 * KB
GROUPED_AT = TAB_AT + 16 * KB
FIRST_ACT_AT = W1_AT + 8 * KB
H0_AT = GROUPED_AT + 4 * KB
H12_AT = H0_AT + 4 * KB
ACT12_AT = H12_AT + 4 * KB
PROD0_AT = ACT12_AT + 16 * KB
PROD12_AT = PROD0_AT + 8 * KB
RT12_AT = PROD12_AT + 16 * KB
ACT0_AT = RT12_AT + 4 * KB


def tile_list_email_expert_return_kernel(
    tc, tab_words, tab_scales, offs, w1, w2_words, w2_scales, rt, w3_words, w3_scales, offs2, wgo, x0, out
):
    nc = tc.nc
    with ExitStack() as ctx:
        keep = ctx.enter_context(tc.tile_pool(name="keep", bufs=1))
        work = ctx.enter_context(tc.tile_pool(name="work", bufs=2))
        arena = ctx.enter_context(tc.tile_pool(name="arena", bufs=1))
        psum = ctx.enter_context(tc.psum_pool(name="psum", bufs=1))

        def held(shape, dtype, name):
            return keep.tile(shape, dtype, name=name, align_bytes=64)

        def placed(shape, dtype, name, offset):
            return arena.tile(shape, dtype, name=name, offset=offset, align_bytes=64)

        def in_bank(shape, name, bank):
            return psum.tile(shape, F32, name=name, offset=bank * 2 * KB)

        idx = keep.tile([P, S // 16], U16, name="idx")
        idx2 = keep.tile([P, S // 16], U16, name="idx2")
        w2_plane_raw = held([P, H], U8, "w2_plane_raw")
        tab_plane = held([P, T], U8, "tab_plane")
        w3_plane = held([P, NB, N], U8, "w3_plane")
        nc.vector.memset(tab_plane[:].bitcast(I32), 0)
        nc.vector.memset(w2_plane_raw[:].bitcast(I32), 0)
        plane_all = held([P, S], U8, "plane_all")
        nc.vector.memset(plane_all[:].bitcast(I32), 0)
        nc.vector.memset(w3_plane[:].rearrange("p a n -> p (a n)").bitcast(I32), 0)

        identity = held([P, P], F32, "identity")
        nc.vector.memset(identity[:], 0.0)
        make_identity(nc, identity[:], nomemset=True)

        warm = held([P, 1], F32, "warm")
        nc.scalar.activation(warm[:], identity[:, :1], ACT.Silu)

        w1_raw, rt_sb = {}, {}

        def load_w1(b):
            tile = placed([P, PACK, PASS], F32, "w1_raw%d" % b, W1_AT + b * 8 * KB)
            nc.sync.dma_start(tile[:], w1[:, b * PASS : (b + 1) * PASS].rearrange("(p j) c -> p j c", j=PACK))
            w1_raw[b] = tile

        def load_rt(c, b, chunks=1):
            name = "rt_%d_%d" % (c, b)
            if (c, b) == (1, 1):
                tile = placed([P, PACK, CHUNK], F32, name, RT12_AT)
            else:
                tile = held([P, PACK, chunks * CHUNK], F32, name)
            rows = rt[b * PASS : (b + 1) * PASS, c * CHUNK : (c + chunks) * CHUNK]
            nc.sync.dma_start(tile[:], rows.rearrange("(p t) n -> p t n", t=PACK))
            for e in range(chunks):
                rt_sb[(c + e, b)] = tile[:, :, e * CHUNK : (e + 1) * CHUNK]

        tab = placed([P, T], U32, "tab", TAB_AT)
        w2_raw = held([P, 2 * H], U8, "w2_raw")
        w3 = held([P, NB, N], U32, "w3")
        wgo_sb = [held([P, width], F32, "wgo%d" % c) for c, width in enumerate((CHUNK, CHUNK, 2 * CHUNK))]

        nc.sync.dma_start(idx[:], offs)
        nc.sync.dma_start(idx2[:], offs2)
        nc.sync.dma_start(w2_raw[:].bitcast(I32), w2_words[0].bitcast(I32))
        nc.sync.dma_start(tab_plane[0:P:8, :].bitcast(I32), tab_scales[0].bitcast(I32))
        load_w1(0)
        for r in range(4):
            nc.sync.dma_start(w2_plane_raw[r:P:32, :].bitcast(I32), w2_scales[0, r:16:4, :].bitcast(I32))
        nc.sync.dma_start(tab[:].bitcast(I32), tab_words[0].rearrange("p t i -> p (t i)").bitcast(I32))
        picked = held([P, S], U8, "picked")
        nc.vector.tensor_copy(picked[:], tab_plane[:].indirect(idx[:]))
        for r in range(4):
            nc.sync.dma_start(plane_all[r:P:32, :].bitcast(I32), picked[8 * r : P : 32, :].bitcast(I32))
        load_w1(1)
        load_rt(0, 0)
        load_w1(2)
        load_rt(0, 1)
        load_rt(0, 2, 2)
        load_rt(1, 0)
        load_rt(1, 1)
        for r in range(4):
            nc.sync.dma_start(w3_plane[W3_ROW + r : P : 32].bitcast(I32), w3_scales[:, r:16:4, :].rearrange("a q n -> q a n").bitcast(I32))
        nc.sync.dma_start(w3[:].bitcast(I32), w3_words.rearrange("a p n i -> p a (n i)").bitcast(I32))
        load_rt(2, 0)
        nc.sync.dma_start(wgo_sb[0][:], wgo[:, :CHUNK])
        load_rt(2, 1)
        load_rt(2, 2)
        load_rt(3, 0)
        nc.sync.dma_start(wgo_sb[1][:], wgo[:, CHUNK : 2 * CHUNK])
        load_rt(3, 1)
        load_rt(3, 2)
        nc.sync.dma_start(wgo_sb[2][:], wgo[:, 2 * CHUNK :])

        v_words = [held([P, HALF], U32, "v_words%d" % h) for h in range(2)]
        v_plane = [plane_all[:, h * HALF : (h + 1) * HALF] for h in range(2)]

        def gather(dst, window, h):
            nc.vector.tensor_copy(dst[h][:], window[:].indirect(idx[:, h * HALF // 16 : (h + 1) * HALF // 16]))

        w2_codes = held([P, NB, 2 * PASS], U8, "w2_codes")
        w2_plane = held([P, NB, PASS], U8, "w2_plane")

        def order_w2():
            nc.vector.tensor_copy(
                w2_codes[:].bitcast(U16).rearrange("p b (t m) -> p t b m", t=PACK),
                w2_raw[:].bitcast(U16).rearrange("p (b m t) -> p t b m", b=NB, t=PACK),
            )
            nc.vector.tensor_copy(
                w2_plane[:].rearrange("p b (t m) -> p t b m", t=PACK),
                w2_plane_raw[:].rearrange("p (b m t) -> p t b m", b=NB, t=PACK),
            )

        w1c = {}
        w1s = [held([P, PASS], U8, "w1s%d" % b) for b in range(NB)]

        def quantize_w1(b):
            grouped = placed([P, PACK, P, PACK], BF16, "w1_grouped%d" % b, (GROUPED_AT, H0_AT, H12_AT)[b])
            w1c[b] = held([P, PASS], U32, "w1c%d" % b) if b < NB - 1 else placed([P, PASS], U32, "w1c%d" % b, FIRST_ACT_AT)
            dst = grouped[:].rearrange("p t m j -> p m t j")
            src = w1_raw[b][:].rearrange("p j (m t) -> p m t j", t=PACK)
            share = CAST_VECTOR[b]
            if share:
                nc.vector.tensor_copy(dst[:, :share], src[:, :share])
            nc.scalar.copy(dst[:, share:], src[:, share:])
            nc.vector.quantize_mx(
                out=w1c[b][:].bitcast(FP8X4), scales=w1s[b][:], in_=grouped[:].rearrange("p t m j -> p (t m j)")
            )

        def four_slots(name, at, codes, plane, dtype, width, j):
            cols = slice((j * UNIT) % HALF, (j * UNIT) % HALF + UNIT)
            rhs, rhs_scale = v_words[j * UNIT // HALF][:, cols].bitcast(FP8X4), v_plane[j * UNIT // HALF][:, cols]
            bank = in_bank([P, PACK, UNIT], name, at)
            for t in range(PACK):
                nc.tensor.matmul_mx(
                    out=bank[:, t, :], lhsT=codes[:, width * t * P : width * (t + 1) * P].bitcast(dtype),
                    lhsT_scale=plane[:, t * P : (t + 1) * P], rhs=rhs, rhs_scale=rhs_scale, start=True, stop=True,
                )
            return bank

        acts, prods = {}, {}

        def new_part(store, name, c, b, first_at, rest_at):
            if b == 0:
                store[(c, 0)] = placed([P, 1, CHUNK, PACK], F32, "%s_%d_0" % (name, c), first_at)[:]
            elif c == 0:
                store[(c, b)] = placed([P, 1, CHUNK, PACK], F32, "%s_%d_%d" % (name, c, b), rest_at + (b - 1) * 4 * KB)[:]
            elif (c, 12) not in store:
                both = placed([P, 2, CHUNK, PACK], F32, "%s_%d_12" % (name, c), rest_at)
                store[(c, 12)] = both[:]
                store[(c, 1)] = both[:, :1]
                store[(c, 2)] = both[:, 1:]
            return store[(c, b)]

        def new_prod(c, b):
            name = "prod_%d_%d" % (c, b)
            if b == 0:
                at = PROD12_AT + 4 * KB if c == 2 else PROD0_AT + (c % 2) * 4 * KB
                prods[(c, 0)] = placed([P, 2, CHUNK, 2], F32, name, at)[:]
            elif c == 0:
                prods[(c, b)] = placed([P, 2, CHUNK, 2], F32, name, PROD12_AT + (b - 1) * 4 * KB)[:]
            elif (c, 12) not in prods:
                both = placed([P, 2, 2 * CHUNK, 2], F32, name, PROD12_AT + 8 * KB)
                prods[(c, 12)] = both[:]
                prods[(c, 1)] = both[:, :, :CHUNK]
                prods[(c, 2)] = both[:, :, CHUNK:]
            return prods[(c, b)]

        def routed(c, b, banks):
            part = new_prod(c, b)
            cols = slice((c * CHUNK) % HALF, (c * CHUNK) % HALF + CHUNK)
            rhs, rhs_scale = v_words[c // 2][:, cols].bitcast(FP8X4), v_plane[c // 2][:, cols]
            for g in range(2):
                bank = in_bank([P, 2, CHUNK], "b_%d_%d_%d" % (c, b, g), banks[g])
                for e in range(2):
                    t = 2 * g + e
                    nc.tensor.matmul_mx(
                        out=bank[:, e, :], lhsT=w2_codes[:, b, 2 * t * P : 2 * (t + 1) * P].bitcast(FP4X4),
                        lhsT_scale=w2_plane[:, b, t * P : (t + 1) * P], rhs=rhs, rhs_scale=rhs_scale, start=True, stop=True,
                    )
                nc.vector.tensor_tensor(
                    part[:, g], bank[:].rearrange("p e n -> p n e"),
                    rt_sb[(c, b)][:, 2 * g : 2 * g + 2, :].rearrange("p e n -> p n e"), MULT,
                )

        def gate(c, b, banks):
            first_at = FIRST_ACT_AT if c == 0 else ACT0_AT + (c % 2) * 4 * KB
            part = new_part(acts, "act", c, b, first_at, ACT12_AT + (c % 2) * 8 * KB)
            for u in range(2):
                bank = four_slots("a_%d_%d_%d" % (c, b, u), banks[u], w1c[b], w1s[b], FP8X4, 1, 2 * c + u)
                nc.scalar.activation(
                    part[:, 0, u * UNIT : (u + 1) * UNIT, :].rearrange("p (c i) t -> p c t i", i=2),
                    bank[:].rearrange("p t (c i) -> p c t i", i=2), ACT.Silu,
                )

        h0, h12 = {}, {}

        def flat(ap):
            return ap.rearrange("p b n t -> p (b n t)")

        def combine(h, act, prod):
            nc.gpsimd.tensor_tensor(
                h.rearrange("p b n (g e) -> p (b n) g e", e=2), act.rearrange("p b n (g e) -> p (b n) g e", e=2),
                prod.rearrange("p g n e -> p n g e"), MULT,
            )

        def combine_first(c):
            h0[c] = placed([P, 1, CHUNK, PACK], BF16, "h0_%d" % c, H0_AT)
            combine(h0[c][:], acts[(c, 0)], prods[(c, 0)])

        def combine_rest(c):
            h12[c] = placed([P, 2, CHUNK, PACK], BF16, "h12_%d" % c, H12_AT)
            if c == 0:
                for b in (1, 2):
                    combine(h12[c][:, b - 1 : b], acts[(c, b)], prods[(c, b)])
            else:
                combine(h12[c][:], acts[(c, 12)], prods[(c, 12)])

        codes, planes = {}, {}

        def quantize_rest(c):
            if c == 0:
                tile = placed([P, 2 * CHUNK], U32, "hc12_0", RT12_AT)
            else:
                tile = work.tile([P, 2 * CHUNK], U32, name="hc12", align_bytes=64)
            plane = work.tile([P, 2 * CHUNK], U8, name="hs12", align_bytes=64)
            nc.vector.quantize_mx(out=tile[:].bitcast(FP8X4), scales=plane[:], in_=flat(h12[c][:]))
            for b in (1, 2):
                codes[(c, b)] = tile[:, (b - 1) * CHUNK : b * CHUNK]
                planes[(c, b)] = plane[:, (b - 1) * CHUNK : b * CHUNK]

        def quantize_first(c):
            tile = placed([P, CHUNK], U32, "hc0_%d" % c, RT12_AT + 2 * KB if c == 0 else ACT12_AT + (c % 2) * 8 * KB)
            plane = work.tile([P, CHUNK], U8, name="hs0", align_bytes=64)
            nc.vector.quantize_mx(out=tile[:].bitcast(FP8X4), scales=plane[:], in_=flat(h0[c][:]))
            codes[(c, 0)], planes[(c, 0)] = tile[:], plane[:]

        def down(c, first, count, at):
            bank = in_bank([P, count, CHUNK], "y_bank_%d_%d" % (c, first), at)
            for b in (1, 2, 0):
                for e in range(count):
                    cols = slice((first + e) * P, (first + e + 1) * P)
                    nc.tensor.matmul_mx(
                        out=bank[:, e, :], lhsT=w3[:, b, cols].bitcast(FP8X4), lhsT_scale=w3_plane[W3_ROW:, b, cols],
                        rhs=codes[(c, b)].bitcast(FP8X4), rhs_scale=planes[(c, b)],
                        start=(b == 1 and e == 0), stop=(b == 0 and e == count - 1),
                    )
            return bank

        def factor(c):
            return wgo_sb[c][:] if c < 2 else wgo_sb[2][:, (c - 2) * CHUNK : (c - 1) * CHUNK]

        def factor_pair(c):
            return factor(c).unsqueeze(1).to_broadcast([P, 2, CHUNK])

        def to_sbuf(c, pair, bank):
            tile = placed([P, 2, CHUNK], F32, "y_%d_%d" % (c, pair), H12_AT + pair * 2 * KB)
            nc.scalar.copy(tile[:], bank[:])
            return tile

        def weigh_pair(engine, c, pair, y):
            tile = held([P, 2, CHUNK], F32, "weighted_%d_%d" % (c, pair))
            engine.tensor_tensor(tile[:], y[:], factor_pair(c), MULT)
            return tile

        page = [held([P, S], F32, "page%d" % i) for i in range(NT)]

        def scatter(i, values, first, width):
            nc.vector.tensor_copy(page[i][:].indirect(idx2[:, first // 16 : (first + width) // 16]), values)

        def scatter_pair(c, pair, weighted):
            for e in range(2):
                scatter(2 * pair + e, weighted[:, e, :], c * CHUNK, CHUNK)

        order_w2()
        quantize_w1(0)
        gather(v_words, tab, 0)
        gather(v_words, tab, 1)
        quantize_w1(1)
        gate(0, 0, (0, 1))
        routed(0, 0, (2, 3))
        gate(0, 1, (4, 5))
        combine_first(0)
        routed(0, 1, (6, 7))
        quantize_w1(2)
        x0_sb = [placed([P, S], F32, "x0_%d" % i, W1_AT + (i // 2) * 16 * KB + (i % 2) * 4 * KB) for i in range(NT)]
        for i in range(NT):
            nc.sync.dma_start(x0_sb[i][:], x0[i * P : (i + 1) * P, :])
        gate(0, 2, (0, 1))
        routed(0, 2, (2, 3))
        combine_rest(0)
        routed(1, 2, (4, 5))
        routed(1, 0, (6, 7))
        routed(1, 1, (2, 3))
        for b in range(NB):
            gate(1, b, (0, 1))

        quantize_rest(0)
        quantize_first(0)
        low = down(0, 0, 2, 2)
        high = to_sbuf(0, 1, down(0, 2, 2, 3))
        combine_first(1)
        routed(2, 0, (4, 5))
        low = weigh_pair(nc.vector, 0, 0, low)
        high = weigh_pair(nc.gpsimd, 0, 1, high)
        for b in range(NB):
            gate(2, b, (3, 2))
        scatter_pair(0, 0, low)
        combine_rest(1)
        scatter_pair(0, 1, high)

        quantize_rest(1)
        quantize_first(1)
        low = to_sbuf(1, 0, down(1, 0, 2, 0))
        combine_first(2)
        routed(2, 1, (6, 7))
        routed(2, 2, (4, 5))
        routed(3, 0, (3, 2))
        high = to_sbuf(1, 1, down(1, 2, 2, 1))
        low = weigh_pair(nc.gpsimd, 1, 0, low)
        high = weigh_pair(nc.gpsimd, 1, 1, high)
        gate(3, 0, (0, 1))
        gate(3, 1, (3, 2))
        gate(3, 2, (0, 1))
        scatter_pair(1, 0, low)
        combine_rest(2)
        scatter_pair(1, 1, high)

        quantize_rest(2)
        quantize_first(2)
        low = down(2, 0, 2, 6)
        combine_first(3)
        routed(3, 1, (3, 2))
        routed(3, 2, (0, 1))
        high = down(2, 2, 2, 7)
        low = weigh_pair(nc.vector, 2, 0, low)
        scatter_pair(2, 0, low)
        combine_rest(3)

        sums = {}

        def add_turned(half, source, opens):
            if opens:
                sums[half] = in_bank([P, PACK, P], "sums%d" % half, (6, 1)[half])
            for k in range(PACK):
                cols = slice(half * HALF + k * P, half * HALF + (k + 1) * P)
                nc.tensor.matmul(
                    sums[half][:, k, :], source[:, cols], identity[:], is_transpose=True,
                    start=(opens and k == 0), stop=(not opens and k == PACK - 1),
                )

        for half in range(2):
            add_turned(half, x0_sb[1], True)
        last = NC - 1
        quantize_rest(last)
        quantize_first(last)
        y_late = placed([P, 3, CHUNK], F32, "y_late", PROD12_AT + 8 * KB)
        nc.scalar.copy(y_late[:, :2], high[:])
        offsets = idx2[:, 2 * CHUNK // 16 : 3 * CHUNK // 16]
        nc.vector.tensor_tensor(page[2][:].indirect(offsets), y_late[:, 0, :], factor(2), MULT)
        banks = [down(last, i, 1, (4, 5, 3, 2)[i])[:, 0] for i in range(NT)]
        values = [held([P, CHUNK], F32, "weighted_last%d" % i) for i in range(NT - 1)]
        nc.vector.tensor_tensor(values[0][:], banks[0], factor(last), MULT)
        for i in (1, 2):
            y = held([P, CHUNK], F32, "y_last%d" % i)
            nc.scalar.copy(y[:], banks[i])
            nc.gpsimd.tensor_tensor(values[i][:], y[:], factor(last), MULT)
        nc.scalar.copy(y_late[:, 2, :], banks[3])
        fourth = held([P, 2 * CHUNK], F32, "fourth")
        nc.gpsimd.tensor_tensor(fourth[:], y_late[:, 1:].rearrange("p c n -> p (c n)"), wgo_sb[2][:], MULT)
        for i in range(NT - 1):
            scatter(i, values[i][:], last * CHUNK, CHUNK)
        scatter(3, fourth[:], 2 * CHUNK, 2 * CHUNK)

        def finish_turned(i):
            turned = placed([P, 2, PACK, P], F32, "turned", TAB_AT + i * 4 * KB)
            for half in range(2):
                add_turned(half, page[i], False)
                nc.scalar.activation(turned[:, half], sums[half][:], ACT.Tanh)
            for half in range(2):
                bank = in_bank([P, PACK, P], "back%d" % half, (0, 7)[half])
                for k in range(PACK):
                    nc.tensor.transpose(bank[:, k, :], turned[:, half, k, :], identity[:])
                cols = slice(half * HALF, (half + 1) * HALF)
                nc.scalar.copy(x0_sb[i][:, cols], bank[:].rearrange("p k m -> p (k m)"))
                nc.sync.dma_start(out[i * P : (i + 1) * P, cols], x0_sb[i][:, cols])

        def finish_summed(i):
            for half in range(2):
                cols = slice(half * HALF, (half + 1) * HALF)
                pre = placed([P, HALF], F32, "pre%d_%d" % (i, half), TAB_AT + i * 4 * KB + half * 2 * KB)
                nc.gpsimd.tensor_tensor(pre[:], page[i][:, cols], x0_sb[i][:, cols], ADD)
                nc.scalar.activation(x0_sb[i][:, cols], pre[:], ACT.Tanh)
                nc.sync.dma_start(out[i * P : (i + 1) * P, cols], x0_sb[i][:, cols])

        def finish_last():
            i = NT - 1
            pre = placed([P, S], F32, "pre", TAB_AT + 6 * KB)
            for piece in range(S // CHUNK):
                cols = slice(piece * CHUNK, (piece + 1) * CHUNK)
                nc.vector.tensor_tensor(pre[:, cols], page[i][:, cols], x0_sb[i][:, cols], ADD)
                nc.scalar.activation(x0_sb[i][:, cols], pre[:, cols], ACT.Tanh)
                nc.sync.dma_start(out[i * P : (i + 1) * P, cols], x0_sb[i][:, cols])

        finish_summed(0)
        finish_turned(1)
        finish_summed(2)
        finish_last()
